import numpy as np, ml_dtypes
CORES = [3,11,19,27,35,43,51,59]
N = 8
BF = ml_dtypes.bfloat16
W, L, C, SX, SL, STEPS = 4096, 1024, 128, 32, 8, 5
def node(q, w):
    u = np.add.reduce(w[..., None] * q, axis=2) & (W - 1)
    return ((u * u >> 5) + 37 * u) & (W - 1)
def parts(rng):
    X = rng.integers(0, 256, (N, 8, 16, W))
    G = np.repeat(rng.integers(0, W, (1, 8, 16, L)), N, axis=0); cut = rng.integers(0, 22, (N, 8, 1, L))
    G = np.where((np.arange(16)[:, None] >= cut) | (rng.random(G.shape) < 0.05), rng.integers(0, W, G.shape), G)
    D = np.repeat(rng.integers(0, L, (1, 8, W)), N, axis=0); D = np.where(rng.random(D.shape) < 0.3, rng.integers(0, L, D.shape), D)
    q = rng.integers(0, 256, (N, 8, 16, C)); E = rng.integers(0, W, (N, 8, 16, C)); w = rng.integers(0, 256, (N, 8, 16))
    th = np.stack([rng.choice(np.array([500, 1100, 1300, 1450, 1600]), (N, 8)) + rng.integers(0, 60, (N, 8)), rng.integers(1000, 1650, (N, 8))], axis=2)
    return X, G, D, q, E, w, th
def pack(X, G, D, q, E, w, th):
    return {"xr": X.reshape(N, 128, W).astype(np.float32).astype(BF), "lg": G.reshape(N, 128, L).astype(np.int32), "dr": D.astype(np.int32), "qd": q.reshape(N, 128, C).astype(np.float32).astype(BF),
            "e0": E.reshape(N, 128, C).astype(np.int32), "wt": w.reshape(N, 128, 1).astype(np.float32).astype(BF), "th": th.astype(np.int32)}
def setup_inputs(rng):
    return pack(*parts(rng))
def setup_inputs_spread(rng):
    X, G, D, q, E, w, th = parts(rng)
    X = np.minimum((np.exp2(8 * rng.random((N, 8, 1, W))) * (0.25 + rng.random(X.shape))).astype(np.int64), 255)
    q = np.minimum((np.exp2(8 * rng.random((N, 8, 1, C))) * (0.25 + rng.random(q.shape))).astype(np.int64), 255)
    w = np.minimum(np.exp2(8 * rng.random(w.shape)).astype(np.int64), 255); th = np.minimum(np.exp2(5 + 7 * rng.random(th.shape)).astype(np.int64), 4079)
    G = np.where(rng.random(G.shape) < 0.5, G, (W * rng.random(G.shape) ** 3).astype(np.int64)); D = np.where(rng.random(D.shape) < 0.5, D, (L * rng.random(D.shape) ** 3).astype(np.int64))
    E = (W * rng.random(E.shape) ** 2).astype(np.int64)
    return pack(X, G, D, q, E, w, th)
def ends_of(rng, shape, hi, share):
    return np.where(rng.random(shape) < share, hi * rng.integers(0, 2, shape), rng.integers(0, hi + 1, shape))
def setup_inputs_ends(rng):
    kx, kq = rng.random((N, 8, 1, W)), rng.random((N, 8, 1, C))
    X = np.where(kx < 0.2, 0, np.where(kx < 0.4, 255, 255 * rng.integers(0, 2, (N, 8, 16, W)))); q = np.where(kq < 0.2, 0, np.where(kq < 0.4, 255, 255 * rng.integers(0, 2, (N, 8, 16, C))))
    X[:, ::2, :, 0] = 255; X[:, ::2, :, W - 1] = 0; X[:, 1::2, :, 0] = 0; X[:, 1::2, :, W - 1] = 255
    G = ends_of(rng, (N, 8, 16, L), W - 1, 0.7); D = ends_of(rng, (N, 8, W), L - 1, 0.7); E = ends_of(rng, (N, 8, 16, C), W - 1, 0.7)
    free = np.argsort(rng.random((N, 8, 16)), axis=2) < 4
    w = np.where(free, rng.integers(0, 256, (N, 8, 16)), 255 * rng.integers(0, 2, (N, 8, 16))); w[:, 0, 0] = 0; w[:, 0, 1] = 255; w[N - 1, 7] = 255
    r, g = np.arange(N)[:, None], np.arange(8)[None, :]
    th = np.stack([np.where((r + g) % 2 == 0, 4079, 0), np.where((g % 2 == 1) & (g < 7), rng.integers(1000, 3000, (N, 8)), np.where((r + (g >> 1)) % 2 == 0, 0, 4079))], axis=2); th[N - 1, 7] = 4079
    q[:, 7, :, C - 1] = 255; q[:, 6, :, C - 1] = 0; q[N - 1, 7][:, [0, 1, C - 1]] = 255
    n = node(q, w)
    for a in range(N):
        D[a, 7, n[a, 7, C - 1]] = L - 1; D[(a + 1) % N, 7, n[a, 7, C - 1]] = L - 1
        G[a, 7, :, L - 1] = (W - 1) * ((a + 1) % 2)
    G[N - 1, 7, :, L - 1] = 0; G[0, 7, :, L - 1] = W - 1; G[0, 7, 15, L - 1] = 0
    return pack(X, G, D, q, E, w, th)
def setup_inputs_corners(rng):
    X, G, D, q, E, w, th = parts(rng)
    m = rng.integers(3, 30, (N, 8)); th[:, :, 0] = 32 * m - 1; th[:, :, 1] = 16 * m; m = m[:, :, None, None]; one = np.eye(16, dtype=np.int64)
    w[..., 0] = 0; w[..., 15] = 255
    nm = SX * np.argsort(rng.random((8, C)), axis=1)[:, :, None] + np.arange(5)
    r0 = rng.integers(4, 90, (N, 8, C, 16)); r2 = r0 + 2 * m
    rec = np.stack([r0, r2 - one[0], r2, r0 - one[1] - one[2], r2 + one[1] + one[2]], axis=3)
    kd = rng.choice(np.array([0, 1, 8, 14, 15, 16]), (N, 8, C)); ks = np.minimum(kd, 15); side = rng.integers(-1, 2, (N, 8, C))
    d = r0 + m + side[..., None] * one[0]
    q = np.ascontiguousarray((d + np.where(kd[..., None] == 0, 0, r0)).transpose(0, 1, 3, 2))
    st = np.maximum(ks + 1, rng.choice(np.array([0, 5, 15, 16]), (N, 8, C)))[..., None]; kk = np.arange(16)
    hj = np.where(kk < st, 0, 3); fj = np.where(kk < kd[..., None], rng.integers(0, 2, (N, 8, C, 16)), np.where(kk < st, 2, 4))
    pal = np.broadcast_to(nm, (N, 8, C, 5)); hn = np.take_along_axis(pal, hj, 3); fn = np.take_along_axis(pal, fj, 3)
    n = node(q, w); col = SL * np.arange(C)
    for a in range(N):
        b = (a + 1) % N
        for g in range(8):
            X[a, g][:, nm[g].reshape(-1)] = rec[a, g].reshape(-1, 16).T
            G[a, g][:, col] = hn[a, g].T; G[b, g][:, col + 1] = fn[a, g].T
            D[b, g, n[a, g]] = col + 1
    for a in range(N):
        for g in range(8): D[a, g, n[a, g]] = col
    return pack(X, G, D, q, E, w, th)
def setup_inputs_crowd(rng):
    X, G, D, q, E, w, th = parts(rng)
    q[:3] = rng.integers(200, 256, q[:3].shape); w[:, 1:3, 0] = 1; w[:, 6] = 0
    q[:, 0:3] = q[:, 0:3, :, :1].copy(); q[:, 1, 0, C - 1] ^= 1; q[:, 2, 0, 0] ^= 1
    q[:, 3, :, 0::2] = q[:, 3, :, :1].copy(); q[:, 3, :, 1::2] = q[:, 3, :, 1:2].copy()
    D[:, 4] = rng.choice(np.array([0, L - 1, L // 2]), (N, W)); G[:, 5, 1:] = rng.choice(np.array([0, 1, W - 1]), (N, 15, L))
    nm = 2 * rng.permutation(W >> 1)[:N] + 1
    for a in range(N): G[a, :, 0, :] = nm[a]
    for a in range(2): X[a, :, :, nm[a]] = 0; X[a, :, :, nm[a + 1]] = 255; th[a, :, 0] = 0
    X[2, :, :, nm[2]] = 255; X[2, :, :, nm[3]] = 0; th[2, :, 0] = 0
    q[1, 7, :, C - 1] = 0
    v = np.arange(1, 4081); u = (255 * v) & (W - 1); k = W - 1 - (((u * u >> 5) + 37 * u) & (W - 1))
    j = int(rng.choice(np.flatnonzero((k >= 1) & (k <= 7 * (C - 1))))); v, u, k = int(v[j]), int(u[j]), int(k[j])
    X[3][:, :, nm] = 0; X[3][:, :, nm[3]] = 255; th[3] = 0; G[3, :, 1, :] = nm[2]
    w[3] = 0; w[3, 7] = rng.permutation(v // 16 + (np.arange(16) < v % 16))
    lose = rng.permutation(7 * (C - 1))[:k]; q[3] = 255; q[3, lose // (C - 1), :, 1 + lose % (C - 1)] = 0
    D[3, :7] |= 1; D[3, 7, W - 1] = SL * int(rng.integers(0, C)) + ((u & (SL - 1)) ^ 1); E[3, 7, :, 0] = nm[3]
    return pack(X, G, D, q, E, w, th)
def setup_inputs_brink(rng):
    X, G, D, q, E, w, th = parts(rng); nm = rng.permutation(W)[:6]
    for a in range(N):
        b = a % 2; own, oth = nm[b], nm[1 - b]
        for g in (0, 7):
            G[a, g, 0, :] = own; X[a, g, :, own] = 0; X[a, g, :, oth] = 0; X[a, g, int(rng.integers(0, 16)), oth] = 1
            q[a, g, :, 1::2] = 255; th[a, g, 0] = 0
        G[a, 2, 0, :] = own; G[a, 2, 3, :] = nm[2 + b]; X[a, 2, :, own] = 0; X[a, 2, :, oth] = 255; X[a, 2, int(rng.integers(0, 16)), oth] = 254
        X[a, 2, :, nm[2 + b]] = 255; X[a, 2, :, nm[3 - b]] = 0; th[a, 2, 0] = 4079
        G[a, 4, 0, :] = own; G[a, 4, 1, :] = nm[4]; G[a, 4, 2, :] = nm[5]; X[a, 4, :, own] = 200; X[a, 4, :, oth] = 100
        X[a, 4, :, nm[4]] = 0; X[a, 4, int(rng.integers(0, 16)), nm[4]] = 1; X[a, 4, :, nm[5]] = 0
        q[a, 4, :, 1::2] = 255; th[a, 4, 0] = 0; th[a, 4, 1] = 4079
    for v in (X, G, D, q, E, w, th): v[2] = v[0]; v[3] = v[1]
    return pack(X, G, D, q, E, w, th)
def check_inputs(d):
    bad = []
    for k, hi in (("xr", 255), ("lg", W - 1), ("dr", L - 1), ("qd", 255), ("e0", W - 1), ("wt", 255), ("th", 4079)):
        v = np.asarray(d[k]).astype(np.float64)
        if not (np.min(v) >= 0 and np.max(v) <= hi): bad.append("range of " + k)
        elif np.any(v != np.floor(v)): bad.append("whole numbers of " + k)
    return bad
def column(logs, book, n):
    return np.take_along_axis(logs, np.take_along_axis(book, n, 1)[:, None, :], 2)
def records(X, names):
    return np.take_along_axis(X, np.ascontiguousarray(names.transpose(0, 2, 1)).reshape(8, 1, C * 16), 2).reshape(8, 16, C, 16)
def reference(xr, lg, dr, qd, e0, wt, th):
    X = xr.astype(np.float32).astype(np.int32).reshape(N, 8, 16, W); G = lg.astype(np.int32).reshape(N, 8, 16, L); D = dr.astype(np.int64).reshape(N, 8, W)
    q = qd.astype(np.float32).astype(np.int32).reshape(N, 8, 16, C); E = e0.astype(np.int32).reshape(N, 8, 16, C)
    w = wt.astype(np.float32).astype(np.int32).reshape(N, 8, 16, 1); h = th.astype(np.int64).reshape(N, 8, 2); A = np.zeros(N, np.int64)
    kk = np.arange(16); i = np.arange(C)
    for t in range(STEPS):
        u = np.add.reduce(w * q, axis=2).astype(np.int64) & (W - 1)
        n = ((u * u >> 5) + 37 * u + A[:, None, None]) & (W - 1)
        own, other = [], []
        for r in range(N):
            f = (r + 1 + t % (N - 1)) % N
            own.append(column(G[r], D[r], n[r])); other.append(column(G[f], D[f], n[r]))
        for r in range(N):
            P, B = own[r], other[r]
            x = records(X[r], P); y = records(X[r], B)
            apart = np.add.reduce(np.abs(x - y), axis=1) > h[r, :, 0][:, None, None]
            ks = np.where(np.any(apart, axis=2), np.argmax(apart, axis=2), 15)
            M = np.max(np.where(kk < ks[:, None, :, None], x, 0), axis=3)
            d = np.abs(q[r] - M)
            xs = np.take_along_axis(x, ks[:, None, :, None], 3)[..., 0]; ys = np.take_along_axis(y, ks[:, None, :, None], 3)[..., 0]
            lost = np.add.reduce(np.abs(ys - d), axis=1) < np.add.reduce(np.abs(xs - d), axis=1)
            z = np.where(lost[:, None, :, None], y, x)
            over = (np.add.reduce(np.abs(z - d[..., None]), axis=1) > h[r, :, 1][:, None, None]) & (kk > ks[:, :, None])
            e = np.where(np.any(over, axis=2), np.argmax(over, axis=2), 16)
            last = np.take_along_axis(z, (e - 1)[:, None, :, None], 3)[..., 0]
            E[r] = np.where(kk[None, :, None] < e[:, None, :], np.where((kk[None, :, None] >= ks[:, None, :]) & lost[:, None, :], B, P), E[r])
            cl = SL * i + (u[r] & (SL - 1)); cx = (SX * i + (u[r] & (SX - 1)))[:, None, :]
            np.put_along_axis(G[r], cl[:, None, :], E[r], 2)
            old = np.take_along_axis(X[r], cx, 2); np.put_along_axis(X[r], cx, (old + d) >> 1, 2)
            if t + 1 < STEPS:
                for g in range(8):
                    v, first = np.unique(n[r, g], return_index=True)
                    D[r, g, v] = cl[g, first]
            q[r] = (d + last) >> 1; A[r] = np.count_nonzero(lost)
    return {"yl": G.reshape(N, 128, L).astype(np.float32), "yx": X.reshape(N, 128, W).astype(np.float32).astype(BF), "yq": q.reshape(N, 128, C).astype(np.float32).astype(BF)}

@@ -1,0 +1,652 @@
+from concourse.bass import DstId, RemoteDMATransfer
+from concourse.mybir import dt, AluOpType, AxisListType, ActivationFunctionType
+
+N, STEPS = 8, 5
+F32, BF, I32, U16 = "float32", "bfloat16", "int32", "uint16"
+
+
+def _sb(cols, d):
+    return ("sbuf", [128, cols], d)
+
+
+SCRATCH = {
+    "X": _sb(4096, BF), "Gi": _sb(1024, I32), "G": _sb(1024, F32), "Dm": _sb(4112, I32), "Dd": _sb(256, I32),
+    "GR1": _sb(1024, F32), "nq": _sb(16, U16), "hq": _sb(128, BF), "Bq": _sb(128, U16), "Bg": _sb(128, F32), "Idf": _sb(128, F32), "nIf": _sb(128, F32),
+    "GR2": _sb(1024, F32), "GR3": _sb(1024, F32), "GR4": _sb(1024, F32),
+    "q0": _sb(128, BF), "w0": _sb(8, BF), "e0i": _sb(128, I32), "thi": _sb(4, I32), "thf": _sb(4, F32), "thc": _sb(8, F32),
+    "qh": _sb(128, BF), "XY": _sb(4096, BF), "pm": _sb(2064, BF), "A1": _sb(2048, BF), "MX": _sb(2048, BF), "AY": _sb(2048, BF),
+    "sc": _sb(256, F32), "ui": _sb(8, I32), "u": _sb(8, I32), "sq": _sb(8, I32), "sq5": _sb(8, I32), "lin": _sb(8, I32), "sm": _sb(8, I32),
+    "nlh": _sb(16, I32), "n16": _sb(16, U16), "hm": _sb(128, BF), "cand": _sb(256, F32), "c16": _sb(16, U16), "PB": _sb(256, U16),
+    "Pf": _sb(128, F32), "tri": _sb(384, F32), "D0": _sb(384, BF), "Ec": _sb(128, F32),
+    "ov": _sb(128, BF), "lt": _sb(128, BF), "s16": _sb(8, U16), "Mq": _sb(128, BF), "dh": _sb(128, BF), "dq": _sb(128, F32),
+    "sd": _sb(256, BF), "sa": _sb(256, BF), "lost": _sb(128, BF), "o2": _sb(256, BF), "e16": _sb(8, U16), "qi": _sb(128, I32),
+    "Ac": _sb(4, F32), "clx0": _sb(16, I32), "clx1": _sb(16, I32), "clx": _sb(16, U16), "clR": _sb(128, F32), "oldh": _sb(128, BF),
+    "xi": _sb(128, I32), "n32": _sb(8, I32), "nf": _sb(8, F32), "bc": _sb(128, F32), "x1": _sb(128, F32), "eq": _sb(128, BF),
+    "eqs": _sb(128, BF), "tt": _sb(8, F32), "o16": _sb(16, U16), "yqb": _sb(128, BF),
+    "colg": _sb(128, BF), "colb": _sb(256, BF), "col": _sb(144, BF), "pI": _sb(4, I32), "pb": _sb(4, I32), "pc": _sb(20, F32),
+    "aq": _sb(16, F32), "Bo": _sb(128, BF), "nBo": _sb(128, BF), "Bf": _sb(128, F32), "W2": _sb(128, BF), "Id": _sb(128, BF), "nI": _sb(128, BF),
+    "BI": _sb(128, BF), "nBI": _sb(128, BF), "Sh": _sb(128, BF), "Tri": _sb(128, BF), "tmp": _sb(128, BF), "tmp2": _sb(256, BF),
+    "ms": _sb(256, BF), "poi": _sb(128, BF), "dl": _sb(128, BF), "rp": _sb(1024, BF), "r2": _sb(128, BF), "S1": _sb(144, BF),
+    "S2": _sb(144, BF), "Sn": _sb(144, BF), "ix": _sb(128, BF), "opn": _sb(256, BF), "c256": _sb(256, BF), "o16th": _sb(128, BF),
+    "ast": _sb(8, U16), "stw": _sb(16, I32), "iot": _sb(512, F32),
+}
+for _t in range(1, STEPS):
+    SCRATCH["DR%d" % _t] = _sb(256, I32)
+    SCRATCH["CR%d" % _t] = _sb(8, U16)
+    SCRATCH["ER%d" % _t] = _sb(128, F32)
+for _b in ("Y00", "Y01", "Y10", "Y11", "T0", "T1", "P0", "P1"):
+    SCRATCH[_b] = ("psum", [128, 512], F32)
+
+CFG = {"gch": 512, "nu": 1, "nm": 2, "sda": 1, "gsp": 2, "seed": 0, "wake": 70.0, "gat": 1.56, "sca": 3.8, "pe": 0.5,
+       "look": 120.0, "noise": 0.0, "vpen": 300.0, "fix": 0.0, "bw": 80.0,
+       "bg": 0.0, "by": 0.0, "ba": 0.0, "bh": 0.0, "hmv": 0, "csp": 0, "slack": 0.0, "pcv": 0, "sgn": 0, "efi": 1, "bu": 0.0}
+CFG.update({"nu":2,"sda":0,"gsp":1,"look":200,"vpen":100,"bh":1500,"csp":1,"slack":150,"pcv":1,"sgn":2,"bu":500,"B":{"y00.1":2500,"y01.1":1500,"A100.1":1500,"A101.1":1500,"P160.1":3000,"AY00.1":-600,"cB0.1":1500,"lin0.1":200,"T1.4":3000,"clx1.1":1500,"MX1":3000,"Y00.3":-600,"Y11.3":-3000,"Y00.4":3000,"bc.1":-600,"u1.1":-1500,"T1.9":-3000,"sc0.4":1500,"pm1.1":-200,"is161.1":-600,"iT0.17":-600,"Y10.3":-3000,"iBg1.1":3000,"x10.1":200,"imq1.1":-3000,"ilp1.1":1500,"T0.9":1500,"x1.1":-200,"cB1.1":1500,"lost0.1":1500,"T1.5":1500,"x11.1":-200,"T0.10":-3000,"T0.7":200,"iMX1":600,"iT1.12":600,"ib32.1":600,"T1.15":-3000,"sq51.1":3000,"T0.20":3000,"sm1.1":3000,"ieqs.1":-600,"T1.11":-3000,"s161.1":-3000,"xp0.1":3000,"Y11.4":1500,"dps0.1":-1500,"x01.1":600,"Y10.1":-3000,"sc1.1":-3000,"Y11.2":-600,"T1.8":-3000,"sa0.1":200,"iY11.4":-1500,"sc1.4":600,"iG1.2":-1500,"isa1.1":1500,"y10.1":-200,"iT1.3":3000},"E":{"ib32.1":"v","ip1.1":"v","clR0.1":"v","y00.1":"a","clR1.1":"a","iIdf.1":"v","Bg1.1":"a","inBI.1":"a","x10.1":"v","imp.1":"a","ilt1.1":"v","y11.1":"a","ix00.1":"a","iS2.1":"a","oldh0.1":"a","x00.1":"a","dq0.1":"v","hm1.1":"a","y01.1":"v","ix11.1":"v","inb2.1":"a","iclR1.1":"v","iBI.1":"a","it1s.1":"v","iD01.1":"v","iix.1":"v","Bg0.1":"v","inI.1":"a","iEc0.1":"v","ix01.1":"v","ib8.1":"a","Ec1.1":"a","ioldh1.1":"a","ihm1.1":"v","hm0.1":"a","iD00.2":"a","iy10.1":"a","ioldh0.1":"v","ib1.1":"a","Ec0.1":"a","iqh1.1":"v","idq1.1":"a"}})
+ADD, SUB, MUL, MAX, MIN = AluOpType.add, AluOpType.subtract, AluOpType.mult, AluOpType.max, AluOpType.min
+AF = ActivationFunctionType
+
+
+def build_ops(cfg):
+    ops, lastw, readers, bias, step = [], {}, {}, [0.0], [-1, {}]
+    ga, sca, pe, fix = cfg["gat"], cfg["sca"], cfg["pe"], cfg["fix"]
+
+    def add(alts, R, W, bank=None, kind="c", lat=0.0, sem=None, extra=()):
+        i = len(ops)
+        deps = set(extra)
+        for r in R:
+            if r in lastw:
+                deps.add(lastw[r])
+        for w in W:
+            if w in lastw:
+                deps.add(lastw[w])
+            deps.update(readers.get(w, ()))
+        for r in R:
+            readers.setdefault(r, []).append(i)
+        for w in W:
+            lastw[w] = i
+            readers[w] = []
+        deps.discard(i)
+        key = (list(W) or [sem])[-1].split("_")[0]
+        if kind != "c" or key[:2] in ("GR",):
+            key = key[:2] + key[3:]
+        if key[:2] not in ("MX", "Dm"):
+            step[1][key] = step[1].get(key, 0) + 1
+            key += ".%d" % step[1][key]
+        key = ("i" if step[0] < 1 else "") + key
+        ops.append({"alts": alts, "deps": deps, "bank": bank, "kind": kind, "lat": lat, "sem": sem, "W": list(W) or [sem], "key": key, "bias": bias[0]})
+        return i
+
+    def V(fn, n, R, W, bank=None):
+        return add({"v": (fix + max(64.0, n), fn)}, R, W, bank)
+
+    def A(fn, n, R, W, bank=None):
+        return add({"a": (fix + max(64.0, n), fn)}, R, W, bank)
+
+    def VA(fv, nv, fa, na, R, W, bank=None):
+        return add({"v": (fix + max(64.0, nv), fv), "a": (fix + max(64.0, na), fa)}, R, W, bank)
+
+    def PE(fn, cyc, R, W, bank):
+        def run(g, T, x):
+            last = None
+            for (o, l, r, s0, s1) in fn(T):
+                last = g.tensor.matmul(o, l, r, s0, s1)
+            return last
+        return add({"p": (cyc * pe, run)}, R, W, bank)
+
+    def GP(fn, n, R, W):
+        return add({"g": (150.0 + 2.0 * n, fn)}, R, W)
+
+    def DMA(q, name, fn, nbytes, R, W):
+        return add({q: (60.0, fn)}, R, W, kind="d", lat=2000.0 + nbytes / 200.0, sem=name)
+
+    def SEND(name, t, src, dst, nbytes, R, W, extra=()):
+        def run(g, T, x):
+            rid, pid, mask = x["to"][t]
+            return g.remote_dma(dst(T), src(T), T.sem["r" + name], T.sem["l" + name], pid, rid, mask)
+        s = add({"g": (400.0, run)}, R, [], kind="s", lat=1500.0 + nbytes / cfg["bw"], sem="l" + name, extra=extra)
+        add({}, [], W, kind="r", lat=500.0, sem="r" + name, extra=(s,))
+        return s
+
+    gv = lambda n: 60.0 + ga * n - fix
+    gs = lambda n: 60.0 + sca * n - fix
+    num = lambda a, T: a if a is None or isinstance(a, (int, float)) else a(T)
+    ts = lambda o, i, a, b, p, q=None: (lambda g, T, x: g.vector.tensor_scalar(o(T), i(T), num(a, T), num(b, T), *([p] if q is None else [p, q])))
+    tt = lambda o, i, j, p: (lambda g, T, x: g.vector.tensor_tensor(o(T), i(T), j(T), p))
+    cp = lambda o, i: (lambda g, T, x: g.vector.tensor_copy(o(T), i(T)))
+    scan = lambda o, a, b, p, q: (lambda g, T, x: g.vector.tensor_tensor_scan(o(T), a(T), b(T), 0.0, p, q))
+    act = lambda o, i, f, b=0.0, s=1.0: (lambda g, T, x: g.scalar.activation(o(T), i(T), f, bias=num(b, T), scale=s) if b != 0.0 else g.scalar.activation(o(T), i(T), f, scale=s))
+    mset = lambda o, c: (lambda g, T, x: g.vector.memset(o(T), c))
+    S = lambda name, a=None, b=None, c=None: (lambda T: T[name][:, a:b:c])
+    IND = lambda name, a, b, off, c, d: (lambda T: T[name][:, a:b].indirect(T[off][:, c:d]))
+    AND, SHR = AluOpType.bitwise_and, AluOpType.arith_shift_right
+    EQ, GT, GE, LT = AluOpType.is_equal, AluOpType.is_gt, AluOpType.is_ge, AluOpType.is_lt
+
+    def GAT(o, src, n, R, W, scale=1.0, bias=0.0):
+        fv = ts(o, src, bias, None, ADD) if bias else (ts(o, src, scale, None, MUL) if scale != 1.0 else cp(o, src))
+        return VA(fv, gv(n), act(o, src, AF.Identity if bias else AF.Copy, bias, scale), gv(n) + 15, R, W)
+
+    ld = lambda o, i: (lambda g, T, x: x["q"].dma_start(o(T), i(T)))
+    gsp = cfg["gsp"]
+    gw = 1024 // gsp
+    gi = ["Gi%d" % j for j in range(gsp)]
+    DMA("s", "dq", ld(S("q0"), lambda T: T.qd[:]), 32768, [], ["q0"])
+    DMA("s", "dw", ld(S("w0", 0, 1), lambda T: T.wt[:]), 256, [], ["w0"])
+    DMA("s", "dd0", ld(S("Dd"), lambda T: T.dr[:]), 131072, [], ["Dd"])
+    for j in range(gsp):
+        DMA("s", "dg%d" % j, ld(S("Gi", gw * j, gw * j + gw), lambda T, j=j: T.lg[:, gw * j:gw * j + gw]), 131072 + 4 * 128 * gw * (j + 1), [], [gi[j]])
+    DMA("s", "dx", ld(S("X"), lambda T: T.xr[:]), 1600000, [], ["X0", "X1"])
+    V(mset(S("thi"), 0), 4, [], ["thi"])
+    DMA("s", "dt", ld(lambda T: T.thi[0:128:16, 0:2], lambda T: T.th[:]), 64, [], ["thi"])
+    DMA("s", "de", ld(S("e0i"), lambda T: T.e0[:]), 65536, [], ["e0i"])
+    DMA("s", "dm", ld(lambda T: T.Dm[0:128:16, 0:4096], lambda T: T.dr[:]), 131072, [], ["Dm"])
+
+    io = lambda o, pat, cm=0, fl=True: (lambda g, T, x: g.iota(o(T), pat, 0, cm, allow_small_or_imprecise_dtypes=True) if fl else g.iota(o(T), pat, 0, cm))
+    GP(io(S("pI", 0, 1), [[1, 1]], 1, False), 1, [], ["pI"])
+    GP(io(S("colg"), [[1, 8], [0, 16]]), 128, [], ["colg"])
+    GP(io(S("colb"), [[0, 16], [1, 16]]), 256, [], ["colb"])
+    GP(io(S("col"), [[1, 144]]), 144, [], ["col"])
+    GP(io(S("aq", 0, 8), [[1, 8]]), 8, [], ["aq0"])
+    GP(io(S("aq", 8, 16), [[0, 2], [1, 4]]), 8, [], ["aq1"])
+    GP(io(S("iot"), [[1, 512]]), 512, [], ["iot"])
+    V(ts(S("pb", 0, 1), S("pI", 0, 1), 15, None, AND), 1, ["pI"], ["pb0"])
+    V(ts(S("pb", 1, 2), S("pI", 0, 1), 4, None, SHR), 1, ["pI"], ["pb1"])
+    V(cp(S("pc", 0, 2), S("pb", 0, 2)), 2, ["pb0", "pb1"], ["b", "gp"])
+    V(cp(S("pc", 2, 3), S("pI", 0, 1)), 1, ["pI"], ["p"])
+    pc = lambda j: S("pc", j, j + 1)
+    lin = lambda j, src, sc_, bi, R, W: VA(ts(pc(j), pc(src), float(sc_), float(bi), MUL, ADD), 1, act(pc(j), pc(src), AF.Identity, float(bi), float(sc_)), 1, R, W)
+    lin(3, 2, 1, 1, ["p"], ["p1"])
+    lin(4, 0, 1, 1, ["b"], ["b1"])
+    lin(5, 0, 8, 0, ["b"], ["b8"])
+    lin(6, 0, 32, 0, ["b"], ["b32"])
+    lin(7, 0, 1, 4096, ["b"], ["b4k"])
+    lin(8, 1, 16, 15, ["gp"], ["top"])
+    V(ts(pc(9), pc(0), 15.0, None, EQ), 1, ["b"], ["is15"])
+    lin(10, 9, 1.0 - 1.0 / 4096, 1.0 / 4096, ["is15"], ["mp"])
+    lin(11, 9, -0.5, 0.5, ["is15"], ["t1s"])
+    lin(12, 9, -1, 0, ["is15"], ["t1b"])
+    V(ts(pc(13), pc(0), 0.0, 1.0e6, EQ, MUL), 1, ["b"], ["t2b"])
+    V(ts(S("Bo"), S("colg"), pc(1), None, EQ), 128, ["colg", "gp"], ["Bo"])
+    scl = lambda o, i, k, n=128: VA(ts(S(o), S(i), float(k), None, MUL), n / 2, act(S(o), S(i), AF.Copy, 0.0, float(k)), n, [i], [o])
+    V(ts(S("W2"), S("Bo"), S("w0", 0, 1), 2.0, MUL, MUL), 64, ["Bo", "w0"], ["W2"])
+    scl("nBo", "Bo", -1)
+    scl("Bf", "Bo", 1)
+    V(ts(S("Id"), S("col", 0, 128), pc(2), None, EQ), 128, ["col", "p"], ["Id"])
+    scl("nI", "Id", -1)
+    scl("Idf", "Id", 1)
+    scl("nIf", "Id", -1)
+    lin(14, 0, -1, 0, ["b"], ["nb"])
+    lin(15, 0, -1, -0.5, ["b"], ["nb1"])
+    lin(16, 0, -2, -1, ["b"], ["nb2"])
+    scl("BI", "Id", 2048)
+    scl("nBI", "Id", -2048)
+    V(ts(S("Sh"), S("col", 0, 128), pc(3), -2048.0, EQ, MUL), 128, ["col", "p1"], ["Sh"])
+    V(ts(S("tmp"), S("col", 0, 128), pc(2), None, GE), 128, ["col", "p"], ["tmp"])
+    V(tt(S("Tri"), S("tmp"), S("Bo"), MUL), 256, ["tmp", "Bo"], ["Tri"])
+    V(ts(S("tmp2"), S("colb"), pc(0), None, GT), 256, ["colb", "b"], ["tmp2"])
+    V(ts(S("ms"), S("colb"), pc(4), 4096.0, EQ, MUL), 256, ["colb", "b1"], ["ms"])
+    V(tt(S("ms", 0, 128), S("ms", 0, 128), S("tmp2", 0, 128), MAX), 256, ["ms", "tmp2"], ["ms0"])
+    V(tt(S("ms", 128, 256), S("ms", 128, 256), S("tmp2", 128, 256), MAX), 256, ["ms", "tmp2"], ["ms1"])
+    V(ts(S("poi"), S("colb", 0, 128), pc(0), -8192.0, GE, MUL), 128, ["colb", "b"], ["poi"])
+    V(ts(S("dl"), S("colb", 0, 128), pc(0), None, EQ), 128, ["colb", "b"], ["dl"])
+    V(mset(S("rp"), 1.0), 512, [], ["rp"])
+    V(mset(S("rp", 15, 1024, 16), 0.0), 64, [], ["rp"])
+    V(cp(S("r2"), S("rp", 0, 128)), 64, ["rp"], ["r2"])
+    V(mset(S("r2", 14, 128, 16), 8192.0), 8, [], ["r2"])
+    V(ts(S("S1"), S("col"), pc(8), None, EQ), 144, ["col", "top"], ["S1"])
+    scl("S2", "S1", 2, 144)
+    scl("Sn", "S1", -1, 144)
+    VA(ts(S("ix"), S("col", 0, 128), 16.0, 2048.0, MUL, ADD), 64, act(S("ix"), S("col", 0, 128), AF.Identity, 2048.0, 16.0), 128, ["col"], ["ix"])
+    V(mset(S("opn", 0, 128), 0.0), 64, [], ["opn0"])
+    V(mset(S("opn", 128, 256), -2048.0), 64, [], ["opn1"])
+    V(mset(S("c256"), 256.0), 128, [], ["c256"])
+    V(mset(S("o16th"), 0.0625), 64, [], ["o16th"])
+    V(cp(S("ast"), S("aq", 0, 8)), 8, ["aq0"], ["ast"])
+    V(ts(S("stw", 0, 8), S("aq", 8, 16), 128.0, pc(5), MUL, ADD), 8, ["aq1", "b8"], ["stw0"])
+    V(ts(S("stw", 8, 16), S("aq", 8, 16), 512.0, pc(6), MUL, ADD), 8, ["aq1", "b32"], ["stw1"])
+    V(mset(S("D0"), 0.0), 192, [], ["D00", "D01"])
+    V(mset(S("pm", 0, 1), 0.0), 1, [], ["pmz"])
+    V(cp(S("thf", 0, 2), S("thi", 0, 2)), 2, ["thi"], ["thf"])
+    PE(lambda T: [(T.P0[:, 128:130], T.Bf[:], T.thf[:, 0:2], True, True)], 256, ["Bf", "thf"], ["unw"], "P0")
+    V(ts(S("thc", 0, 1), S("P0", 128, 129), pc(11), pc(12), MUL, ADD), 1, ["unw", "t1s", "t1b"], ["th1"], "P0")
+    V(ts(S("thc", 1, 2), S("P0", 129, 130), 0.5, pc(13), MUL, ADD), 1, ["unw", "t2b"], ["th2"], "P0")
+    V(ts(S("thc", 2, 4), S("thc", 0, 2), -1.0, -0.25, MUL, ADD), 1, ["th1", "th2"], ["nth"])
+    VA(ts(S("qh"), S("q0"), 0.5, None, MUL), 64, act(S("qh"), S("q0"), AF.Copy, 0.0, 0.5), 128, ["q0"], ["qh0", "qh1"])
+    V(cp(S("tri", 2, 384, 3), S("e0i")), 128, ["e0i"], ["tri0", "tri1"])
+    for j in range(4):
+        V(cp(S("G", 256 * j, 256 * j + 256), S("Gi", 256 * j, 256 * j + 256)), 256, gi, ["G%d" % (j // 2)])
+
+    gch = cfg["gch"]
+    nch = 1024 // gch
+    halves = lambda k: [[0, 1]] if k == 1 else [[0], [1]]
+    for t in range(STEPS):
+        last = t == STEPS - 1
+        step[0], step[1] = t, {}
+        GR, DR = "GR%d" % t, "DR%d" % t
+        GO, gtag = ("G", ["G0", "G1"]) if t else ("Gi", gi)
+        rtag = [GR + "a", GR + "b"]
+        bulk = lambda extra, t=t: SEND("g%d" % (t + 1), t + 1, S("G"), S("GR%d" % (t + 1)), 524288, ["G0", "G1"], ["GR%da" % (t + 1), "GR%db" % (t + 1)], extra)
+        if 1 <= t < STEPS - 1:
+            bulk(())
+        if t:
+            for h in range(2):
+                V(cp(IND(GR, 512 * h, 512 * h + 512, "CR%d" % t, 4 * h, 4 * h + 4), S("ER%d" % t, 64 * h, 64 * h + 64)), gs(64),
+                  ["CR%d" % t, "ER%d%d" % (t, h)], [GR + "ab"[h]])
+        for hs in halves(cfg["nu"] if t else 1):
+            tg = lambda s, hs=hs: [s + str(h) for h in hs]
+            TB = "T%d" % hs[0]
+            bias[0] = cfg["bu"] * (1 - hs[0]) * (len(hs) == 1)
+            c0, n = 64 * hs[0], 64 * len(hs)
+            c1, w0, nw, s0 = c0 + n, c0 // 16, n // 16, 2 * c0
+            w1, n0 = w0 + nw, 2 * w0
+            PE(lambda T, TB=TB, c0=c0, c1=c1, n=n: [(T[TB][:, 0:n], T.Bo[:], T.c256[:, 0:n], True, False), (T[TB][:, 0:n], T.W2[:], T.qh[:, c0:c1], False, True)], 2 * n,
+               ["Bo", "c256", "W2"] + tg("qh"), [TB], TB)
+            V(scan(S("sc", s0, s0 + n), S("ms", 0, n), S(TB, 0, n), MUL, MAX), n, ["ms0"], [TB] + tg("sc"), TB)
+            V(ts(S("ui", w0, w1), S("sc", s0 + 15, s0 + n, 16), pc(10), None, MUL), 4, tg("sc") + ["mp"], tg("ui"))
+            V(ts(S("u", w0, w1), S("ui", w0, w1), 4095, None, AND), 4, tg("ui"), tg("u"))
+            V(tt(S("sq", w0, w1), S("u", w0, w1), S("u", w0, w1), MUL), 4, tg("u"), tg("sq"))
+            if t:
+                V(ts(S("lin", w0, w1), S("u", w0, w1), 37.0, S("Ac", 0, 1), MUL, ADD), 4, tg("u") + ["Ac"], tg("lin"))
+            else:
+                V(ts(S("lin", w0, w1), S("u", w0, w1), 37.0, None, MUL), 4, tg("u"), tg("lin"))
+            V(ts(S("sq5", w0, w1), S("sq", w0, w1), 5, None, SHR), 4, tg("sq"), tg("sq5"))
+            V(tt(S("sm", w0, w1), S("sq5", w0, w1), S("lin", w0, w1), ADD), 4, tg("sq5") + tg("lin"), tg("sm"))
+            V(ts(S("nlh", n0, n0 + nw), S("sm", w0, w1), 255, None, AND), 4, tg("sm"), tg("nlo"))
+            V(ts(S("nlh", n0 + nw, n0 + 2 * nw), S("sm", w0, w1), 8, 15, SHR, AND), 4, tg("sm"), tg("nhi"))
+            V(cp(S("n16", n0, n0 + 2 * nw), S("nlh", n0, n0 + 2 * nw)), 8, tg("nlo") + tg("nhi"), tg("n16"))
+            if cfg["hmv"]:
+                V(cp(S("hm", c0, c1), IND("dl", 0, 16, "n16", n0 + nw, n0 + 2 * nw)), gv(n), ["dl"] + tg("n16"), tg("hm"))
+            else:
+                GAT(S("hm", c0, c1), IND("dl", 0, 16, "n16", n0 + nw, n0 + 2 * nw), n, ["dl"] + tg("n16"), tg("hm"))
+            V(tt(S("cand", s0, s0 + n), IND("Dd", 0, 256, "n16", n0, n0 + nw), S("hm", c0, c1), MUL), gv(n), ["Dd"] + tg("n16") + tg("hm"), tg("caP"))
+            if t:
+                V(tt(S("cand", s0 + n, s0 + 2 * n), IND(DR, 0, 256, "n16", n0, n0 + nw), S("hm", c0, c1), MUL), gv(n), [DR] + tg("n16") + tg("hm"), tg("caB"))
+            else:
+                SEND("nb", "b", S("n16"), S("nq"), 4096, tg("n16"), ["nq"])
+                GAT(S("hq"), IND("dl", 0, 16, "nq", 8, 16), n, ["dl", "nq"], ["hq"])
+                V(tt(S("cand", n, 2 * n), IND("Dd", 0, 256, "nq", 0, 8), S("hq"), MUL), gv(n), ["Dd", "nq", "hq"], tg("caB"))
+            if t and not cfg["csp"]:
+                parts = [(0, 2 * n, tg("caP") + tg("caB"), tg("cP") + tg("cB"))]
+            else:
+                parts = [(0, n, tg("caP"), tg("cP")), (n, 2 * n, tg("caB"), tg("cB"))]
+            for (a, b, R, W) in parts:
+                PE(lambda T, TB=TB, a=a, b=b, s0=s0, n=n: [(T[TB][:, n + a:n + b], T.Bo[:], T.c256[:, a:b], True, False),
+                                                         (T[TB][:, n + a:n + b], T.Bf[:], T.cand[:, s0 + a:s0 + b], False, True)], 5 * (b - a), ["Bo", "c256", "Bf"] + R, [TB], TB)
+                V(scan(S("sc", s0 + a, s0 + b), S("ms", 0, b - a), S(TB, n + a, n + b), MUL, MAX), b - a, ["ms0", "ms1"] if b - a > 128 else ["ms0"], [TB] + tg("sc"), TB)
+                V(ts(S("c16", n0 + a // 16, n0 + b // 16), S("sc", s0 + a + 15, s0 + b, 16), pc(10), -4096.0, MUL, ADD), 8, tg("sc") + ["mp"], W)
+            own, oth = IND(GO, 0, 1024, "c16", n0, n0 + nw), IND(GR, 0, 1024, "c16", n0 + nw, n0 + 2 * nw)
+            if t == 0:
+                V(cp(S("PB", c0, c1), own), gv(n), gtag + tg("cP"), tg("P16"))
+                V(cp(S("Bq"), IND(GO, 0, 1024, "c16", 8, 16)), gv(n), gtag + tg("cB"), ["Bq"])
+                bulk((SEND("b0", 0, S("Bq"), S("PB", 128, 256), 32768, ["Bq"], tg("B16")),))
+                V(cp(S("Pf"), S("PB", 0, 128)), n, tg("P16"), tg("Pf"))
+                V(cp(S("Bg"), S("PB", 128, 256)), n, tg("B16"), tg("Bg"))
+            else:
+                GAT(S("Pf", c0, c1), own, n, gtag + tg("cP"), tg("Pf"))
+                GAT(S("Bg", c0, c1), oth, n, rtag + tg("cB"), tg("Bg"))
+                if cfg["pcv"] & 1:
+                    V(cp(S("PB", c0, c1), S("Pf", c0, c1)), n, tg("Pf"), tg("P16"))
+                else:
+                    V(cp(S("PB", c0, c1), own), gv(n), gtag + tg("cP"), tg("P16"))
+                if cfg["pcv"] & 2:
+                    V(cp(S("PB", 128 + c0, 128 + c1), S("Bg", c0, c1)), n, tg("Bg"), tg("B16"))
+                else:
+                    V(cp(S("PB", 128 + c0, 128 + c1), oth), gv(n), rtag + tg("cB"), tg("B16"))
+        bias[0] = 0.0
+        for h in range(2):
+            TB, a0, a3 = "T%d" % h, 64 * h, 192 * h
+            PE(lambda T, TB=TB, a0=a0, a3=a3: [(T[TB][:, 1:192:3], T.Idf[:], T.Pf[:, a0:a0 + 64], True, False), (T[TB][:, 1:192:3], T.nIf[:], T.tri[:, a3 + 2:a3 + 192:3], False, True),
+                                             (T[TB][:, 2:192:3], T.Idf[:], T.tri[:, a3 + 2:a3 + 192:3], True, True)], 768, ["Idf", "nIf", "Pf%d" % h, "tri%d" % h], [TB], TB)
+            PE(lambda T, TB=TB, a0=a0: [(T[TB][:, 0:192:3], T.Idf[:], T.Bg[:, a0:a0 + 64], True, False), (T[TB][:, 0:192:3], T.nIf[:], T.Pf[:, a0:a0 + 64], False, True)], 512,
+               ["Idf", "nIf", "Pf%d" % h, "Bg%d" % h], [TB], TB)
+        for z, nm in ((0, "x"), (1, "y")):
+            for h in range(2):
+                for j in range(nch):
+                    o0 = 2048 * z + 1024 * h + gch * j
+                    f0 = 128 * z + 64 * h + gch // 16 * j
+                    bias[0] = cfg["bg"] * (2048 - 1024 * h - gch * j) / 512.0 - cfg["by"] * z
+                    GAT(S("XY", o0, o0 + gch), IND("X", 0, 4096, "PB", f0, f0 + gch // 16), gch, ["X0", "X1", "PB"[z] + "16" + str(h)], ["%s%d%d" % (nm, h, j)], 0.5)
+        bias[0] = 0.0
+        V(ts(S("clx0", 0, 8), S("u"), 7, None, AND), 8, ["u0", "u1"], ["cl0"])
+        V(ts(S("clx0", 8, 16), S("u"), 31, None, AND), 8, ["u0", "u1"], ["cx0"])
+        V(tt(S("clx1"), S("clx0"), S("stw"), ADD), 32, ["cl0", "cx0", "stw0", "stw1"], ["clx1"])
+        V(cp(S("clx"), S("clx1")), 16, ["clx1"], ["clx"])
+        for h in range(2):
+            GAT(S("oldh", 64 * h, 64 * h + 64), IND("X", 2048 * h, 2048 * h + 2048, "clx", 8 + 4 * h, 12 + 4 * h), 64, ["X%d" % h, "clx"], ["oldh%d" % h], 0.5)
+        if not last:
+            SEND("c%d" % (t + 1), t + 1, S("clx", 0, 8), S("CR%d" % (t + 1)), 2048, ["clx"], ["CR%d" % (t + 1)])
+            for h in range(2):
+                GAT(S("clR", 64 * h, 64 * h + 64), IND("iot", 0, 512, "clx", 4 * h, 4 * h + 4), 64, ["iot", "clx"], ["clR%d" % h], 1.0, 512.0 * h)
+            V(ts(S("n32"), S("sm"), 4095, None, AND), 8, ["sm0", "sm1"], ["n32"])
+            V(cp(S("nf"), S("n32")), 8, ["n32"], ["nf"])
+            GAT(S("bc"), IND("nf", 0, 8, "ast", 0, 8), 128, ["nf", "ast"], ["bc"])
+            V(tt(S("x1"), S("bc"), S("dl"), MUL), 256, ["bc", "dl"], ["x1"])
+            PE(lambda T: [(T.P0[:, 128:256], T.Id[:], T.poi[:], True, False), (T.P0[:, 128:256], T.Bf[:], T.x1[:], False, True)], 640, ["Id", "poi", "Bf", "x1"], ["unw"], "P0")
+            V(tt(S("eq"), S("P0", 128, 256), S("bc"), EQ), 128, ["unw", "bc"], ["eq"], "P0")
+            V(scan(S("eqs"), S("eq"), S("r2"), MAX, MUL), 64, ["eq", "r2"], ["eqs"])
+            V(tt(S("tt"), S("eqs", 14, 128, 16), S("nf"), ADD), 16, ["eqs", "nf"], ["tt"])
+            V(ts(S("o16", 0, 16, 2), S("tt"), pc(7), None, MIN), 8, ["tt", "b4k"], ["o16"])
+            for a in range(7, -1, -1):
+                V(cp(IND("Dm", 0, 4112, "o16", 2 * a, 2 * a + 1), S("clR", 16 * a, 16 * a + 16)), gs(16), ["o16", "clR%d" % (a // 4)], ["Dm"])
+            DMA("s", "dd%d" % (t + 1), ld(S("Dd"), lambda T: T.Dm[0:128:16, 0:4096]), 131072, ["Dm"], ["Dd"])
+            SEND("d%d" % (t + 1), t + 1, S("Dd"), S("DR%d" % (t + 1)), 131072, ["Dd"], ["DR%d" % (t + 1)])
+        xs = [["x%d%d" % (h, j) for j in range(nch)] for h in range(2)]
+        ys = [["y%d%d" % (h, j) for j in range(nch)] for h in range(2)]
+        for h in range(2):
+            k0 = 1024 * h
+            for c in range(2):
+                Y, o0 = "Y%d%d" % (h, c), k0 + 512 * c
+                part = slice(c * nch // 2, (c + 1) * nch // 2) if nch > 1 else slice(0, 1)
+                PE(lambda T, Y=Y, o0=o0: [(T[Y][:], T.Id[:], T.XY[:, o0:o0 + 512], True, False)], 512, ["Id"] + xs[h][part], [Y], Y)
+                PE(lambda T, Y=Y, o0=o0: [(T[Y][:], T.nI[:], T.XY[:, 2048 + o0:2048 + o0 + 512], False, True)], 512, ["nI"] + ys[h][part], [Y], Y)
+                bias[0] = cfg["ba"]
+                A(act(S("A1", o0, o0 + 512), S(Y), AF.Abs), 512, [], [Y, "A1%d%d" % (h, c)], Y)
+                bias[0] = 0.0
+            V(scan(S("pm", 1 + k0, 1 + k0 + 1024), S("XY", k0, k0 + 1024), S("rp"), MAX, MUL), 512, xs[h] + ["rp"], ["pm%d" % h])
+        for hs in halves(cfg["nm"]):
+            tg = lambda s, hs=hs: [s + str(h) for h in hs]
+            full = len(hs) == 2
+            h0 = hs[0]
+            TB, T2, PB_, PO = ("T0", "T1", "P0", "P1") if full else ("T%d" % h0, "T%d" % h0, "P%d" % h0, "P%d" % (1 - h0))
+            c0, n = 64 * h0, 64 * len(hs)
+            c1, w0, w1, s0, k0, k1, b3, b4 = c0 + n, c0 // 16, (c0 + n) // 16, 2 * c0, 16 * c0, 16 * (c0 + n), 3 * c0, 3 * (c0 + n)
+            r1, rc, rs, r2, rl = (384, 0, 128, 0, 0) if full else (192, 256, 320, 384, 64)
+            X_ = [a for h in hs for a in xs[h]]
+            allx = [a for h in range(hs[-1] + 1) for a in xs[h]]
+            ally = [a for h in range(hs[-1] + 1) for a in ys[h]]
+            pw = 1024 * (hs[-1] + 1)
+            d_ = lambda T, c0=c0, c1=c1: T.dh[:, c0:c1]
+            bias[0] = cfg["bh"] * (1 - h0) * (not full)
+            for h in hs:
+                PE(lambda T, TB=TB, k0=1024 * h, r1=r1 + 64 * (h - h0): [(T[TB][:, r1:r1 + 64], T.S1[:, 15 - k:143 - k], T.A1[:, k0 + k:k0 + 1024:16], k == 0, k == 15) for k in range(16)], 1024,
+                   ["S1"] + ["A1%d%d" % (h, c) for c in range(2)], [TB], TB)
+            for h in hs:
+                for c in range(2):
+                    Y = "Y%d%d" % (h, c)
+                    PE(lambda T, Y=Y, o0=2048 + 1024 * h + c, o1=3072 + 1024 * h: [(T[Y][:], T.Id[:], T.XY[:, o0:o1:2], True, False)], 512, ["Id"] + ys[h], [Y], Y)
+            if cfg["sgn"] & 1:
+                A(act(S("ov", c0, c1), S(TB, r1, r1 + n), AF.Sign, S("thc", 2, 3)), n, ["nth"], [TB] + tg("ov"), TB)
+            else:
+                V(ts(S("ov", c0, c1), S(TB, r1, r1 + n), S("thc", 0, 1), None, GT), n, ["th1"], [TB] + tg("ov"), TB)
+            PE(lambda T, TB=TB, c0=c0, c1=c1, rc=rc, n=n: [(T[TB][:, rc:rc + n], T.Tri[:], T.ov[:, c0:c1], True, True)], n, ["Tri"] + tg("ov"), [TB], TB)
+            lv, lb = (pc(15), pc(14)) if cfg["sgn"] & 1 else (0.5, 1.0)
+            VA(ts(S("lt", c0, c1), S(TB, rc, rc + n), lv, None, LT), n, act(S("lt", c0, c1), S(TB, rc, rc + n), AF.Relu, lb, -1.0), n, ["nb", "nb1"], [TB] + tg("lt"), TB)
+            PE(lambda T, TB=TB, c0=c0, c1=c1, rs=rs, n=n: [(T[TB][:, rs:rs + n], T.Id[:], T.ix[:, c0:c1], True, False), (T[TB][:, rs:rs + n], T.Bo[:], T.lt[:, c0:c1], False, True)], 2 * n,
+               ["Id", "ix", "Bo"] + tg("lt"), [TB], TB)
+            V(scan(S("sc", s0, s0 + n), S("ms", 0, n), S(TB, rs, rs + n), MUL, MAX), n, ["ms0"], [TB] + tg("sc"), TB)
+            V(ts(S("s16", w0, w1), S("sc", s0 + 15, s0 + n, 16), pc(10), -2048.0, MUL, ADD), 4, tg("sc") + ["mp"], tg("s16"))
+            dx = lambda T, B=T2, r2=r2, n=n: T[B][:, r2:r2 + n]
+            dy = lambda T, B=T2, r2=r2, n=n: T[B][:, r2 + n:r2 + 2 * n]
+            opened = lambda T, B=T2, r2=r2, n=n: [(T[B][:, r2:r2 + 2 * n], T.Id[:], T.opn[:, 128 - n:128 + n], True, False)]
+            corr = lambda T, dx=dx, k0=k0, k1=k1, ks=range(16): [(dx(T), T.Sn[:, 15 - k:143 - k], T.XY[:, k0 + k:k1:16], False, False) for k in ks]
+            PE(lambda T, o=opened, c=corr: o(T) + c(T, ks=range(1, 8)), 9 * n, ["Id", "opn0", "opn1", "Sn"] + X_, [T2], T2)
+            PE(lambda T, c=corr: c(T, ks=range(8, 16)), 8 * n, ["Sn"] + X_, [T2], T2)
+            PE(lambda T, dx=dx, dy=dy, c0=c0, c1=c1: [(dx(T), T.Sh[:], T.lt[:, c0:c1], False, False), (dy(T), T.Sh[:], T.lt[:, c0:c1], False, False)], 2 * n, ["Sh"] + tg("lt"), [T2], T2)
+            V(tt(S("Mq", c0, c1), IND("pm", 0, pw, "s16", w0, w1), S("qh", c0, c1), SUB), gv(n), ["pmz", "pm0"] + tg("pm") + tg("s16") + tg("qh"), tg("Mq"))
+            A(act(S("dh", c0, c1), S("Mq", c0, c1), AF.Abs), n, tg("Mq"), tg("dh"))
+            PE(lambda T, B=PB_, d_=d_, n=n: [(T[B][:, 0:n], T.Id[:], d_(T), True, True)], n, ["Id"] + tg("dh"), tg("dps"), PB_)
+            for c in range(2):
+                for h in hs:
+                    Y = "Y%d%d" % (h, c)
+                    PE(lambda T, Y=Y, h=h: [(T[Y][:, j:512:8], T.nI[:], T.dh[:, 64 * h:64 * h + 64], False, j == 7) for j in range(8)], 512, ["nI", "dh%d" % h], [Y], Y)
+                    A(act(S("AY", 1024 * c + 512 * h, 1024 * c + 512 * h + 512), S(Y), AF.Abs), 512, [], [Y, "AY%d%d" % (h, c)], Y)
+            gx, gy = IND("XY", 0, pw, "s16", w0, w1), IND("XY", 2048, 2048 + pw, "s16", w0, w1)
+            if cfg["sda"]:
+                GAT(S("sd", s0, s0 + n), gx, n, allx + tg("s16"), tg("sdx"))
+                GAT(S("sd", s0 + n, s0 + 2 * n), gy, n, ally + tg("s16"), tg("sdy"))
+                PE(lambda T, B=PO, s0=s0, n=n, d_=d_: [(T[B][:, 256:256 + 2 * n], T.Id[:], T.sd[:, s0:s0 + 2 * n], True, False), (T[B][:, 256:256 + n], T.nI[:], d_(T), False, False),
+                                                     (T[B][:, 256 + n:256 + 2 * n], T.nI[:], d_(T), False, True)], 4 * n, ["Id", "nI"] + tg("sdx") + tg("sdy") + tg("dh"), tg("sp"), PO)
+                A(act(S("sa", s0, s0 + 2 * n), S(PO, 256, 256 + 2 * n), AF.Abs), 2 * n, tg("sp"), tg("sa"), PO)
+            else:
+                V(tt(S("sd", s0, s0 + n), gx, S("dh", c0, c1), SUB), gv(n), allx + tg("s16") + tg("dh"), tg("sdx"))
+                V(tt(S("sd", s0 + n, s0 + 2 * n), gy, S("dh", c0, c1), SUB), gv(n), ally + tg("s16") + tg("dh"), tg("sdy"))
+                A(act(S("sa", s0, s0 + 2 * n), S("sd", s0, s0 + 2 * n), AF.Abs), 2 * n, tg("sdx") + tg("sdy"), tg("sa"))
+            PE(lambda T, B=PO, s0=s0, n=n, rl=rl: [(T[B][:, rl:rl + n], T.Bo[:], T.sa[:, s0 + n:s0 + 2 * n], True, False), (T[B][:, rl:rl + n], T.nBo[:], T.sa[:, s0:s0 + n], False, True)], 2 * n,
+               ["Bo", "nBo"] + tg("sa"), tg("lp"), PO)
+            V(ts(S("lost", c0, c1), S(PO, rl, rl + n), 0.0, None, LT), n, tg("lp"), tg("lost"), PO)
+            VA(ts(S("dq", c0, c1), S("dh", c0, c1), -0.25, None, ADD), n, act(S("dq", c0, c1), S("dh", c0, c1), AF.Identity, -0.25), n, tg("dh"), tg("dq"))
+            for k in range(1, 16):
+                V(tt(S("MX", k0 + n * k, k0 + n * k + n), S("XY", k0 + k, k1, 16), S(PB_, 0, n), MAX), n, X_ + tg("dps"), ["MX%d_%d" % (h, k) for h in hs], PB_)
+            PE(lambda T, dx=dx, d_=d_: [(dx(T), T.nBo[:], d_(T), False, False)], n, ["nBo"] + tg("dh"), [T2], T2)
+            for j in range(4):
+                PE(lambda T, dx=dx, k0=k0, j=j, n=n: [(dx(T), T.S2[:, 15 - k:143 - k], T.MX[:, k0 + n * k:k0 + n * k + n], False, False) for k in range(max(1, 4 * j), 4 * j + 4)], 4 * n,
+                   ["S2"] + ["MX%d_%d" % (h, k) for h in hs for k in range(4 * j, 4 * j + 4)], [T2], T2)
+                if j % 2:
+                    c = j // 2
+                    PE(lambda T, dy=dy, o0=1024 * c + 8 * c0, c=c, n=n: [(dy(T), T.S1[:, 15 - (2 * i + c):143 - (2 * i + c)], T.AY[:, o0 + i:o0 + 8 * n:8], False, False) for i in range(8)], 8 * n,
+                       ["S1"] + ["AY%d%d" % (h, c) for h in hs], [T2], T2)
+                if j == 2:
+                    PE(lambda T, dx=dx, dy=dy, c0=c0, c1=c1: [(dx(T), T.nBI[:], T.lost[:, c0:c1], False, False), (dy(T), T.BI[:], T.lost[:, c0:c1], False, False)], 2 * n,
+                       ["nBI", "BI"] + tg("lost"), [T2], T2)
+            fn = ops[-1]["alts"]["p"]
+            o0 = 1024 + 8 * c0
+            ops[-1]["alts"]["p"] = (fn[0], lambda g, T, x, dy=dy, o0=o0, n=n: [g.tensor.matmul(dy(T), T.S1[:, 14 - 2 * i:142 - 2 * i], T.AY[:, o0 + i:o0 + 8 * n:8], False, i == 7) for i in range(8)][-1])
+            PE(lambda T, B=PO, c0=c0, c1=c1: [(T[B][:, 384:448], T.Id[:], T.lost[:, c0:c1], True, False), (T[B][:, 384:448], T.nI[:], T.lt[:, c0:c1], False, True)], 2 * n,
+               ["Id", "nI"] + tg("lost") + tg("lt"), tg("mq"), PO)
+            mm = S("D0", b3 + 1, b4, 3)
+            VA(ts(mm, S(PO, 384, 448), 0.0, None, MAX), n, act(mm, S(PO, 384, 448), AF.Relu), n, tg("mq"), tg("D0"), PO)
+            if cfg["sgn"] & 2:
+                A(act(S("o2", s0, s0 + 2 * n), S(T2, r2, r2 + 2 * n), AF.Sign, S("thc", 3, 4)), 2 * n, ["nth"], [T2] + tg("o2"), T2)
+            else:
+                V(ts(S("o2", s0, s0 + 2 * n), S(T2, r2, r2 + 2 * n), S("thc", 1, 2), None, GT), 2 * n, ["th2"], [T2] + tg("o2"), T2)
+            PE(lambda T, TB=TB, s0=s0, rc=rc, n=n: [(T[TB][:, rc:rc + n], T.Tri[:], T.o2[:, s0:s0 + n], True, False), (T[TB][:, rc:rc + n], T.Tri[:], T.o2[:, s0 + n:s0 + 2 * n], False, True)], 2 * n,
+               ["Tri"] + tg("o2"), [TB], TB)
+            l2 = S("D0", b3 + 2, b4, 3)
+            lv, lb, ls = (pc(16), pc(14), -0.5) if cfg["sgn"] & 2 else (0.5, 1.0, -1.0)
+            VA(ts(l2, S(TB, rc, rc + n), lv, None, LT), n, act(l2, S(TB, rc, rc + n), AF.Relu, lb, ls), n, ["nb", "nb2"], [TB] + tg("D0"), TB)
+
+            def wrap_e(TB=TB, s0=s0, n=n, rs=rs, tg=tg):
+                V(scan(S("sc", s0, s0 + n), S("ms", 0, n), S(TB, rs, rs + n), MUL, MAX), n, ["ms0"], [TB] + tg("sc"), TB)
+            PE(lambda T, TB=TB, c0=c0, c1=c1, l2=l2, rs=rs, n=n: [(T[TB][:, rs:rs + n], T.Id[:], T.ix[:, c0:c1], True, False), (T[TB][:, rs:rs + n], T.BI[:], T.lost[:, c0:c1], False, False),
+                                                                (T[TB][:, rs:rs + n], T.Bo[:], l2(T), False, True)], 3 * n,
+               ["Id", "ix", "BI", "Bo"] + tg("lost") + tg("D0"), [TB], TB)
+            if not cfg["efi"]:
+                wrap_e()
+            for h in hs:
+                H, a0, a3 = str(h), 64 * h, 192 * h
+                V(scan(S("tri", a3, a3 + 192), S("D0", a3, a3 + 192), S(TB, 0, 192), MUL, ADD), 192, ["D0" + H], [TB, "tri" + H], TB)
+                en = S("tri", a3 + 2, a3 + 192, 3)
+                if not last:
+                    ec = S("Ec", a0, a0 + 64)
+                    VA(cp(ec, en), 64, act(ec, en, AF.Copy), 64, ["tri" + H], ["Ec" + H])
+                    if not full:
+                        SEND("e%d%d" % (t + 1, h), t + 1, ec, S("ER%d" % (t + 1), a0, a0 + 64), 32768, ["Ec" + H], ["ER%d%d" % (t + 1, h)])
+                V(cp(IND("G", 512 * h, 512 * h + 512, "clx", 4 * h, 4 * h + 4), en), gs(64), ["clx", "tri" + H], ["G" + H])
+            if full and not last:
+                SEND("e%d" % (t + 1), t + 1, S("Ec"), S("ER%d" % (t + 1)), 65536, ["Ec0", "Ec1"], ["ER%d0" % (t + 1), "ER%d1" % (t + 1)])
+            if cfg["efi"]:
+                wrap_e()
+            V(ts(S("e16", w0, w1), S("sc", s0 + 15, s0 + n, 16), pc(10), -2049.0, MUL, ADD), 4, tg("sc") + ["mp"], tg("e16"))
+            V(tt(S("qi", c0, c1), IND("XY", 0, 2048 + pw, "e16", w0, w1), S("dq", c0, c1), ADD), gv(n), xs[0] + xs[1] + ally + tg("e16") + tg("dq"), tg("qi"))
+            if last:
+                V(cp(S("yqb", c0, c1), S("qi", c0, c1)), n, tg("qi"), tg("yq"))
+            else:
+                V(ts(S("qh", c0, c1), S("qi", c0, c1), 0.5, None, MUL), n, tg("qi"), tg("qh"))
+            PE(lambda T, B=PO, c0=c0, c1=c1, d_=d_: [(T[B][:, 448:512], T.Id[:], T.oldh[:, c0:c1], True, False), (T[B][:, 448:512], T.Id[:], d_(T), False, True)], 2 * n,
+               ["Id"] + tg("oldh") + tg("dh"), tg("xp"), PO)
+            V(ts(S("xi", c0, c1), S(PO, 448, 512), -0.25, None, ADD), n, tg("xp"), tg("xi"), PO)
+            for h in hs:
+                H = str(h)
+                V(cp(IND("X", 2048 * h, 2048 * h + 2048, "clx", 8 + 4 * h, 12 + 4 * h), S("xi", 64 * h, 64 * h + 64)), gs(64), ["clx", "xi" + H], ["X" + H])
+                if last:
+                    DMA("s", "ox" + H, ld(lambda T, h=h: T.yx[:, 2048 * h:2048 * h + 2048], S("X", 2048 * h, 2048 * h + 2048)), 524288, ["X" + H], [])
+                    DMA("s", "ol" + H, ld(lambda T, h=h: T.yl[:, 512 * h:512 * h + 512], S("G", 512 * h, 512 * h + 512)), 262144, ["G" + H], [])
+        bias[0] = 0.0
+        if last:
+            DMA("s", "oq", ld(lambda T: T.yq[:], S("yqb")), 32768, ["yq0", "yq1"], [])
+        else:
+            PE(lambda T: [(T.P1[:, 128:192], T.o16th[:], T.lost[:, 0:64], True, False), (T.P1[:, 128:192], T.o16th[:], T.lost[:, 64:128], False, True)], 128,
+               ["o16th", "lost0", "lost1"], ["Ap"], "P1")
+            V(lambda g, T, x: g.vector.tensor_reduce(T.Ac[:, 0:1], T.P1[:, 128:192], AxisListType.X, ADD), 64, ["Ap"], ["Ac"], "P1")
+    return ops
+
+
+def schedule(ops, cfg, fixed=None):
+    n, wake = len(ops), cfg["wake"]
+    succ = [[] for _ in range(n)]
+    for i, o in enumerate(ops):
+        for d in o["deps"]:
+            succ[d].append(i)
+    seed = [cfg["seed"] * 7919 + 12345]
+
+    def rnd():
+        seed[0] = (seed[0] * 1103515245 + 12345) % 2147483648
+        return seed[0] / 2147483648.0
+    prio = [0.0] * n
+    for i in range(n - 1, -1, -1):
+        c = min([a[0] for a in ops[i]["alts"].values()] or [0.0]) + ops[i]["lat"]
+        prio[i] = c + wake + max([prio[s] for s in succ[i]] or [0.0])
+    prio = [p + cfg["noise"] * rnd() + o["bias"] + cfg["B"].get(o["key"], 0.0) for p, o in zip(prio, ops)]
+    engs = [[cfg["E"][o["key"]]] if len(o["alts"]) == 2 and o["key"] in cfg["E"] else list(o["alts"]) for o in ops]
+    rdy = [0.0] * n
+    left = [len(o["deps"]) for o in ops]
+    fin, eng = [0.0] * n, [None] * n
+    free = {e: 0.0 for e in "vapgs"}
+    order = {e: [] for e in "vapgs"}
+    banks = {}
+    more = [set() for _ in range(n)]
+    ready = [i for i in range(n) if left[i] == 0]
+
+    def done(i):
+        for s in succ[i]:
+            left[s] -= 1
+            if left[s] == 0:
+                if ops[s]["kind"] == "r":
+                    fin[s] = fin[i] + ops[s]["lat"]
+                    eng[s] = "r"
+                    done(s)
+                else:
+                    pe_ = engs[s][0] == "p"
+                    rdy[s] = max([fin[d] + wake for d in ops[s]["deps"] if not (pe_ and eng[d] == "p")] or [0.0])
+                    ready.append(s)
+
+    def start(i, e):
+        t = max(free[e], rdy[i])
+        b = ops[i]["bank"]
+        if b:
+            for e2, j in banks.get(b, {}).items():
+                if e2 != e:
+                    t = max(t, fin[j] + wake)
+        return t
+    while ready:
+        cands = []
+        for i in ready:
+            es = engs[i]
+            if len(es) == 1:
+                cands.append((start(i, es[0]), i, es[0]))
+                continue
+            sv, sa = start(i, "v"), start(i, "a")
+            cands.append((sa, i, "a"))
+            if sa - sv >= cfg["vpen"]:
+                cands.append((sv, i, "v"))
+        t0, _, e0 = min(cands)
+        near = [c for c in cands if c[2] == e0 and c[0] <= t0 + cfg["look"]]
+        t, i, e = max(near, key=lambda c: prio[c[1]] - (c[0] - t0))
+        fits = [c for c in near if c[0] + ops[c[1]]["alts"][e][0] <= t + cfg["slack"] and c[0] < t]
+        if fits:
+            t, i, e = max(fits, key=lambda c: prio[c[1]])
+        ready.remove(i)
+        cost = ops[i]["alts"][e][0]
+        free[e] = t + cost
+        fin[i] = t + cost + ops[i]["lat"]
+        eng[i] = e
+        order[e].append(i)
+        b = ops[i]["bank"]
+        if b:
+            more[i].update(j for e2, j in banks.get(b, {}).items() if e2 != e)
+            banks.setdefault(b, {})[e] = i
+        done(i)
+    return order, eng, more, max(fin), fin
+
+
+def plan(cfg):
+    ops = build_ops(cfg)
+    order, eng, more, total, fin = schedule(ops, cfg)
+    token = {}
+    for e in "vapg":
+        k = 0
+        for i in order[e]:
+            if ops[i]["kind"] == "c":
+                k += 1
+                token[i] = ("c" + e, k)
+    for i, o in enumerate(ops):
+        if o["kind"] == "d":
+            token[i] = (o["sem"], 16)
+        elif o["kind"] in "sr":
+            token[i] = (o["sem"], -1)
+    know, waits = {}, {}
+    clock = {e: {} for e in "vapgs"}
+    pos = {e: 0 for e in "vapgs"}
+    for i, o in enumerate(ops):
+        if o["kind"] == "r":
+            know[i] = {token[i][0]: 1}
+    moved = True
+    while moved:
+        moved = False
+        for e in "vapgs":
+            while pos[e] < len(order[e]):
+                i = order[e][pos[e]]
+                deps = [d for d in ops[i]["deps"] | more[i] if not (e == "p" and eng[d] == "p")]
+                if any(d not in know for d in deps):
+                    break
+                w = []
+                for d in sorted(deps, key=lambda d: -fin[d]):
+                    s, v = token[d]
+                    if clock[e].get(s, 0) < abs(v):
+                        w.append((s, v))
+                        for s2, v2 in know[d].items():
+                            if clock[e].get(s2, 0) < v2:
+                                clock[e][s2] = v2
+                waits[i] = w
+                kn = dict(clock[e])
+                kn[token[i][0]] = max(kn.get(token[i][0], 0), abs(token[i][1]))
+                know[i] = kn
+                pos[e] += 1
+                moved = True
+    seen = {}
+    for e in "vapgs":
+        for s, v in clock[e].items():
+            seen[s] = max(seen.get(s, 0), v)
+    top = {}
+    for i in sorted(token, key=lambda i: fin[i]):
+        s, v = token[i]
+        if abs(v) >= abs(top.get(s, 0)):
+            top[s] = v
+    tail = [(s, v) for s, v in top.items() if seen.get(s, 0) < abs(v)]
+    return ops, order, waits, token, tail, total
+
+
+_PLAN = plan(CFG)
+SEMAPHORES = sorted({s for s, _v in _PLAN[3].values()})
+
+
+def rank_program(g, core, T, topo):
+    rank = T.rank_of(core)
+    if rank is None:
+        return
+    ops, order, waits, token, tail, _total = _PLAN
+    to, frm = {}, {}
+    for t in range(STEPS):
+        dst = T.cores[(rank - 1 - t % (N - 1)) % N]
+        src = T.cores[(rank + 1 + t % (N - 1)) % N]
+        rid, pid, _se = topo.addr(dst)
+        to[t] = (rid, pid, topo.mask(core, dst))
+        frm[t] = (len(topo.engines(core, dst)), len(topo.engines(src, core)))
+        if t == 0:
+            rid, pid, _se = topo.addr(src)
+            to["b"] = (rid, pid, topo.mask(core, src))
+            frm["b"] = (len(topo.engines(core, src)), len(topo.engines(dst, core)))
+    queues = {"v": g.vector, "a": g.scalar, "p": g.tensor, "g": g, "s": g.sync}
+
+    def count(s, v):
+        return v if v > 0 else frm[s[2] if s[2] == "b" else int(s[2])][0 if s[0] == "l" else 1]
+    for e in "sgvap":
+        q = queues[e]
+        for i in order[e]:
+            for s, v in waits[i]:
+                q.wait_ge(T.sem[s], count(s, v))
+            ins = ops[i]["alts"][e][1](g, T, {"to": to, "q": q})
+            if ops[i]["kind"] == "c":
+                ins.then_inc(T.sem[token[i][0]], 1)
+            elif ops[i]["kind"] == "d":
+                ins.then_inc(T.sem[token[i][0]], 16)
+    for s, v in tail:
+        g.sync.wait_ge(T.sem[s], count(s, v))

@@ -17,7 +17,7 @@ SCRATCH = {
     "qh": _sb(128, BF), "XY": _sb(4096, BF), "pm": _sb(2064, BF), "A1": _sb(2048, BF), "MX": _sb(2048, BF), "AY": _sb(2048, BF),
     "sc": _sb(256, F32), "ui": _sb(8, I32), "u": _sb(8, I32), "sq": _sb(8, I32), "sq5": _sb(8, I32), "lin": _sb(8, I32), "sm": _sb(8, I32),
     "nlh": _sb(16, I32), "n16": _sb(16, U16), "hm": _sb(128, BF), "cand": _sb(256, F32), "c16": _sb(16, U16), "PB": _sb(256, U16),
-    "Pf": _sb(128, F32), "tri": _sb(384, F32), "D0": _sb(384, BF), "Ec": _sb(128, F32),
+    "Pf": _sb(128, F32), "tri": _sb(384, F32), "trj": _sb(384, F32), "D0": _sb(384, BF), "Ec": _sb(128, F32),
     "ov": _sb(128, BF), "lt": _sb(128, BF), "s16": _sb(8, U16), "Mq": _sb(128, BF), "dh": _sb(128, BF), "dq": _sb(128, F32),
     "sd": _sb(256, BF), "sa": _sb(256, BF), "lost": _sb(128, BF), "o2": _sb(256, BF), "e16": _sb(8, U16), "qi": _sb(128, I32),
     "Ac": _sb(4, F32), "clx0": _sb(16, I32), "clx1": _sb(16, I32), "clx": _sb(16, U16), "clR": _sb(128, F32), "oldh": _sb(128, BF),
@@ -39,8 +39,25 @@ for _b in ("Y00", "Y01", "Y10", "Y11", "T0", "T1", "P0", "P1"):
 
 CFG = {"gch": 512, "nu": 1, "nm": 2, "sda": 1, "gsp": 2, "seed": 0, "wake": 70.0, "gat": 1.56, "sca": 3.8, "pe": 0.5,
        "look": 120.0, "noise": 0.0, "vpen": 300.0, "fix": 0.0, "bw": 80.0,
-       "bg": 0.0, "by": 0.0, "ba": 0.0, "bh": 0.0, "hmv": 0, "csp": 0, "slack": 0.0, "pcv": 0, "sgn": 0, "efi": 1, "bu": 0.0}
+       "bg": 0.0, "by": 0.0, "ba": 0.0, "bh": 0.0, "hmv": 0, "csp": 0, "slack": 0.0, "pcv": 0, "sgn": 0, "efi": 1, "bu": 0.0, "trv": 1}
 CFG.update({"nu":2,"sda":0,"gsp":1,"look":200,"vpen":100,"bh":1500,"csp":1,"slack":150,"pcv":1,"sgn":2,"bu":500,"B":{"y00.1":2500,"y01.1":1500,"A100.1":1500,"A101.1":1500,"P160.1":3000,"AY00.1":-600,"cB0.1":1500,"lin0.1":200,"T1.4":3000,"clx1.1":1500,"MX1":3000,"Y00.3":-600,"Y11.3":-3000,"Y00.4":3000,"bc.1":-600,"u1.1":-1500,"T1.9":-3000,"sc0.4":1500,"pm1.1":-200,"is161.1":-600,"iT0.17":-600,"Y10.3":-3000,"iBg1.1":3000,"x10.1":200,"imq1.1":-3000,"ilp1.1":1500,"T0.9":1500,"x1.1":-200,"cB1.1":1500,"lost0.1":1500,"T1.5":1500,"x11.1":-200,"T0.10":-3000,"T0.7":200,"iMX1":600,"iT1.12":600,"ib32.1":600,"T1.15":-3000,"sq51.1":3000,"T0.20":3000,"sm1.1":3000,"ieqs.1":-600,"T1.11":-3000,"s161.1":-3000,"xp0.1":3000,"Y11.4":1500,"dps0.1":-1500,"x01.1":600,"Y10.1":-3000,"sc1.1":-3000,"Y11.2":-600,"T1.8":-3000,"sa0.1":200,"iY11.4":-1500,"sc1.4":600,"iG1.2":-1500,"isa1.1":1500,"y10.1":-200,"iT1.3":3000},"E":{"ib32.1":"v","ip1.1":"v","clR0.1":"v","y00.1":"a","clR1.1":"a","iIdf.1":"v","Bg1.1":"a","inBI.1":"a","x10.1":"v","imp.1":"a","ilt1.1":"v","y11.1":"a","ix00.1":"a","iS2.1":"a","oldh0.1":"a","x00.1":"a","dq0.1":"v","hm1.1":"a","y01.1":"v","ix11.1":"v","inb2.1":"a","iclR1.1":"v","iBI.1":"a","it1s.1":"v","iD01.1":"v","iix.1":"v","Bg0.1":"v","inI.1":"a","iEc0.1":"v","ix01.1":"v","ib8.1":"a","Ec1.1":"a","ioldh1.1":"a","ihm1.1":"v","hm0.1":"a","iD00.2":"a","iy10.1":"a","ioldh0.1":"v","ib1.1":"a","Ec0.1":"a","iqh1.1":"v","idq1.1":"a"}})
+CFG.update({"nu":1,"sda":1,"wake":150.0,"fix":64.0,"pcv":3,"efi":0,"trv":0,"B":{"ix01.1":200,"ix10.1":200,"xi0.1":-3000,"iG0.2":-1500,"T1.5":1500,"A100.1":3000,"dps1.1":600,"itri0.1":3000,"qi1.1":1500,"MX1":-1500,"iT0.10":-1500,"ib4k.1":3000,"T0.14":-3000,"caB1.1":-3000,"iis15.1":-1500,"x00.1":3000,"dps0.1":3000,"sc1.5":-1500,"iast.1":3000,"icl0.1":-3000,"ith2.1":-600,"iPf1.1":-1500,"yq0.1":-3000,"iBo.1":-1500,"lp0.1":-1500,"e161.1":3000,"iIdf.1":1500,"iD01.1":1500,"ipm0.1":-600,"ieqs.1":-3000,"B161.1":3000,"AY10.1":-600,"iG1.2":-3000,"ix11.1":1500,"iBI.1":200,"MX0":-600,"ipoi.1":1500,"icx0.1":1500},"E":{"ib4k.1":"v","it1s.1":"v","idq1.1":"v","ib1.1":"a","inI.1":"a","ibc.1":"v","ip1.1":"a","iBI.1":"v","Bg1.1":"v","ioldh1.1":"a","iS2.1":"v","iIdf.1":"v","x00.1":"v","ix00.1":"a","iclR1.1":"a","inb.1":"a","dq1.1":"v","iclR0.1":"v","inb1.1":"a","ix11.1":"v","idq0.1":"v","inBo.1":"a","iBf.1":"v","iix.1":"v","iEc1.1":"a","clR1.1":"v","ioldh0.1":"v","iD00.2":"a","y00.1":"v","ihm1.1":"a","D00.1":"v","itop.1":"a","Pf1.1":"a","iy11.1":"v","iD00.1":"a","ib32.1":"a","ib8.1":"a","lt0.1":"v","iy10.1":"a","x10.1":"v","lt1.1":"a","Ec1.1":"a","Ec0.1":"a"}})
+CFG.update({"look":300,"bh":1500,"by":0,"gch":512,"nu":2,"sda":0,"wake":240.0,"gat":2.0,"vpen":600,"fix":10.0,"bg":1000,"ba":3000,"hmv":1,"csp":0,"pcv":2,"sgn":0,"bu":0,"B":{"o20.1":-600,"ix01.1":-3000,"dps0.1":1500,"T0.19":1500,"itmp.1":600,"T1.4":-1500,"lost0.1":600,"xi1.1":3000,"iy10.1":-3000,"icx0.1":3000,"iT0.15":-600,"iBo.1":-3000,"icolg.1":1500,"GRa.1":3000,"istw0.1":-3000,"iA110.1":600,"Dm":-3000,"lp1.1":1500,"MX0":-1500,"T1.8":-1500,"it2b.1":1500,"pm0.1":-1500,"n160.1":1500,"Bg1.1":3000,"lp0.1":600,"iS2.1":1500,"y10.1":600,"AY01.1":3000,"T1.13":-1500,"iY00.4":200,"ilost0.1":600,"AY00.1":3000,"xi0.1":200},"E":{"x01.1":"a","x02.1":"a","x03.1":"a","y02.1":"a","y03.1":"a","lt1.1":"v","ilt0.1":"v","ilt1.1":"v","ib32.1":"v","it1s.1":"v","clR1.1":"v","idq0.1":"a","iix.1":"v","iD01.2":"v","ix10.1":"v","iy00.1":"a","iS2.1":"v","ix01.1":"a","ib1.1":"a","lt0.1":"v","Bg0.1":"a","ib8.1":"a","ix00.1":"a","itop.1":"v","x10.1":"v","y10.1":"v","dq0.1":"a","y11.1":"a","inBI.1":"v","iqh1.1":"a","Bg1.1":"a","y00.1":"v","idq1.1":"v","Pf1.1":"a","ip1.1":"a","D00.2":"a","oldh1.1":"a","x00.1":"a","iy11.1":"a","inBo.1":"v","iIdf.1":"v","D00.1":"a","D01.2":"a","Ec1.1":"a","inIf.1":"v"}})
+CFG.update({"sda":1,"look":200,"sgn":1,"B":{"dps0.1":-3000,"iy10.1":-3000,"icx0.1":3000,"iT0.15":-1500,"Bg1.1":3000,"AY01.1":3000,"T1.7":-600,"T1.8":-3000,"y11.1":200,"icolg.1":1500,"lost0.1":3000,"T0.15":-3000,"pm1.1":-600,"x10.1":-3000,"iSh.1":-600,"itmp.1":-1500,"e161.1":3000,"icl0.1":-3000,"T0.11":-3000,"iG1.1":1500,"y01.1":1500,"qi0.1":-1500,"Y10.1":-1500,"iG0.2":200,"in32.1":-3000,"lp1.1":3000,"T0.19":1500,"istw1.1":600,"GRb.2":-1500,"sc0.2":-1500,"ith2.1":-200,"iis15.1":3000},"E":{"x01.1":"a","x02.1":"a","x03.1":"a","y02.1":"a","y03.1":"a","ilt1.1":"v","iix.1":"a","ix10.1":"a","ix01.1":"a","ib1.1":"a","itop.1":"a","idq1.1":"v","inBo.1":"v","iIdf.1":"a","iBf.1":"a","Pf0.1":"a","Bg1.1":"a","it1s.1":"a","it1b.1":"v","inI.1":"a","inb1.1":"a","inb.1":"a","ib8.1":"v","iD01.1":"a","ihq.1":"v","iD00.1":"a","bc.1":"a","ib4k.1":"a","dq1.1":"a","y00.1":"v","oldh1.1":"a","inBI.1":"v","ib32.1":"v","D00.2":"a","D01.1":"a","iy11.1":"a","clR0.1":"a","Ec0.1":"v","iSn.1":"a","x00.1":"a","inb2.1":"v","iclR0.1":"a","dq0.1":"v","oldh0.1":"a","lt0.1":"a","iy00.1":"a","ioldh0.1":"a","Pf1.1":"v","Ec1.1":"a","y10.1":"v","clR1.1":"a"}})
+CFG.update({"sca":5.0,"vpen":100,"hmv":0,"sgn":3,"B":{"icl0.1":-1500,"GRb.2":-1500,"G1.1":200,"ithi.1":600,"isp1.1":1500,"caP1.1":-1500,"Y10.2":1500,"T1.9":-3000,"P161.1":-600,"tri1.1":-1500,"ir2.1":-600,"AY10.1":-1500,"P160.1":3000,"iMX0":-1500,"ithf.1":-3000,"ib1.1":-3000,"T0.17":-3000,"A110.1":-200,"B161.1":600,"itmp.1":-600,"GRa.1":600,"e160.1":3000,"iD01.1":-1500,"sm1.1":-600,"iT0.12":3000,"sp1.1":200,"ib8.1":-600,"ov0.1":3000,"e161.1":-1500,"irp.1":3000,"iT1.6":3000},"E":{"x02.1":"a","x03.1":"a","y02.1":"a","y03.1":"a","iix.1":"a","ix10.1":"a","ix01.1":"a","inBo.1":"a","it1b.1":"a","ib8.1":"v","iD01.1":"v","ib4k.1":"a","iy11.1":"v","Ec0.1":"a","inb2.1":"v","y10.1":"v","x11.1":"a","iD01.2":"v","inIf.1":"v","imp.1":"a","iEc0.1":"v","iEc1.1":"v","iqh1.1":"a","D01.2":"a","inb1.1":"v","isdx0.1":"v","hm0.1":"v","sdx1.1":"a","iS2.1":"a","iD00.2":"a","ilt0.1":"a","iy00.1":"v","itop.1":"v","oldh1.1":"a","iIdf.1":"a","isdx1.1":"a","inI.1":"a","y11.1":"a","x10.1":"v","D00.1":"a","clR0.1":"a","bc.1":"a","ib1.1":"v","sdy1.1":"v","x00.1":"v","clR1.1":"a","ioldh0.1":"v","inBI.1":"v","inb.1":"v","sdy0.1":"a","ix11.1":"a","Ec1.1":"v","D00.2":"v","sdx0.1":"a","oldh0.1":"a","ioldh1.1":"v","lt0.1":"v"}})
+CFG["sgn"] = 1
+CFG["B"].update({"T1.9": -1500, "x11.1": 1500, "Y00.2": -3000, "Y10.4": -600, "T0.9": -600, "iT0.11": -1500, "T1.4": -600, "tri0.1": -1500, "x10.1": 3000, "T1.11": -600, "Y11.3": 3000, "cB0.1": 600, "istw1.1": 3000})
+CFG["E"].update({"iD01.1": "a", "inb2.1": "a", "iD01.2": "a", "iEc1.1": "a", "iqh1.1": "v", "clR0.1": "v", "clR1.1": "v", "iclR0.1": "v", "dq1.1": "a", "hm1.1": "a", "ihq.1": "v", "iBI.1": "a", "iy01.1": "a", "iS2.1": "v", "ilt1.1": "v", "ibc.1": "v", "it1s.1": "a", "iD00.1": "v", "idq1.1": "a", "D00.2": "a", "y00.1": "v", "Ec0.1": "v", "isdy1.1": "a", "dq0.1": "a", "ip1.1": "a", "ihm1.1": "a", "Bg0.1": "a", "Ec1.1": "a", "x10.1": "a"})
+for _k in ['icl0.1', 'GRb.2', 'G1.1', 'ithi.1', 'caP1.1', 'Y10.2', 'P161.1', 'tri1.1', 'ir2.1', 'AY10.1', 'ithf.1', 'ib1.1', 'A110.1', 'B161.1', 'itmp.1', 'GRa.1', 'e160.1', 'iD01.1', 'ov0.1', 'e161.1', 'irp.1']:
+    CFG["B"].pop(_k)
+for _k in ['it1b.1', 'ib4k.1', 'iy11.1', 'x11.1', 'imp.1', 'iEc0.1', 'D01.2', 'isdx0.1', 'itop.1', 'oldh1.1', 'iIdf.1', 'isdx1.1', 'inI.1', 'y11.1', 'bc.1', 'oldh0.1']:
+    CFG["E"].pop(_k)
+CFG["B"].update({"iMX0": -600, "sp1.1": 1500, "idps1.1": -200, "irp.2": -3000, "clR0.1": -1500, "sq1.1": -600, "T1.11": 3000, "T1.17": -1500, "P161.1": 3000, "mq0.1": -1500, "iSh.1": 200, "D00.1": 3000, "e160.1": 3000, "Dm": 1500, "inb1.1": -1500, "MX0": -3000, "T0.19": 600})
+CFG["E"].update({"iix.1": "v", "clR1.1": "a", "ilt1.1": "a", "it1s.1": "v", "ip1.1": "v", "isdy0.1": "v", "D01.1": "a", "dq1.1": "v", "y00.1": "a", "iy10.1": "a", "lt1.1": "v", "D01.2": "a", "iEc0.1": "v", "imp.1": "a", "inI.1": "v", "itop.1": "a", "oldh1.1": "v", "sdx0.1": "v", "Pf1.1": "v", "ilt0.1": "v", "iBf.1": "a", "Bg1.1": "a"})
+for _k in ['sm1.1', 'ib8.1', 'x11.1', 'Y00.2', 'T0.9', 'iT0.11', 'T1.4', 'tri0.1', 'x10.1', 'Y11.3']:
+    CFG["B"].pop(_k)
+for _k in ['iD01.1', 'iD01.2', 'iqh1.1', 'iD00.2', 'x10.1', 'D00.1', 'ioldh0.1', 'inBI.1', 'ioldh1.1', 'lt0.1', 'hm1.1', 'ibc.1', 'dq0.1', 'ihm1.1', 'Bg0.1']:
+    CFG["E"].pop(_k)
 ADD, SUB, MUL, MAX, MIN = AluOpType.add, AluOpType.subtract, AluOpType.mult, AluOpType.max, AluOpType.min
 AF = ActivationFunctionType
 
@@ -66,6 +83,7 @@ def build_ops(cfg):
             readers[w] = []
         deps.discard(i)
         key = (list(W) or [sem])[-1].split("_")[0]
+        key = key.replace("trj", "tri")
         if kind != "c" or key[:2] in ("GR",):
             key = key[:2] + key[3:]
         if key[:2] not in ("MX", "Dm"):
@@ -102,6 +120,13 @@ def build_ops(cfg):
         def run(g, T, x):
             rid, pid, mask = x["to"][t]
             return g.remote_dma(dst(T), src(T), T.sem["r" + name], T.sem["l" + name], pid, rid, mask)
+        def hand(g, T, x):
+            rid, pid, mask = x["helper"]
+            return g.remote_dma(dst(T), src(T), T.sem["h" + name], T.sem["l" + name], pid, rid, mask)
+        if name[0] == "g":
+            s = add({"g": (400.0, hand)}, R, [], kind="s", lat=1500.0 + nbytes / 150.0, sem="l" + name, extra=extra)
+            add({}, [], W, kind="r", lat=3000.0 + nbytes / cfg["bw"], sem="r" + name, extra=(s,))
+            return s
         s = add({"g": (400.0, run)}, R, [], kind="s", lat=1500.0 + nbytes / cfg["bw"], sem="l" + name, extra=extra)
         add({}, [], W, kind="r", lat=500.0, sem="r" + name, extra=(s,))
         return s
@@ -220,10 +245,12 @@ def build_ops(cfg):
     for t in range(STEPS):
         last = t == STEPS - 1
         step[0], step[1] = t, {}
+        cur, nxt = (("tri", "trj") if t % 2 == 0 else ("trj", "tri")) if cfg["trv"] else ("tri", "tri")
         GR, DR = "GR%d" % t, "DR%d" % t
         GO, gtag = ("G", ["G0", "G1"]) if t else ("Gi", gi)
         rtag = [GR + "a", GR + "b"]
-        bulk = lambda extra, t=t: SEND("g%d" % (t + 1), t + 1, S("G"), S("GR%d" % (t + 1)), 524288, ["G0", "G1"], ["GR%da" % (t + 1), "GR%db" % (t + 1)], extra)
+        bulk = lambda extra, t=t: (SEND("f%d" % (t + 1), t + 1, S("G", 0, 512), S("GR%d" % (t + 1), 0, 512), 262144, ["G0"], ["GR%da" % (t + 1)], extra),
+                                   SEND("g%d" % (t + 1), t + 1, S("G", 512, 1024), S("GR%d" % (t + 1), 512, 1024), 262144, ["G1"], ["GR%db" % (t + 1)], extra))
         if 1 <= t < STEPS - 1:
             bulk(())
         if t:
@@ -293,6 +320,10 @@ def build_ops(cfg):
         bias[0] = 0.0
         for h in range(2):
             TB, a0, a3 = "T%d" % h, 64 * h, 192 * h
+            if cfg["trv"]:
+                V(tt(S(cur, a3 + 1, a3 + 192, 3), S("Pf", a0, a0 + 64), S(cur, a3 + 2, a3 + 192, 3), SUB), 128, ["Pf%d" % h], [cur + str(h)])
+                V(tt(S(cur, a3, a3 + 192, 3), S("Bg", a0, a0 + 64), S("Pf", a0, a0 + 64), SUB), 128, ["Pf%d" % h, "Bg%d" % h], [cur + str(h)])
+                continue
             PE(lambda T, TB=TB, a0=a0, a3=a3: [(T[TB][:, 1:192:3], T.Idf[:], T.Pf[:, a0:a0 + 64], True, False), (T[TB][:, 1:192:3], T.nIf[:], T.tri[:, a3 + 2:a3 + 192:3], False, True),
                                              (T[TB][:, 2:192:3], T.Idf[:], T.tri[:, a3 + 2:a3 + 192:3], True, True)], 768, ["Idf", "nIf", "Pf%d" % h, "tri%d" % h], [TB], TB)
             PE(lambda T, TB=TB, a0=a0: [(T[TB][:, 0:192:3], T.Idf[:], T.Bg[:, a0:a0 + 64], True, False), (T[TB][:, 0:192:3], T.nIf[:], T.Pf[:, a0:a0 + 64], False, True)], 512,
@@ -442,14 +473,17 @@ def build_ops(cfg):
                 wrap_e()
             for h in hs:
                 H, a0, a3 = str(h), 64 * h, 192 * h
-                V(scan(S("tri", a3, a3 + 192), S("D0", a3, a3 + 192), S(TB, 0, 192), MUL, ADD), 192, ["D0" + H], [TB, "tri" + H], TB)
-                en = S("tri", a3 + 2, a3 + 192, 3)
+                if cfg["trv"]:
+                    V(scan(S(nxt, a3, a3 + 192), S("D0", a3, a3 + 192), S(cur, a3, a3 + 192), MUL, ADD), 192, ["D0" + H, cur + H], [nxt + H])
+                else:
+                    V(scan(S(nxt, a3, a3 + 192), S("D0", a3, a3 + 192), S(TB, 0, 192), MUL, ADD), 192, ["D0" + H], [TB, nxt + H], TB)
+                en = S(nxt, a3 + 2, a3 + 192, 3)
                 if not last:
                     ec = S("Ec", a0, a0 + 64)
-                    VA(cp(ec, en), 64, act(ec, en, AF.Copy), 64, ["tri" + H], ["Ec" + H])
+                    VA(cp(ec, en), 64, act(ec, en, AF.Copy), 64, [nxt + H], ["Ec" + H])
                     if not full:
                         SEND("e%d%d" % (t + 1, h), t + 1, ec, S("ER%d" % (t + 1), a0, a0 + 64), 32768, ["Ec" + H], ["ER%d%d" % (t + 1, h)])
-                V(cp(IND("G", 512 * h, 512 * h + 512, "clx", 4 * h, 4 * h + 4), en), gs(64), ["clx", "tri" + H], ["G" + H])
+                V(cp(IND("G", 512 * h, 512 * h + 512, "clx", 4 * h, 4 * h + 4), en), gs(64), ["clx", nxt + H], ["G" + H])
             if full and not last:
                 SEND("e%d" % (t + 1), t + 1, S("Ec"), S("ER%d" % (t + 1)), 65536, ["Ec0", "Ec1"], ["ER%d0" % (t + 1), "ER%d1" % (t + 1)])
             if cfg["efi"]:
@@ -615,13 +649,29 @@ def plan(cfg):
 
 
 _PLAN = plan(CFG)
-SEMAPHORES = sorted({s for s, _v in _PLAN[3].values()})
+SEMAPHORES = sorted({s for s, _v in _PLAN[3].values()}) + ["hg%d" % _t for _t in range(1, STEPS)] + ["kg%d" % _t for _t in range(1, STEPS)]
+
+
+def helper_of(c, T, topo):
+    return [k for k in topo.cores_of(c) if T.rank_of(k) is None and topo.die(k) != topo.die(c)
+            and all(topo.may_write(k, r) for r in T.cores)][0]
 
 
 def rank_program(g, core, T, topo):
     rank = T.rank_of(core)
     if rank is None:
+        for r, c in enumerate(T.cores):
+            if helper_of(c, T, topo) == core:
+                for t in range(1, STEPS):
+                    dst = T.cores[(r - 1 - t % (N - 1)) % N]
+                    rid, pid, _se = topo.addr(dst)
+                    g.wait_ge(T.sem["hg%d" % t], len(topo.engines(c, core)))
+                    g.remote_dma(T["GR%d" % t][:, 512:1024], T["GR%d" % t][:, 512:1024], T.sem["rg%d" % t], T.sem["kg%d" % t], pid, rid, topo.mask(core, dst))
+                for t in range(1, STEPS):
+                    g.wait_ge(T.sem["kg%d" % t], len(topo.engines(core, T.cores[(r - 1 - t % (N - 1)) % N])))
         return
+    hc = helper_of(core, T, topo)
+    helper = (topo.addr(hc)[0], topo.addr(hc)[1], topo.mask(core, hc))
     ops, order, waits, token, tail, _total = _PLAN
     to, frm = {}, {}
     for t in range(STEPS):
@@ -637,13 +687,17 @@ def rank_program(g, core, T, topo):
     queues = {"v": g.vector, "a": g.scalar, "p": g.tensor, "g": g, "s": g.sync}
 
     def count(s, v):
+        if v < 0 and s[1] == "g":
+            if s[0] == "l":
+                return len(topo.engines(core, hc))
+            return len(topo.engines(helper_of(T.cores[(rank + 1 + int(s[2]) % (N - 1)) % N], T, topo), core))
         return v if v > 0 else frm[s[2] if s[2] == "b" else int(s[2])][0 if s[0] == "l" else 1]
     for e in "sgvap":
         q = queues[e]
         for i in order[e]:
             for s, v in waits[i]:
                 q.wait_ge(T.sem[s], count(s, v))
-            ins = ops[i]["alts"][e][1](g, T, {"to": to, "q": q})
+            ins = ops[i]["alts"][e][1](g, T, {"to": to, "q": q, "helper": helper})
             if ops[i]["kind"] == "c":
                 ins.then_inc(T.sem[token[i][0]], 1)
             elif ops[i]["kind"] == "d":

@@ -1,519 +1,527 @@
-from concourse.bass import DstId, RemoteDMATransfer
 from concourse.mybir import dt, AluOpType, AxisListType, ActivationFunctionType
 
 N, STEPS = 8, 5
-F32, BF, I32, U16 = "float32", "bfloat16", "int32", "uint16"
+F32, BF, H16, I32, U16 = "float32", "bfloat16", "float16", "int32", "uint16"
+ADD, SUB, MUL, MAX, MIN = AluOpType.add, AluOpType.subtract, AluOpType.mult, AluOpType.max, AluOpType.min
+AND, SHR = AluOpType.bitwise_and, AluOpType.arith_shift_right
+EQ, NE, GT, GE = AluOpType.is_equal, AluOpType.not_equal, AluOpType.is_gt, AluOpType.is_ge
+AF = ActivationFunctionType
+BIG = 4096.0
 
-
-def _sb(cols, d):
-    return ("sbuf", [128, cols], d)
-
-
-SCRATCH = {
-    "X": _sb(4096, BF), "Gi": _sb(1024, I32), "G": _sb(1024, F32), "Dm": _sb(4112, I32), "Dd": _sb(256, I32),
-    "GR1": _sb(1024, F32), "nq": _sb(16, U16), "hq": _sb(128, BF), "Bq": _sb(128, U16), "Bg": _sb(128, F32), "Idf": _sb(128, F32), "nIf": _sb(128, F32),
-    "GR2": _sb(1024, F32), "GR3": _sb(1024, F32), "GR4": _sb(1024, F32),
-    "q0": _sb(128, BF), "w0": _sb(8, BF), "e0i": _sb(128, I32), "thi": _sb(4, I32), "thf": _sb(4, F32), "thc": _sb(8, F32),
-    "qh": _sb(128, BF), "XY": _sb(4096, BF), "pm": _sb(2064, BF), "A1": _sb(2048, BF), "MX": _sb(2048, BF), "AY": _sb(2048, BF),
-    "sc": _sb(256, F32), "ui": _sb(8, I32), "u": _sb(8, I32), "sq": _sb(8, I32), "sq5": _sb(8, I32), "lin": _sb(8, I32), "sm": _sb(8, I32),
-    "nlh": _sb(16, I32), "n16": _sb(16, U16), "hm": _sb(128, BF), "cand": _sb(256, F32), "c16": _sb(16, U16), "PB": _sb(256, U16),
-    "Pf": _sb(128, F32), "tri": _sb(384, F32), "trj": _sb(384, F32), "D0": _sb(384, BF), "Ec": _sb(128, F32),
-    "ov": _sb(128, BF), "lt": _sb(128, BF), "s16": _sb(8, U16), "Mq": _sb(128, BF), "dh": _sb(128, BF), "dq": _sb(128, F32),
-    "sd": _sb(256, BF), "sa": _sb(256, BF), "lost": _sb(128, BF), "o2": _sb(256, BF), "e16": _sb(8, U16), "qi": _sb(128, I32),
-    "Ac": _sb(4, F32), "clx0": _sb(16, I32), "clx1": _sb(16, I32), "clx": _sb(16, U16), "clR": _sb(128, F32), "oldh": _sb(128, BF),
-    "xi": _sb(128, I32), "n32": _sb(8, I32), "nf": _sb(8, F32), "bc": _sb(128, F32), "x1": _sb(128, F32), "eq": _sb(128, BF),
-    "eqs": _sb(128, BF), "tt": _sb(8, F32), "o16": _sb(16, U16), "yqb": _sb(128, BF),
-    "colg": _sb(128, BF), "colb": _sb(256, BF), "col": _sb(144, BF), "pI": _sb(4, I32), "pb": _sb(4, I32), "pc": _sb(20, F32),
-    "aq": _sb(16, F32), "Bo": _sb(128, BF), "nBo": _sb(128, BF), "Bf": _sb(128, F32), "W2": _sb(128, BF), "Id": _sb(128, BF), "nI": _sb(128, BF),
-    "BI": _sb(128, BF), "nBI": _sb(128, BF), "Sh": _sb(128, BF), "Tri": _sb(128, BF), "tmp": _sb(128, BF), "tmp2": _sb(256, BF),
-    "ms": _sb(256, BF), "poi": _sb(128, BF), "dl": _sb(128, BF), "rp": _sb(1024, BF), "r2": _sb(128, BF), "S1": _sb(144, BF),
-    "S2": _sb(144, BF), "Sn": _sb(144, BF), "ix": _sb(128, BF), "opn": _sb(256, BF), "c256": _sb(256, BF), "o16th": _sb(128, BF),
-    "ast": _sb(8, U16), "stw": _sb(16, I32), "iot": _sb(512, F32),
+COLUMNS = {
+    BF: {"X": 4096, "qb": 128, "w0": 8, "XY": 4096, "pm": 2080, "MX": 2048, "AY": 2048, "hm": 128, "hq": 128, "lor": 128, "lt": 128,
+         "Mq": 128, "d": 128, "sd": 256, "sa": 256, "nl": 128, "o2": 256, "l2": 128, "xn": 128, "ab": 512, "mn": 512, "junk": 64,
+         "colg": 128, "colb": 1024, "col": 144, "pos": 256, "poi": 256, "Bo": 128, "nBo": 128, "Bhi": 128, "Id": 128, "nI": 128, "I8k": 128,
+         "BI": 128, "nBI": 128, "Sh": 128, "tmp": 128, "Tri": 128, "TB": 128, "nTB": 128, "R0": 128, "S1": 144, "S2": 144, "Sn": 144,
+         "S4": 144, "Sw": 144, "dl": 16, "LT": 1024, "rp": 1024, "frc": 64, "eb": 8, "n16th": 128, "c2k": 128, "opn": 128, "cu": 16, "xo": 128, "colm": 128, "nB0": 128, "nB1": 128},
+    H16: {"qp": 128, "cand": 256, "PBh": 256, "Za": 128, "Z": 128, "xt": 128, "W1": 144, "W2": 128, "th16": 8},
+    F32: {"G": 1024, "v": 8, "sq": 8, "Ac": 4, "sc": 128, "d2": 128, "Ea": 128, "En": 128, "clR": 128, "nn": 8, "ow": 8, "oo": 8,
+          "pc": 20, "thc": 8, "idx": 64, "idc": 64, "aq": 8, "spare": 8, "iot": 512},
+    I32: {"Gi": 1024, "Dm": 4160, "Dd": 256, "e0i": 128, "thi": 4, "hh": 8, "nf": 8, "nlh": 16, "ui": 8, "cx0": 16, "cx1": 16,
+          "n32": 8, "pI": 4, "pb": 4, "stw": 16},
+    U16: {"n16": 16, "nq": 16, "c16": 16, "PB": 256, "Bq": 128, "s16": 8, "e16": 8, "clx": 16, "o16": 8},
 }
 for _t in range(1, STEPS):
-    SCRATCH["DR%d" % _t] = _sb(256, I32)
-    SCRATCH["CR%d" % _t] = _sb(8, U16)
-    SCRATCH["ER%d" % _t] = _sb(128, F32)
+    COLUMNS[F32].update({"GR%d" % _t: 1024, "ER%d" % _t: 128})
+    COLUMNS[I32]["DR%d" % _t] = 256
+    COLUMNS[U16]["CR%d" % _t] = 8
+SCRATCH = {_n: ("sbuf", [128, _c], _d) for _d in COLUMNS for _n, _c in COLUMNS[_d].items()}
+SCRATCH["A1"] = ("sbuf", [128, 8, 256], BF)
 for _b in ("Y00", "Y01", "Y10", "Y11", "T0", "T1", "P0", "P1"):
     SCRATCH[_b] = ("psum", [128, 512], F32)
 
-CFG = {"gch": 512, "nu": 1, "nm": 2, "sda": 1, "gsp": 2, "seed": 0, "wake": 70.0, "gat": 1.56, "sca": 3.8, "pe": 0.5,
-       "look": 120.0, "noise": 0.0, "vpen": 300.0, "fix": 0.0, "bw": 80.0,
-       "bg": 0.0, "by": 0.0, "ba": 0.0, "bh": 0.0, "hmv": 0, "csp": 0, "slack": 0.0, "pcv": 0, "sgn": 0, "efi": 1, "bu": 0.0, "trv": 1}
-CFG.update({"nu":2,"sda":0,"gsp":1,"look":200,"vpen":100,"bh":1500,"csp":1,"slack":150,"pcv":1,"sgn":2,"bu":500,"B":{"y00.1":2500,"y01.1":1500,"A100.1":1500,"A101.1":1500,"P160.1":3000,"AY00.1":-600,"cB0.1":1500,"lin0.1":200,"T1.4":3000,"clx1.1":1500,"MX1":3000,"Y00.3":-600,"Y11.3":-3000,"Y00.4":3000,"bc.1":-600,"u1.1":-1500,"T1.9":-3000,"sc0.4":1500,"pm1.1":-200,"is161.1":-600,"iT0.17":-600,"Y10.3":-3000,"iBg1.1":3000,"x10.1":200,"imq1.1":-3000,"ilp1.1":1500,"T0.9":1500,"x1.1":-200,"cB1.1":1500,"lost0.1":1500,"T1.5":1500,"x11.1":-200,"T0.10":-3000,"T0.7":200,"iMX1":600,"iT1.12":600,"ib32.1":600,"T1.15":-3000,"sq51.1":3000,"T0.20":3000,"sm1.1":3000,"ieqs.1":-600,"T1.11":-3000,"s161.1":-3000,"xp0.1":3000,"Y11.4":1500,"dps0.1":-1500,"x01.1":600,"Y10.1":-3000,"sc1.1":-3000,"Y11.2":-600,"T1.8":-3000,"sa0.1":200,"iY11.4":-1500,"sc1.4":600,"iG1.2":-1500,"isa1.1":1500,"y10.1":-200,"iT1.3":3000},"E":{"ib32.1":"v","ip1.1":"v","clR0.1":"v","y00.1":"a","clR1.1":"a","iIdf.1":"v","Bg1.1":"a","inBI.1":"a","x10.1":"v","imp.1":"a","ilt1.1":"v","y11.1":"a","ix00.1":"a","iS2.1":"a","oldh0.1":"a","x00.1":"a","dq0.1":"v","hm1.1":"a","y01.1":"v","ix11.1":"v","inb2.1":"a","iclR1.1":"v","iBI.1":"a","it1s.1":"v","iD01.1":"v","iix.1":"v","Bg0.1":"v","inI.1":"a","iEc0.1":"v","ix01.1":"v","ib8.1":"a","Ec1.1":"a","ioldh1.1":"a","ihm1.1":"v","hm0.1":"a","iD00.2":"a","iy10.1":"a","ioldh0.1":"v","ib1.1":"a","Ec0.1":"a","iqh1.1":"v","idq1.1":"a"}})
-CFG.update({"nu":1,"sda":1,"wake":150.0,"fix":64.0,"pcv":3,"efi":0,"trv":0,"B":{"ix01.1":200,"ix10.1":200,"xi0.1":-3000,"iG0.2":-1500,"T1.5":1500,"A100.1":3000,"dps1.1":600,"itri0.1":3000,"qi1.1":1500,"MX1":-1500,"iT0.10":-1500,"ib4k.1":3000,"T0.14":-3000,"caB1.1":-3000,"iis15.1":-1500,"x00.1":3000,"dps0.1":3000,"sc1.5":-1500,"iast.1":3000,"icl0.1":-3000,"ith2.1":-600,"iPf1.1":-1500,"yq0.1":-3000,"iBo.1":-1500,"lp0.1":-1500,"e161.1":3000,"iIdf.1":1500,"iD01.1":1500,"ipm0.1":-600,"ieqs.1":-3000,"B161.1":3000,"AY10.1":-600,"iG1.2":-3000,"ix11.1":1500,"iBI.1":200,"MX0":-600,"ipoi.1":1500,"icx0.1":1500},"E":{"ib4k.1":"v","it1s.1":"v","idq1.1":"v","ib1.1":"a","inI.1":"a","ibc.1":"v","ip1.1":"a","iBI.1":"v","Bg1.1":"v","ioldh1.1":"a","iS2.1":"v","iIdf.1":"v","x00.1":"v","ix00.1":"a","iclR1.1":"a","inb.1":"a","dq1.1":"v","iclR0.1":"v","inb1.1":"a","ix11.1":"v","idq0.1":"v","inBo.1":"a","iBf.1":"v","iix.1":"v","iEc1.1":"a","clR1.1":"v","ioldh0.1":"v","iD00.2":"a","y00.1":"v","ihm1.1":"a","D00.1":"v","itop.1":"a","Pf1.1":"a","iy11.1":"v","iD00.1":"a","ib32.1":"a","ib8.1":"a","lt0.1":"v","iy10.1":"a","x10.1":"v","lt1.1":"a","Ec1.1":"a","Ec0.1":"a"}})
-CFG.update({"look":300,"bh":1500,"by":0,"gch":512,"nu":2,"sda":0,"wake":240.0,"gat":2.0,"vpen":600,"fix":10.0,"bg":1000,"ba":3000,"hmv":1,"csp":0,"pcv":2,"sgn":0,"bu":0,"B":{"o20.1":-600,"ix01.1":-3000,"dps0.1":1500,"T0.19":1500,"itmp.1":600,"T1.4":-1500,"lost0.1":600,"xi1.1":3000,"iy10.1":-3000,"icx0.1":3000,"iT0.15":-600,"iBo.1":-3000,"icolg.1":1500,"GRa.1":3000,"istw0.1":-3000,"iA110.1":600,"Dm":-3000,"lp1.1":1500,"MX0":-1500,"T1.8":-1500,"it2b.1":1500,"pm0.1":-1500,"n160.1":1500,"Bg1.1":3000,"lp0.1":600,"iS2.1":1500,"y10.1":600,"AY01.1":3000,"T1.13":-1500,"iY00.4":200,"ilost0.1":600,"AY00.1":3000,"xi0.1":200},"E":{"x01.1":"a","x02.1":"a","x03.1":"a","y02.1":"a","y03.1":"a","lt1.1":"v","ilt0.1":"v","ilt1.1":"v","ib32.1":"v","it1s.1":"v","clR1.1":"v","idq0.1":"a","iix.1":"v","iD01.2":"v","ix10.1":"v","iy00.1":"a","iS2.1":"v","ix01.1":"a","ib1.1":"a","lt0.1":"v","Bg0.1":"a","ib8.1":"a","ix00.1":"a","itop.1":"v","x10.1":"v","y10.1":"v","dq0.1":"a","y11.1":"a","inBI.1":"v","iqh1.1":"a","Bg1.1":"a","y00.1":"v","idq1.1":"v","Pf1.1":"a","ip1.1":"a","D00.2":"a","oldh1.1":"a","x00.1":"a","iy11.1":"a","inBo.1":"v","iIdf.1":"v","D00.1":"a","D01.2":"a","Ec1.1":"a","inIf.1":"v"}})
-CFG.update({"sda":1,"look":200,"sgn":1,"B":{"dps0.1":-3000,"iy10.1":-3000,"icx0.1":3000,"iT0.15":-1500,"Bg1.1":3000,"AY01.1":3000,"T1.7":-600,"T1.8":-3000,"y11.1":200,"icolg.1":1500,"lost0.1":3000,"T0.15":-3000,"pm1.1":-600,"x10.1":-3000,"iSh.1":-600,"itmp.1":-1500,"e161.1":3000,"icl0.1":-3000,"T0.11":-3000,"iG1.1":1500,"y01.1":1500,"qi0.1":-1500,"Y10.1":-1500,"iG0.2":200,"in32.1":-3000,"lp1.1":3000,"T0.19":1500,"istw1.1":600,"GRb.2":-1500,"sc0.2":-1500,"ith2.1":-200,"iis15.1":3000},"E":{"x01.1":"a","x02.1":"a","x03.1":"a","y02.1":"a","y03.1":"a","ilt1.1":"v","iix.1":"a","ix10.1":"a","ix01.1":"a","ib1.1":"a","itop.1":"a","idq1.1":"v","inBo.1":"v","iIdf.1":"a","iBf.1":"a","Pf0.1":"a","Bg1.1":"a","it1s.1":"a","it1b.1":"v","inI.1":"a","inb1.1":"a","inb.1":"a","ib8.1":"v","iD01.1":"a","ihq.1":"v","iD00.1":"a","bc.1":"a","ib4k.1":"a","dq1.1":"a","y00.1":"v","oldh1.1":"a","inBI.1":"v","ib32.1":"v","D00.2":"a","D01.1":"a","iy11.1":"a","clR0.1":"a","Ec0.1":"v","iSn.1":"a","x00.1":"a","inb2.1":"v","iclR0.1":"a","dq0.1":"v","oldh0.1":"a","lt0.1":"a","iy00.1":"a","ioldh0.1":"a","Pf1.1":"v","Ec1.1":"a","y10.1":"v","clR1.1":"a"}})
-CFG.update({"sca":5.0,"vpen":100,"hmv":0,"sgn":3,"B":{"icl0.1":-1500,"GRb.2":-1500,"G1.1":200,"ithi.1":600,"isp1.1":1500,"caP1.1":-1500,"Y10.2":1500,"T1.9":-3000,"P161.1":-600,"tri1.1":-1500,"ir2.1":-600,"AY10.1":-1500,"P160.1":3000,"iMX0":-1500,"ithf.1":-3000,"ib1.1":-3000,"T0.17":-3000,"A110.1":-200,"B161.1":600,"itmp.1":-600,"GRa.1":600,"e160.1":3000,"iD01.1":-1500,"sm1.1":-600,"iT0.12":3000,"sp1.1":200,"ib8.1":-600,"ov0.1":3000,"e161.1":-1500,"irp.1":3000,"iT1.6":3000},"E":{"x02.1":"a","x03.1":"a","y02.1":"a","y03.1":"a","iix.1":"a","ix10.1":"a","ix01.1":"a","inBo.1":"a","it1b.1":"a","ib8.1":"v","iD01.1":"v","ib4k.1":"a","iy11.1":"v","Ec0.1":"a","inb2.1":"v","y10.1":"v","x11.1":"a","iD01.2":"v","inIf.1":"v","imp.1":"a","iEc0.1":"v","iEc1.1":"v","iqh1.1":"a","D01.2":"a","inb1.1":"v","isdx0.1":"v","hm0.1":"v","sdx1.1":"a","iS2.1":"a","iD00.2":"a","ilt0.1":"a","iy00.1":"v","itop.1":"v","oldh1.1":"a","iIdf.1":"a","isdx1.1":"a","inI.1":"a","y11.1":"a","x10.1":"v","D00.1":"a","clR0.1":"a","bc.1":"a","ib1.1":"v","sdy1.1":"v","x00.1":"v","clR1.1":"a","ioldh0.1":"v","inBI.1":"v","inb.1":"v","sdy0.1":"a","ix11.1":"a","Ec1.1":"v","D00.2":"v","sdx0.1":"a","oldh0.1":"a","ioldh1.1":"v","lt0.1":"v"}})
-CFG["sgn"] = 1
-CFG["B"].update({"T1.9": -1500, "x11.1": 1500, "Y00.2": -3000, "Y10.4": -600, "T0.9": -600, "iT0.11": -1500, "T1.4": -600, "tri0.1": -1500, "x10.1": 3000, "T1.11": -600, "Y11.3": 3000, "cB0.1": 600, "istw1.1": 3000})
-CFG["E"].update({"iD01.1": "a", "inb2.1": "a", "iD01.2": "a", "iEc1.1": "a", "iqh1.1": "v", "clR0.1": "v", "clR1.1": "v", "iclR0.1": "v", "dq1.1": "a", "hm1.1": "a", "ihq.1": "v", "iBI.1": "a", "iy01.1": "a", "iS2.1": "v", "ilt1.1": "v", "ibc.1": "v", "it1s.1": "a", "iD00.1": "v", "idq1.1": "a", "D00.2": "a", "y00.1": "v", "Ec0.1": "v", "isdy1.1": "a", "dq0.1": "a", "ip1.1": "a", "ihm1.1": "a", "Bg0.1": "a", "Ec1.1": "a", "x10.1": "a"})
-for _k in ['icl0.1', 'GRb.2', 'G1.1', 'ithi.1', 'caP1.1', 'Y10.2', 'P161.1', 'tri1.1', 'ir2.1', 'AY10.1', 'ithf.1', 'ib1.1', 'A110.1', 'B161.1', 'itmp.1', 'GRa.1', 'e160.1', 'iD01.1', 'ov0.1', 'e161.1', 'irp.1']:
-    CFG["B"].pop(_k)
-for _k in ['it1b.1', 'ib4k.1', 'iy11.1', 'x11.1', 'imp.1', 'iEc0.1', 'D01.2', 'isdx0.1', 'itop.1', 'oldh1.1', 'iIdf.1', 'isdx1.1', 'inI.1', 'y11.1', 'bc.1', 'oldh0.1']:
-    CFG["E"].pop(_k)
-CFG["B"].update({"iMX0": -600, "sp1.1": 1500, "idps1.1": -200, "irp.2": -3000, "clR0.1": -1500, "sq1.1": -600, "T1.11": 3000, "T1.17": -1500, "P161.1": 3000, "mq0.1": -1500, "iSh.1": 200, "D00.1": 3000, "e160.1": 3000, "Dm": 1500, "inb1.1": -1500, "MX0": -3000, "T0.19": 600})
-CFG["E"].update({"iix.1": "v", "clR1.1": "a", "ilt1.1": "a", "it1s.1": "v", "ip1.1": "v", "isdy0.1": "v", "D01.1": "a", "dq1.1": "v", "y00.1": "a", "iy10.1": "a", "lt1.1": "v", "D01.2": "a", "iEc0.1": "v", "imp.1": "a", "inI.1": "v", "itop.1": "a", "oldh1.1": "v", "sdx0.1": "v", "Pf1.1": "v", "ilt0.1": "v", "iBf.1": "a", "Bg1.1": "a"})
-for _k in ['sm1.1', 'ib8.1', 'x11.1', 'Y00.2', 'T0.9', 'iT0.11', 'T1.4', 'tri0.1', 'x10.1', 'Y11.3']:
-    CFG["B"].pop(_k)
-for _k in ['iD01.1', 'iD01.2', 'iqh1.1', 'iD00.2', 'x10.1', 'D00.1', 'ioldh0.1', 'inBI.1', 'ioldh1.1', 'lt0.1', 'hm1.1', 'ibc.1', 'dq0.1', 'ihm1.1', 'Bg0.1']:
-    CFG["E"].pop(_k)
-ADD, SUB, MUL, MAX, MIN = AluOpType.add, AluOpType.subtract, AluOpType.mult, AluOpType.max, AluOpType.min
-AF = ActivationFunctionType
+CFG = {"nu": 2, "gch": 512, "sda": 0, "wake": 240.0, "fix": 10.0, "gat": 1.56, "sca": 3.8, "pe": 0.5, "bw": 80.0, "rlat": 2000.0,
+       "look": 200.0, "vpen": 300.0, "slack": 150.0, "noise": 0.0, "seed": 0, "pin": {}, "ax": (0, 0), "xta": 0, "passes": 8, "stag": 2000.0}
+
+
+def S(name, a=None, b=None, c=None):
+    r = range(SCRATCH[name][1][1])[a:b:c]
+    return ("s", name, min(r[0], r[-1]), max(r[0], r[-1]) + 1, len(r), slice(a, b, c))
+
+
+def S3(name, j0, j1, a, b):
+    w = SCRATCH[name][1][2]
+    return ("3", name, j0 * w + a, (j1 - 1) * w + b, (j1 - j0) * (b - a), (slice(j0, j1), slice(a, b)))
+
+
+def LEAD(name, a, b):
+    return ("l", name, a, b, b - a, slice(a, b))
+
+
+def HBM(name, a=None, b=None):
+    return ("h", name, 0, 0, 0, slice(a, b))
+
+
+def IND(win, off):
+    return ("i", win, off)
+
+
+def ap(T, a):
+    if not isinstance(a, tuple):
+        return a
+    if a[0] == "i":
+        return ap(T, a[1]).indirect(ap(T, a[2]))
+    if a[0] == "3":
+        return T[a[1]][:, a[5][0], a[5][1]]
+    if a[0] == "l":
+        return T[a[1]][0:128:16, a[5]]
+    return T[a[1]][:, a[5]]
 
 
 def build_ops(cfg):
-    ops, lastw, readers, bias, step = [], {}, {}, [0.0], [-1, {}]
-    ga, sca, pe, fix = cfg["gat"], cfg["sca"], cfg["pe"], cfg["fix"]
+    ops, writes, reads, step = [], {}, {}, [-1, 0]
+    fix, pe = cfg["fix"], cfg["pe"]
+    psum = lambda a: SCRATCH[a[1]][0] == "psum"
+    narrow = lambda a: SCRATCH[a[1]][2] in (BF, H16, U16)
 
-    def add(alts, R, W, bank=None, kind="c", lat=0.0, sem=None, extra=()):
-        i = len(ops)
-        deps = set(extra)
-        for r in R:
-            if r in lastw:
-                deps.add(lastw[r])
-        for w in W:
-            if w in lastw:
-                deps.add(lastw[w])
-            deps.update(readers.get(w, ()))
-        for r in R:
-            readers.setdefault(r, []).append(i)
-        for w in W:
-            lastw[w] = i
-            readers[w] = []
-        deps.discard(i)
-        key = (list(W) or [sem])[-1].split("_")[0]
-        key = key.replace("trj", "tri")
-        if kind != "c" or key[:2] in ("GR",):
-            key = key[:2] + key[3:]
-        if key[:2] not in ("MX", "Dm"):
-            step[1][key] = step[1].get(key, 0) + 1
-            key += ".%d" % step[1][key]
-        key = ("i" if step[0] < 1 else "") + key
-        ops.append({"alts": alts, "deps": deps, "bank": bank, "kind": kind, "lat": lat, "sem": sem, "W": list(W) or [sem], "key": key, "bias": bias[0]})
+    def add(alts, R, W, kind="c", lat=0.0, sem=None, extra=()):
+        i, deps = len(ops), set(extra)
+        for a in R + W:
+            deps.update(j for lo, hi, j in writes.get(a[1], ()) if lo < a[3] and a[2] < hi)
+        for a in W:
+            deps.update(j for lo, hi, j in reads.get(a[1], ()) if lo < a[3] and a[2] < hi)
+        for a in W:
+            for book in (writes, reads):
+                book[a[1]] = [e for e in book.get(a[1], ()) if not (a[2] <= e[0] and e[1] <= a[3])]
+            writes[a[1]].append((a[2], a[3], i))
+        for a in R:
+            reads.setdefault(a[1], []).append((a[2], a[3], i))
+        banks = sorted({a[1] for a in R + W if a[1] in SCRATCH and psum(a)})
+        name = (W[0][1] if W else sem) or "-"
+        if name in cfg["pin"] and cfg["pin"][name] in alts:
+            alts = {cfg["pin"][name]: alts[cfg["pin"][name]]}
+        ops.append({"alts": alts, "deps": deps, "banks": banks, "kind": kind, "lat": lat, "sem": sem, "name": name, "step": step[0],
+                    "half": step[1]})
         return i
 
-    def V(fn, n, R, W, bank=None):
-        return add({"v": (fix + max(64.0, n), fn)}, R, W, bank)
+    def sides(out, ins):
+        R, W = [], [out[1] if out[0] == "i" else out]
+        for a in ins:
+            if isinstance(a, tuple):
+                R += [a[1], a[2]] if a[0] == "i" else [a]
+        return R + ([out[2]] if out[0] == "i" else []), W
 
-    def A(fn, n, R, W, bank=None):
-        return add({"a": (fix + max(64.0, n), fn)}, R, W, bank)
+    def cost(out, first, rate):
+        if out[0] == "i":
+            return 60.0 + cfg["sca"] * first[4]
+        if first[0] == "i":
+            return 60.0 + cfg["gat"] * out[4]
+        return fix + max(64.0, rate * first[4])
+    half = lambda *a: 0.5 if all(narrow(x) for x in a if x[0] != "i") else 1.0
+    ts = lambda o, i, a, b, p, q=None: ("v", cost(o, i, half(o, i)), o, [i, a, b],
+                                        lambda g, T, x: g.vector.tensor_scalar(ap(T, o), ap(T, i), ap(T, a), ap(T, b), *([p] if q is None else [p, q])))
+    cp = lambda o, i: ("v", cost(o, i, half(o, i)), o, [i], lambda g, T, x: g.vector.tensor_copy(ap(T, o), ap(T, i)))
+    tt = lambda o, i, j, p: ("v", cost(o, i, 1.0 if i[0] == "i" or psum(i) or psum(j) else 2.0), o, [i, j],
+                             lambda g, T, x: g.vector.tensor_tensor(ap(T, o), ap(T, i), ap(T, j), p))
+    scan = lambda o, i, j, p, q: ("v", cost(o, i, half(o, i, j)), o, [i, j],
+                                  lambda g, T, x: g.vector.tensor_tensor_scan(ap(T, o), ap(T, i), ap(T, j), 0.0, p, q))
+    mset = lambda o, c: ("v", cost(o, o, half(o)), o, [], lambda g, T, x: g.vector.memset(ap(T, o), c))
 
-    def VA(fv, nv, fa, na, R, W, bank=None):
-        return add({"v": (fix + max(64.0, nv), fv), "a": (fix + max(64.0, na), fa)}, R, W, bank)
-
-    def PE(fn, cyc, R, W, bank):
+    def act(o, i, f, b=0.0, s=1.0, acc=None):
         def run(g, T, x):
-            last = None
-            for (o, l, r, s0, s1) in fn(T):
-                last = g.tensor.matmul(o, l, r, s0, s1)
-            return last
-        return add({"p": (cyc * pe, run)}, R, W, bank)
+            more = {} if b == 0.0 else {"bias": ap(T, b)}
+            if acc:
+                more["accum_out"] = ap(T, acc)
+            return g.scalar.activation(ap(T, o), ap(T, i), f, scale=ap(T, s), **more)
+        return ("a", cost(o, i, 1.0) + (15.0 if i[0] == "i" else 0.0), o, [i, b, s], run)
 
-    def GP(fn, n, R, W):
-        return add({"g": (150.0 + 2.0 * n, fn)}, R, W)
+    def do(*forms, also=()):
+        R, W = [], []
+        for f in forms:
+            r, W = sides(f[2], f[3])
+            R += r
+        return add({f[0]: (f[1], f[4]) for f in forms}, R, W + list(also))
 
-    def DMA(q, name, fn, nbytes, R, W):
-        return add({q: (60.0, fn)}, R, W, kind="d", lat=2000.0 + nbytes / 200.0, sem=name)
+    def lin(o, i, s=1.0, b=0.0):
+        fv = cp(o, i) if s == 1.0 and b == 0.0 else (ts(o, i, s, None, MUL) if b == 0.0 else ts(o, i, s, b, MUL, ADD))
+        return do(fv, act(o, i, AF.Copy if b == 0.0 and not isinstance(s, tuple) else AF.Identity, b, s))
 
-    def SEND(name, t, src, dst, nbytes, R, W, extra=()):
+    def mm(calls, first=True, last=True):
         def run(g, T, x):
-            rid, pid, mask = x["to"][t]
-            return g.remote_dma(dst(T), src(T), T.sem["r" + name], T.sem["l" + name], pid, rid, mask)
-        def hand(g, T, x):
-            rid, pid, mask = x["helper"]
-            return g.remote_dma(dst(T), src(T), T.sem["h" + name], T.sem["l" + name], pid, rid, mask)
-        if name[0] == "g":
-            s = add({"g": (400.0, hand)}, R, [], kind="s", lat=1500.0 + nbytes / 150.0, sem="l" + name, extra=extra)
-            add({}, [], W, kind="r", lat=3000.0 + nbytes / cfg["bw"], sem="r" + name, extra=(s,))
-            return s
-        s = add({"g": (400.0, run)}, R, [], kind="s", lat=1500.0 + nbytes / cfg["bw"], sem="l" + name, extra=extra)
-        add({}, [], W, kind="r", lat=500.0, sem="r" + name, extra=(s,))
+            for k, c in enumerate(calls):
+                ins = g.tensor.matmul(ap(T, c[0]), ap(T, c[1]), ap(T, c[2]), c[3] == 1 if c[3:] else first and k == 0, c[3] == 2 if c[3:] else last and k == len(calls) - 1)
+            return ins
+        outs = [c[0] for c in calls]
+        R = [a for c in calls for a in c[1:3]]
+        bank = outs[0][1]
+        turn = [("t", "turn" + bank, 0, 1)] if bank[0] in "YT" else []
+        cyc = sum(max(64.0, c[2][4]) for c in calls) * pe
+        if first or last:
+            return add({"p": (cyc, run)}, R, outs + turn)
+        i = add({"p": (cyc, run)}, R + outs + turn, [])
+        ops[i]["name"] = bank
+        return i
+
+    def iota(o, pat, cm=0):
+        loose = {} if SCRATCH[o[1]][2] == I32 else {"allow_small_or_imprecise_dtypes": True}
+        return add({"g": (150.0 + 2.0 * o[4], lambda g, T, x: g.iota(ap(T, o), pat, 0, cm, **loose))}, [], [o])
+
+    def dma(q, name, o, i, nbytes):
+        return add({q: (60.0, lambda g, T, x: x["q"].dma_start(ap(T, o), ap(T, i)))}, [i] if i[0] != "h" else [], [o] if o[0] != "h" else [],
+                   kind="d", lat=2000.0 + nbytes / 200.0, sem=name)
+
+    def send(name, to, src, dst, nbytes, extra=()):
+        via = name[0] == "g"
+
+        def run(g, T, x):
+            rid, pid, mask = x["helper"] if via else x["to"][to]
+            return g.remote_dma(ap(T, dst), ap(T, src), T.sem[("h" if via else "r") + name], T.sem["l" + name], pid, rid, mask)
+        s = add({"g": (400.0, run)}, [src], [], kind="s", lat=cfg["rlat"] - 500.0 + nbytes / (150.0 if via else cfg["bw"]), sem="l" + name, extra=extra)
+        add({}, [], [dst], kind="r", lat=cfg["rlat"] + 1000.0 + nbytes / cfg["bw"] if via else 500.0, sem="r" + name, extra=(s,))
+        ops[s]["move"] = (to, src, dst)
         return s
+    slide = lambda name, k: S(name, 15 - k, 143 - k)
 
-    gv = lambda n: 60.0 + ga * n - fix
-    gs = lambda n: 60.0 + sca * n - fix
-    num = lambda a, T: a if a is None or isinstance(a, (int, float)) else a(T)
-    ts = lambda o, i, a, b, p, q=None: (lambda g, T, x: g.vector.tensor_scalar(o(T), i(T), num(a, T), num(b, T), *([p] if q is None else [p, q])))
-    tt = lambda o, i, j, p: (lambda g, T, x: g.vector.tensor_tensor(o(T), i(T), j(T), p))
-    cp = lambda o, i: (lambda g, T, x: g.vector.tensor_copy(o(T), i(T)))
-    scan = lambda o, a, b, p, q: (lambda g, T, x: g.vector.tensor_tensor_scan(o(T), a(T), b(T), 0.0, p, q))
-    act = lambda o, i, f, b=0.0, s=1.0: (lambda g, T, x: g.scalar.activation(o(T), i(T), f, bias=num(b, T), scale=s) if b != 0.0 else g.scalar.activation(o(T), i(T), f, scale=s))
-    mset = lambda o, c: (lambda g, T, x: g.vector.memset(o(T), c))
-    S = lambda name, a=None, b=None, c=None: (lambda T: T[name][:, a:b:c])
-    IND = lambda name, a, b, off, c, d: (lambda T: T[name][:, a:b].indirect(T[off][:, c:d]))
-    AND, SHR = AluOpType.bitwise_and, AluOpType.arith_shift_right
-    EQ, GT, GE, LT = AluOpType.is_equal, AluOpType.is_gt, AluOpType.is_ge, AluOpType.is_lt
+    dma("s", "dq", S("qb"), HBM("qd"), 32768)
+    dma("a", "dw", S("w0", 0, 1), HBM("wt"), 256)
+    dma("s", "dd0", S("Dd"), HBM("dr"), 160000)
+    dma("s", "dg", S("Gi"), HBM("lg"), 690000)
+    dma("s", "dx", S("X"), HBM("xr"), 1700000)
+    do(mset(S("thi"), 0))
+    dma("a", "dt", LEAD("thi", 0, 2), HBM("th"), 64)
+    dma("s", "de", S("e0i"), HBM("e0"), 1800000)
+    dma("s", "dm", LEAD("Dm", 0, 4096), HBM("dr"), 1900000)
 
-    def GAT(o, src, n, R, W, scale=1.0, bias=0.0):
-        fv = ts(o, src, bias, None, ADD) if bias else (ts(o, src, scale, None, MUL) if scale != 1.0 else cp(o, src))
-        return VA(fv, gv(n), act(o, src, AF.Identity if bias else AF.Copy, bias, scale), gv(n) + 15, R, W)
-
-    ld = lambda o, i: (lambda g, T, x: x["q"].dma_start(o(T), i(T)))
-    gsp = cfg["gsp"]
-    gw = 1024 // gsp
-    gi = ["Gi%d" % j for j in range(gsp)]
-    DMA("s", "dq", ld(S("q0"), lambda T: T.qd[:]), 32768, [], ["q0"])
-    DMA("s", "dw", ld(S("w0", 0, 1), lambda T: T.wt[:]), 256, [], ["w0"])
-    DMA("s", "dd0", ld(S("Dd"), lambda T: T.dr[:]), 131072, [], ["Dd"])
-    for j in range(gsp):
-        DMA("s", "dg%d" % j, ld(S("Gi", gw * j, gw * j + gw), lambda T, j=j: T.lg[:, gw * j:gw * j + gw]), 131072 + 4 * 128 * gw * (j + 1), [], [gi[j]])
-    DMA("s", "dx", ld(S("X"), lambda T: T.xr[:]), 1600000, [], ["X0", "X1"])
-    V(mset(S("thi"), 0), 4, [], ["thi"])
-    DMA("s", "dt", ld(lambda T: T.thi[0:128:16, 0:2], lambda T: T.th[:]), 64, [], ["thi"])
-    DMA("s", "de", ld(S("e0i"), lambda T: T.e0[:]), 65536, [], ["e0i"])
-    DMA("s", "dm", ld(lambda T: T.Dm[0:128:16, 0:4096], lambda T: T.dr[:]), 131072, [], ["Dm"])
-
-    io = lambda o, pat, cm=0, fl=True: (lambda g, T, x: g.iota(o(T), pat, 0, cm, allow_small_or_imprecise_dtypes=True) if fl else g.iota(o(T), pat, 0, cm))
-    GP(io(S("pI", 0, 1), [[1, 1]], 1, False), 1, [], ["pI"])
-    GP(io(S("colg"), [[1, 8], [0, 16]]), 128, [], ["colg"])
-    GP(io(S("colb"), [[0, 16], [1, 16]]), 256, [], ["colb"])
-    GP(io(S("col"), [[1, 144]]), 144, [], ["col"])
-    GP(io(S("aq", 0, 8), [[1, 8]]), 8, [], ["aq0"])
-    GP(io(S("aq", 8, 16), [[0, 2], [1, 4]]), 8, [], ["aq1"])
-    GP(io(S("iot"), [[1, 512]]), 512, [], ["iot"])
-    V(ts(S("pb", 0, 1), S("pI", 0, 1), 15, None, AND), 1, ["pI"], ["pb0"])
-    V(ts(S("pb", 1, 2), S("pI", 0, 1), 4, None, SHR), 1, ["pI"], ["pb1"])
-    V(cp(S("pc", 0, 2), S("pb", 0, 2)), 2, ["pb0", "pb1"], ["b", "gp"])
-    V(cp(S("pc", 2, 3), S("pI", 0, 1)), 1, ["pI"], ["p"])
     pc = lambda j: S("pc", j, j + 1)
-    lin = lambda j, src, sc_, bi, R, W: VA(ts(pc(j), pc(src), float(sc_), float(bi), MUL, ADD), 1, act(pc(j), pc(src), AF.Identity, float(bi), float(sc_)), 1, R, W)
-    lin(3, 2, 1, 1, ["p"], ["p1"])
-    lin(4, 0, 1, 1, ["b"], ["b1"])
-    lin(5, 0, 8, 0, ["b"], ["b8"])
-    lin(6, 0, 32, 0, ["b"], ["b32"])
-    lin(7, 0, 1, 4096, ["b"], ["b4k"])
-    lin(8, 1, 16, 15, ["gp"], ["top"])
-    V(ts(pc(9), pc(0), 15.0, None, EQ), 1, ["b"], ["is15"])
-    lin(10, 9, 1.0 - 1.0 / 4096, 1.0 / 4096, ["is15"], ["mp"])
-    lin(11, 9, -0.5, 0.5, ["is15"], ["t1s"])
-    lin(12, 9, -1, 0, ["is15"], ["t1b"])
-    V(ts(pc(13), pc(0), 0.0, 1.0e6, EQ, MUL), 1, ["b"], ["t2b"])
-    V(ts(S("Bo"), S("colg"), pc(1), None, EQ), 128, ["colg", "gp"], ["Bo"])
-    scl = lambda o, i, k, n=128: VA(ts(S(o), S(i), float(k), None, MUL), n / 2, act(S(o), S(i), AF.Copy, 0.0, float(k)), n, [i], [o])
-    V(ts(S("W2"), S("Bo"), S("w0", 0, 1), 2.0, MUL, MUL), 64, ["Bo", "w0"], ["W2"])
-    scl("nBo", "Bo", -1)
-    scl("Bf", "Bo", 1)
-    V(ts(S("Id"), S("col", 0, 128), pc(2), None, EQ), 128, ["col", "p"], ["Id"])
-    scl("nI", "Id", -1)
-    scl("Idf", "Id", 1)
-    scl("nIf", "Id", -1)
-    lin(14, 0, -1, 0, ["b"], ["nb"])
-    lin(15, 0, -1, -0.5, ["b"], ["nb1"])
-    lin(16, 0, -2, -1, ["b"], ["nb2"])
-    scl("BI", "Id", 2048)
-    scl("nBI", "Id", -2048)
-    V(ts(S("Sh"), S("col", 0, 128), pc(3), -2048.0, EQ, MUL), 128, ["col", "p1"], ["Sh"])
-    V(ts(S("tmp"), S("col", 0, 128), pc(2), None, GE), 128, ["col", "p"], ["tmp"])
-    V(tt(S("Tri"), S("tmp"), S("Bo"), MUL), 256, ["tmp", "Bo"], ["Tri"])
-    V(ts(S("tmp2"), S("colb"), pc(0), None, GT), 256, ["colb", "b"], ["tmp2"])
-    V(ts(S("ms"), S("colb"), pc(4), 4096.0, EQ, MUL), 256, ["colb", "b1"], ["ms"])
-    V(tt(S("ms", 0, 128), S("ms", 0, 128), S("tmp2", 0, 128), MAX), 256, ["ms", "tmp2"], ["ms0"])
-    V(tt(S("ms", 128, 256), S("ms", 128, 256), S("tmp2", 128, 256), MAX), 256, ["ms", "tmp2"], ["ms1"])
-    V(ts(S("poi"), S("colb", 0, 128), pc(0), -8192.0, GE, MUL), 128, ["colb", "b"], ["poi"])
-    V(ts(S("dl"), S("colb", 0, 128), pc(0), None, EQ), 128, ["colb", "b"], ["dl"])
-    V(mset(S("rp"), 1.0), 512, [], ["rp"])
-    V(mset(S("rp", 15, 1024, 16), 0.0), 64, [], ["rp"])
-    V(cp(S("r2"), S("rp", 0, 128)), 64, ["rp"], ["r2"])
-    V(mset(S("r2", 14, 128, 16), 8192.0), 8, [], ["r2"])
-    V(ts(S("S1"), S("col"), pc(8), None, EQ), 144, ["col", "top"], ["S1"])
-    scl("S2", "S1", 2, 144)
-    scl("Sn", "S1", -1, 144)
-    VA(ts(S("ix"), S("col", 0, 128), 16.0, 2048.0, MUL, ADD), 64, act(S("ix"), S("col", 0, 128), AF.Identity, 2048.0, 16.0), 128, ["col"], ["ix"])
-    V(mset(S("opn", 0, 128), 0.0), 64, [], ["opn0"])
-    V(mset(S("opn", 128, 256), -2048.0), 64, [], ["opn1"])
-    V(mset(S("c256"), 256.0), 128, [], ["c256"])
-    V(mset(S("o16th"), 0.0625), 64, [], ["o16th"])
-    V(cp(S("ast"), S("aq", 0, 8)), 8, ["aq0"], ["ast"])
-    V(ts(S("stw", 0, 8), S("aq", 8, 16), 128.0, pc(5), MUL, ADD), 8, ["aq1", "b8"], ["stw0"])
-    V(ts(S("stw", 8, 16), S("aq", 8, 16), 512.0, pc(6), MUL, ADD), 8, ["aq1", "b32"], ["stw1"])
-    V(mset(S("D0"), 0.0), 192, [], ["D00", "D01"])
-    V(mset(S("pm", 0, 1), 0.0), 1, [], ["pmz"])
-    V(cp(S("thf", 0, 2), S("thi", 0, 2)), 2, ["thi"], ["thf"])
-    PE(lambda T: [(T.P0[:, 128:130], T.Bf[:], T.thf[:, 0:2], True, True)], 256, ["Bf", "thf"], ["unw"], "P0")
-    V(ts(S("thc", 0, 1), S("P0", 128, 129), pc(11), pc(12), MUL, ADD), 1, ["unw", "t1s", "t1b"], ["th1"], "P0")
-    V(ts(S("thc", 1, 2), S("P0", 129, 130), 0.5, pc(13), MUL, ADD), 1, ["unw", "t2b"], ["th2"], "P0")
-    V(ts(S("thc", 2, 4), S("thc", 0, 2), -1.0, -0.25, MUL, ADD), 1, ["th1", "th2"], ["nth"])
-    VA(ts(S("qh"), S("q0"), 0.5, None, MUL), 64, act(S("qh"), S("q0"), AF.Copy, 0.0, 0.5), 128, ["q0"], ["qh0", "qh1"])
-    V(cp(S("tri", 2, 384, 3), S("e0i")), 128, ["e0i"], ["tri0", "tri1"])
+    iota(S("pI", 0, 1), [[1, 1]], 1)
+    iota(S("col"), [[1, 144]])
+    iota(S("colg"), [[1, 8], [0, 16]])
+    iota(S("colb"), [[0, 64], [1, 16]])
+    iota(S("aq"), [[0, 2], [1, 4]])
+    iota(S("idx"), [[256, 4], [1, 16]])
+    iota(S("iot"), [[1, 512]])
+    iota(S("ab", 0, 256), [[-16, 4], [1, 64]])
+    do(ts(S("pb", 0, 1), S("pI", 0, 1), 15, None, AND))
+    do(ts(S("pb", 1, 2), S("pI", 0, 1), 4, None, SHR))
+    do(cp(S("pc", 0, 2), S("pb", 0, 2)))
+    do(cp(pc(2), S("pI", 0, 1)))
+    for j, src, s, b in ((3, 2, 1, 1), (4, 0, 8, 0), (5, 0, 32, 0), (6, 0, 16, 0), (7, 1, 16, 15), (8, 0, 1, 4096), (9, 0, 2.0 ** 21, 0)):
+        lin(pc(j), pc(src), float(s), float(b))
+    do(ts(pc(10), pc(0), 0.0, None, EQ))
+    for j, s, b in ((11, -2048, 0), (12, 7, 1), (13, 127, 1), (14, 128, 0), (15, 1.0e6, 2048)):
+        lin(pc(j), pc(10), float(s), float(b))
+    do(ts(S("S1"), S("col"), pc(7), None, EQ))
+    do(ts(S("Bo"), S("colg"), pc(1), None, EQ))
+    do(ts(S("Id"), S("col", 0, 128), pc(2), None, EQ))
+    do(ts(S("W1"), S("S1"), S("w0", 0, 1), 2.0 ** -13, MUL, MUL))
+    do(ts(S("W2"), S("Bo"), S("w0", 0, 1), 2.0 ** -13, MUL, MUL))
+    for o, i, s in (("nBo", "Bo", -1.0), ("Bhi", "Bo", pc(9)), ("nI", "Id", -1.0), ("I8k", "Id", 8192.0), ("BI", "Id", BIG), ("nBI", "Id", -BIG),
+                    ("R0", "Id", pc(14)), ("S2", "S1", 2.0), ("Sn", "S1", -1.0), ("S4", "S1", -BIG), ("Sw", "S1", pc(12))):
+        lin(S(o), S(i), s)
+    do(ts(S("Sh"), S("col", 0, 128), pc(3), -BIG, EQ, MUL))
+    do(ts(S("tmp"), S("col", 0, 128), pc(2), None, GE))
+    do(tt(S("Tri"), S("tmp"), S("Bo"), MUL))
+    for h in range(2 if any(cfg["ax"]) else 0):
+        do(ts(S("colm"), S("colb", 0, 128), 15.5 - cfg["ax"][h], -1.0, AluOpType.is_lt, MUL))
+        do(tt(S("nB%d" % h), S("colm"), S("Bo"), MUL))
+    lin(S("TB"), S("Tri"), BIG)
+    lin(S("nTB"), S("Tri"), -BIG)
+    do(ts(S("dl"), S("col", 0, 16), pc(0), None, EQ))
+    do(ts(S("LT"), S("colb"), pc(0), None, GT))
+    do(ts(S("rp"), S("colb"), 15.0, None, NE))
+    do(ts(S("frc"), S("colb", 0, 64), 15.0, -2.0 ** 25, EQ, MUL))
+    do(ts(S("poi"), S("ab", 0, 256), pc(0), 8192.0, GE, MUL))
+    lin(S("eb"), S("aq"), 256.0)
+    do(ts(S("spare"), S("aq"), 16.0, pc(8), MUL, ADD))
+    do(ts(S("stw", 0, 8), S("aq"), 128.0, pc(4), MUL, ADD))
+    do(ts(S("stw", 8, 16), S("aq"), 512.0, pc(5), MUL, ADD))
+    for o, c in ((S("cu", 0, 8), -2048.0), (S("cu", 8, 16), 592.0 / 4096), (S("n16th"), -0.0625), (S("c2k"), 2048.0), (S("opn", 0, 64), -BIG),
+                 (S("opn", 64, 128), 0.0), (S("pm", 0, 2080, 1040), 0.0)):
+        do(mset(o, c))
+    thc = lambda j: S("thc", j, j + 1)
+    do(ts(S("th16", 0, 2), S("thi", 0, 2), pc(11), None, ADD))
+    mm([(S("P0", 256, 258), S("Bo"), S("th16", 0, 2))])
+    do(ts(thc(0), S("P0", 256, 257), BIG, 2048.0 * BIG + 2048.0, MUL, ADD))
+    do(ts(thc(1), thc(0), -1.0, pc(6), MUL, ADD))
+    do(ts(thc(2), S("P0", 257, 258), pc(15), None, ADD))
+    do(ts(thc(3), thc(2), -1.0, None, MUL))
+    do(ts(S("idc"), S("idx"), thc(1), None, ADD))
+    do(ts(S("qp"), S("qb"), 2.0, 2048.0, MUL, ADD))
     for j in range(4):
-        V(cp(S("G", 256 * j, 256 * j + 256), S("Gi", 256 * j, 256 * j + 256)), 256, gi, ["G%d" % (j // 2)])
+        do(cp(S("G", 256 * j, 256 * j + 256), S("Gi", 256 * j, 256 * j + 256)))
 
+    A0 = -10952.0 - 13.0 / 32
     gch = cfg["gch"]
-    nch = 1024 // gch
-    halves = lambda k: [[0, 1]] if k == 1 else [[0], [1]]
     for t in range(STEPS):
         last = t == STEPS - 1
-        step[0], step[1] = t, {}
-        cur, nxt = (("tri", "trj") if t % 2 == 0 else ("trj", "tri")) if cfg["trv"] else ("tri", "tri")
-        GR, DR = "GR%d" % t, "DR%d" % t
-        GO, gtag = ("G", ["G0", "G1"]) if t else ("Gi", gi)
-        rtag = [GR + "a", GR + "b"]
-        bulk = lambda extra, t=t: (SEND("f%d" % (t + 1), t + 1, S("G", 0, 512), S("GR%d" % (t + 1), 0, 512), 262144, ["G0"], ["GR%da" % (t + 1)], extra),
-                                   SEND("g%d" % (t + 1), t + 1, S("G", 512, 1024), S("GR%d" % (t + 1), 512, 1024), 262144, ["G1"], ["GR%db" % (t + 1)], extra))
+        step[0] = t
+        GR, DR, G1 = "GR%d" % t, "DR%d" % t, "GR%d" % (t + 1)
+        GO = S("G") if t else S("Gi")
+        bulk = lambda extra: [send("%s%d" % (k, t + 1), t + 1, S("G", a, a + 512), S(G1, a, a + 512), 262144, extra) for k, a in (("f", 0), ("g", 512))]
         if 1 <= t < STEPS - 1:
             bulk(())
         if t:
             for h in range(2):
-                V(cp(IND(GR, 512 * h, 512 * h + 512, "CR%d" % t, 4 * h, 4 * h + 4), S("ER%d" % t, 64 * h, 64 * h + 64)), gs(64),
-                  ["CR%d" % t, "ER%d%d" % (t, h)], [GR + "ab"[h]])
-        for hs in halves(cfg["nu"] if t else 1):
-            tg = lambda s, hs=hs: [s + str(h) for h in hs]
-            TB = "T%d" % hs[0]
-            bias[0] = cfg["bu"] * (1 - hs[0]) * (len(hs) == 1)
-            c0, n = 64 * hs[0], 64 * len(hs)
-            c1, w0, nw, s0 = c0 + n, c0 // 16, n // 16, 2 * c0
-            w1, n0 = w0 + nw, 2 * w0
-            PE(lambda T, TB=TB, c0=c0, c1=c1, n=n: [(T[TB][:, 0:n], T.Bo[:], T.c256[:, 0:n], True, False), (T[TB][:, 0:n], T.W2[:], T.qh[:, c0:c1], False, True)], 2 * n,
-               ["Bo", "c256", "W2"] + tg("qh"), [TB], TB)
-            V(scan(S("sc", s0, s0 + n), S("ms", 0, n), S(TB, 0, n), MUL, MAX), n, ["ms0"], [TB] + tg("sc"), TB)
-            V(ts(S("ui", w0, w1), S("sc", s0 + 15, s0 + n, 16), pc(10), None, MUL), 4, tg("sc") + ["mp"], tg("ui"))
-            V(ts(S("u", w0, w1), S("ui", w0, w1), 4095, None, AND), 4, tg("ui"), tg("u"))
-            V(tt(S("sq", w0, w1), S("u", w0, w1), S("u", w0, w1), MUL), 4, tg("u"), tg("sq"))
-            if t:
-                V(ts(S("lin", w0, w1), S("u", w0, w1), 37.0, S("Ac", 0, 1), MUL, ADD), 4, tg("u") + ["Ac"], tg("lin"))
-            else:
-                V(ts(S("lin", w0, w1), S("u", w0, w1), 37.0, None, MUL), 4, tg("u"), tg("lin"))
-            V(ts(S("sq5", w0, w1), S("sq", w0, w1), 5, None, SHR), 4, tg("sq"), tg("sq5"))
-            V(tt(S("sm", w0, w1), S("sq5", w0, w1), S("lin", w0, w1), ADD), 4, tg("sq5") + tg("lin"), tg("sm"))
-            V(ts(S("nlh", n0, n0 + nw), S("sm", w0, w1), 255, None, AND), 4, tg("sm"), tg("nlo"))
-            V(ts(S("nlh", n0 + nw, n0 + 2 * nw), S("sm", w0, w1), 8, 15, SHR, AND), 4, tg("sm"), tg("nhi"))
-            V(cp(S("n16", n0, n0 + 2 * nw), S("nlh", n0, n0 + 2 * nw)), 8, tg("nlo") + tg("nhi"), tg("n16"))
-            if cfg["hmv"]:
-                V(cp(S("hm", c0, c1), IND("dl", 0, 16, "n16", n0 + nw, n0 + 2 * nw)), gv(n), ["dl"] + tg("n16"), tg("hm"))
-            else:
-                GAT(S("hm", c0, c1), IND("dl", 0, 16, "n16", n0 + nw, n0 + 2 * nw), n, ["dl"] + tg("n16"), tg("hm"))
-            V(tt(S("cand", s0, s0 + n), IND("Dd", 0, 256, "n16", n0, n0 + nw), S("hm", c0, c1), MUL), gv(n), ["Dd"] + tg("n16") + tg("hm"), tg("caP"))
-            if t:
-                V(tt(S("cand", s0 + n, s0 + 2 * n), IND(DR, 0, 256, "n16", n0, n0 + nw), S("hm", c0, c1), MUL), gv(n), [DR] + tg("n16") + tg("hm"), tg("caB"))
-            else:
-                SEND("nb", "b", S("n16"), S("nq"), 4096, tg("n16"), ["nq"])
-                GAT(S("hq"), IND("dl", 0, 16, "nq", 8, 16), n, ["dl", "nq"], ["hq"])
-                V(tt(S("cand", n, 2 * n), IND("Dd", 0, 256, "nq", 0, 8), S("hq"), MUL), gv(n), ["Dd", "nq", "hq"], tg("caB"))
-            if t and not cfg["csp"]:
-                parts = [(0, 2 * n, tg("caP") + tg("caB"), tg("cP") + tg("cB"))]
-            else:
-                parts = [(0, n, tg("caP"), tg("cP")), (n, 2 * n, tg("caB"), tg("cB"))]
-            for (a, b, R, W) in parts:
-                PE(lambda T, TB=TB, a=a, b=b, s0=s0, n=n: [(T[TB][:, n + a:n + b], T.Bo[:], T.c256[:, a:b], True, False),
-                                                         (T[TB][:, n + a:n + b], T.Bf[:], T.cand[:, s0 + a:s0 + b], False, True)], 5 * (b - a), ["Bo", "c256", "Bf"] + R, [TB], TB)
-                V(scan(S("sc", s0 + a, s0 + b), S("ms", 0, b - a), S(TB, n + a, n + b), MUL, MAX), b - a, ["ms0", "ms1"] if b - a > 128 else ["ms0"], [TB] + tg("sc"), TB)
-                V(ts(S("c16", n0 + a // 16, n0 + b // 16), S("sc", s0 + a + 15, s0 + b, 16), pc(10), -4096.0, MUL, ADD), 8, tg("sc") + ["mp"], W)
-            own, oth = IND(GO, 0, 1024, "c16", n0, n0 + nw), IND(GR, 0, 1024, "c16", n0 + nw, n0 + 2 * nw)
+                do(cp(IND(S(GR, 512 * h, 512 * h + 512), S("CR%d" % t, 4 * h, 4 * h + 4)), S("ER%d" % t, 64 * h, 64 * h + 64)))
+        for c0, n in ([(0, 128)] if t == 0 or cfg["nu"] == 1 else [(0, 64), (64, 64)]):
+            c1, w0, nw = c0 + n, c0 // 16, n // 16
+            step[1] = c0 // 64
+            w1, n0, Y = w0 + nw, 2 * w0, "P%d" % (c0 // 64)
+            y, tile = S(Y, 128, 128 + nw), lambda name: S(name, w0, w1)
+            mm([(y, S("W2"), S("cu", 0, nw)), (y, S("Id"), S("cu", 8, 8 + nw))] + [(y, slide("W1", b), S("qp", c0 + b, c1, 16)) for b in range(16)])
+            do(ts(tile("hh"), y, -2639.5 / 4096, None, ADD))
+            do(tt(tile("v"), y, tile("hh"), SUB))
+            do(tt(tile("sq"), tile("v"), tile("v"), MUL), act(tile("sq"), tile("v"), AF.Square))
+            do(ts(tile("nf"), tile("sq"), 2.0 ** 19, S("Ac", 0, 1) if t else A0, MUL, ADD))
+            do(ts(S("nlh", n0, n0 + nw), tile("nf"), 255, None, AND))
+            do(ts(S("nlh", n0 + nw, n0 + 2 * nw), tile("nf"), 8, 15, SHR, AND))
+            do(cp(S("n16", n0, n0 + 2 * nw), S("nlh", n0, n0 + 2 * nw)))
+            lo, hi = S("n16", n0, n0 + nw), S("n16", n0 + nw, n0 + 2 * nw)
             if t == 0:
-                V(cp(S("PB", c0, c1), own), gv(n), gtag + tg("cP"), tg("P16"))
-                V(cp(S("Bq"), IND(GO, 0, 1024, "c16", 8, 16)), gv(n), gtag + tg("cB"), ["Bq"])
-                bulk((SEND("b0", 0, S("Bq"), S("PB", 128, 256), 32768, ["Bq"], tg("B16")),))
-                V(cp(S("Pf"), S("PB", 0, 128)), n, tg("P16"), tg("Pf"))
-                V(cp(S("Bg"), S("PB", 128, 256)), n, tg("B16"), tg("Bg"))
+                send("nb", "b", S("n16"), S("nq"), 4096)
+            lin(S("hm", c0, c1), IND(S("dl"), hi))
+            s0 = 2 * c0
+            do(tt(S("cand", s0, s0 + n), IND(S("Dd"), lo), S("hm", c0, c1), MUL))
+            if t:
+                do(tt(S("cand", s0 + n, s0 + 2 * n), IND(S(DR), lo), S("hm", c0, c1), MUL))
+                parts = [(0, 2 * n)]
             else:
-                GAT(S("Pf", c0, c1), own, n, gtag + tg("cP"), tg("Pf"))
-                GAT(S("Bg", c0, c1), oth, n, rtag + tg("cB"), tg("Bg"))
-                if cfg["pcv"] & 1:
-                    V(cp(S("PB", c0, c1), S("Pf", c0, c1)), n, tg("Pf"), tg("P16"))
-                else:
-                    V(cp(S("PB", c0, c1), own), gv(n), gtag + tg("cP"), tg("P16"))
-                if cfg["pcv"] & 2:
-                    V(cp(S("PB", 128 + c0, 128 + c1), S("Bg", c0, c1)), n, tg("Bg"), tg("B16"))
-                else:
-                    V(cp(S("PB", 128 + c0, 128 + c1), oth), gv(n), rtag + tg("cB"), tg("B16"))
-        bias[0] = 0.0
-        for h in range(2):
-            TB, a0, a3 = "T%d" % h, 64 * h, 192 * h
-            if cfg["trv"]:
-                V(tt(S(cur, a3 + 1, a3 + 192, 3), S("Pf", a0, a0 + 64), S(cur, a3 + 2, a3 + 192, 3), SUB), 128, ["Pf%d" % h], [cur + str(h)])
-                V(tt(S(cur, a3, a3 + 192, 3), S("Bg", a0, a0 + 64), S("Pf", a0, a0 + 64), SUB), 128, ["Pf%d" % h, "Bg%d" % h], [cur + str(h)])
-                continue
-            PE(lambda T, TB=TB, a0=a0, a3=a3: [(T[TB][:, 1:192:3], T.Idf[:], T.Pf[:, a0:a0 + 64], True, False), (T[TB][:, 1:192:3], T.nIf[:], T.tri[:, a3 + 2:a3 + 192:3], False, True),
-                                             (T[TB][:, 2:192:3], T.Idf[:], T.tri[:, a3 + 2:a3 + 192:3], True, True)], 768, ["Idf", "nIf", "Pf%d" % h, "tri%d" % h], [TB], TB)
-            PE(lambda T, TB=TB, a0=a0: [(T[TB][:, 0:192:3], T.Idf[:], T.Bg[:, a0:a0 + 64], True, False), (T[TB][:, 0:192:3], T.nIf[:], T.Pf[:, a0:a0 + 64], False, True)], 512,
-               ["Idf", "nIf", "Pf%d" % h, "Bg%d" % h], [TB], TB)
-        for z, nm in ((0, "x"), (1, "y")):
+                lin(S("lt"), IND(S("dl"), S("nq", 8, 16)))
+                do(tt(S("cand", n, 2 * n), IND(S("Dd"), S("nq", 0, 8)), S("lt"), MUL))
+                parts = [(0, n), (n, 2 * n)]
+            for a, b in parts:
+                ct = S(Y, 144 + a // 16, 144 + b // 16)
+                mm([(ct, slide("S1", k), S("cand", s0 + a + k, s0 + b, 16)) for k in range(16)])
+                do(cp(S("c16", n0 + a // 16, n0 + b // 16), ct))
+            if not last:
+                lin(S("lor", c0, c1), IND(S("iot", 0, 256), lo))
+            do(cp(S("PB", c0, c1), IND(GO, S("c16", n0, n0 + nw))))
+            if t:
+                do(cp(S("PB", 128 + c0, 128 + c1), IND(S(GR), S("c16", n0 + nw, n0 + 2 * nw))))
+            else:
+                do(cp(S("Bq"), IND(GO, S("c16", 8, 16))))
+                bulk((send("b0", 0, S("Bq"), S("PB", 128, 256), 32768),))
+        for z in range(2):
+            do(ts(S("PBh", 128 * z, 128 * z + 128), S("PB", 128 * z, 128 * z + 128), -2048.0, None, ADD))
+        for z in range(2):
             for h in range(2):
-                for j in range(nch):
-                    o0 = 2048 * z + 1024 * h + gch * j
-                    f0 = 128 * z + 64 * h + gch // 16 * j
-                    bias[0] = cfg["bg"] * (2048 - 1024 * h - gch * j) / 512.0 - cfg["by"] * z
-                    GAT(S("XY", o0, o0 + gch), IND("X", 0, 4096, "PB", f0, f0 + gch // 16), gch, ["X0", "X1", "PB"[z] + "16" + str(h)], ["%s%d%d" % (nm, h, j)], 0.5)
-        bias[0] = 0.0
-        V(ts(S("clx0", 0, 8), S("u"), 7, None, AND), 8, ["u0", "u1"], ["cl0"])
-        V(ts(S("clx0", 8, 16), S("u"), 31, None, AND), 8, ["u0", "u1"], ["cx0"])
-        V(tt(S("clx1"), S("clx0"), S("stw"), ADD), 32, ["cl0", "cx0", "stw0", "stw1"], ["clx1"])
-        V(cp(S("clx"), S("clx1")), 16, ["clx1"], ["clx"])
-        for h in range(2):
-            GAT(S("oldh", 64 * h, 64 * h + 64), IND("X", 2048 * h, 2048 * h + 2048, "clx", 8 + 4 * h, 12 + 4 * h), 64, ["X%d" % h, "clx"], ["oldh%d" % h], 0.5)
+                step[1] = h
+                for j in range(0, 1024, gch):
+                    o0, f0 = 2048 * h + 1024 * z + j, 128 * z + 64 * h + j // 16
+                    lin(S("XY", o0, o0 + gch), IND(S("X"), S("PB", f0, f0 + gch // 16)))
+        do(ts(S("ui"), S("v"), 4096.0, -592.0, MUL, ADD))
+        do(ts(S("cx0", 0, 8), S("ui"), 7, None, AND))
+        do(ts(S("cx0", 8, 16), S("ui"), 31, None, AND))
+        do(tt(S("cx1"), S("cx0"), S("stw"), ADD))
+        do(cp(S("clx"), S("cx1")))
         if not last:
-            SEND("c%d" % (t + 1), t + 1, S("clx", 0, 8), S("CR%d" % (t + 1)), 2048, ["clx"], ["CR%d" % (t + 1)])
+            send("c%d" % (t + 1), t + 1, S("clx", 0, 8), S("CR%d" % (t + 1)), 2048)
+            do(ts(S("n32"), S("nf"), 4095, None, AND))
+            do(ts(S("nn"), S("n32"), -8192.0, None, MUL))
             for h in range(2):
-                GAT(S("clR", 64 * h, 64 * h + 64), IND("iot", 0, 512, "clx", 4 * h, 4 * h + 4), 64, ["iot", "clx"], ["clR%d" % h], 1.0, 512.0 * h)
-            V(ts(S("n32"), S("sm"), 4095, None, AND), 8, ["sm0", "sm1"], ["n32"])
-            V(cp(S("nf"), S("n32")), 8, ["n32"], ["nf"])
-            GAT(S("bc"), IND("nf", 0, 8, "ast", 0, 8), 128, ["nf", "ast"], ["bc"])
-            V(tt(S("x1"), S("bc"), S("dl"), MUL), 256, ["bc", "dl"], ["x1"])
-            PE(lambda T: [(T.P0[:, 128:256], T.Id[:], T.poi[:], True, False), (T.P0[:, 128:256], T.Bf[:], T.x1[:], False, True)], 640, ["Id", "poi", "Bf", "x1"], ["unw"], "P0")
-            V(tt(S("eq"), S("P0", 128, 256), S("bc"), EQ), 128, ["unw", "bc"], ["eq"], "P0")
-            V(scan(S("eqs"), S("eq"), S("r2"), MAX, MUL), 64, ["eq", "r2"], ["eqs"])
-            V(tt(S("tt"), S("eqs", 14, 128, 16), S("nf"), ADD), 16, ["eqs", "nf"], ["tt"])
-            V(ts(S("o16", 0, 16, 2), S("tt"), pc(7), None, MIN), 8, ["tt", "b4k"], ["o16"])
-            for a in range(7, -1, -1):
-                V(cp(IND("Dm", 0, 4112, "o16", 2 * a, 2 * a + 1), S("clR", 16 * a, 16 * a + 16)), gs(16), ["o16", "clR%d" % (a // 4)], ["Dm"])
-            DMA("s", "dd%d" % (t + 1), ld(S("Dd"), lambda T: T.Dm[0:128:16, 0:4096]), 131072, ["Dm"], ["Dd"])
-            SEND("d%d" % (t + 1), t + 1, S("Dd"), S("DR%d" % (t + 1)), 131072, ["Dd"], ["DR%d" % (t + 1)])
-        xs = [["x%d%d" % (h, j) for j in range(nch)] for h in range(2)]
-        ys = [["y%d%d" % (h, j) for j in range(nch)] for h in range(2)]
+                c0, c1 = 64 * h, 64 * h + 64
+                lin(S("clR", c0, c1), IND(S("iot"), S("clx", 4 * h, 4 * h + 4)), 1.0, 512.0 * h)
+                rep = S("P%d" % h, 320, 384)
+                mm([(rep, S("Bhi"), S("hm", c0, c1)), (rep, S("I8k"), S("lor", c0, c1))])
+                for a in range(4 * h, 4 * h + 4):
+                    do(act(S("ab", 64 * a, 64 * a + 64), rep, AF.Abs, S("nn", a, a + 1)))
+                back = lambda name: S(name, 256 * h + 255, 256 * h - 1 if h else None, -1)
+                do(scan(back("mn"), back("ab"), S("poi", None, None, -1), MIN, MAX))
+            do(tt(S("ow"), S("spare"), S("mn", 0, 512, 64), SUB))
+            do(tt(S("ow"), S("ow"), S("n32"), MAX))
+            do(cp(S("o16"), S("ow")))
+            for h in (1, 0):
+                do(cp(IND(S("Dm"), S("o16", 4 * h, 4 * h + 4)), S("clR", 64 * h, 64 * h + 64)))
+            dma("s", "dd%d" % (t + 1), S("Dd"), LEAD("Dm", 0, 4096), 131072)
+            send("d%d" % (t + 1), t + 1, S("Dd"), S("DR%d" % (t + 1)), 131072)
         for h in range(2):
-            k0 = 1024 * h
+            k0 = 2048 * h
+            step[1] = h
             for c in range(2):
-                Y, o0 = "Y%d%d" % (h, c), k0 + 512 * c
-                part = slice(c * nch // 2, (c + 1) * nch // 2) if nch > 1 else slice(0, 1)
-                PE(lambda T, Y=Y, o0=o0: [(T[Y][:], T.Id[:], T.XY[:, o0:o0 + 512], True, False)], 512, ["Id"] + xs[h][part], [Y], Y)
-                PE(lambda T, Y=Y, o0=o0: [(T[Y][:], T.nI[:], T.XY[:, 2048 + o0:2048 + o0 + 512], False, True)], 512, ["nI"] + ys[h][part], [Y], Y)
-                bias[0] = cfg["ba"]
-                A(act(S("A1", o0, o0 + 512), S(Y), AF.Abs), 512, [], [Y, "A1%d%d" % (h, c)], Y)
-                bias[0] = 0.0
-            V(scan(S("pm", 1 + k0, 1 + k0 + 1024), S("XY", k0, k0 + 1024), S("rp"), MAX, MUL), 512, xs[h] + ["rp"], ["pm%d" % h])
-        for hs in halves(cfg["nm"]):
-            tg = lambda s, hs=hs: [s + str(h) for h in hs]
-            full = len(hs) == 2
-            h0 = hs[0]
-            TB, T2, PB_, PO = ("T0", "T1", "P0", "P1") if full else ("T%d" % h0, "T%d" % h0, "P%d" % h0, "P%d" % (1 - h0))
-            c0, n = 64 * h0, 64 * len(hs)
-            c1, w0, w1, s0, k0, k1, b3, b4 = c0 + n, c0 // 16, (c0 + n) // 16, 2 * c0, 16 * c0, 16 * (c0 + n), 3 * c0, 3 * (c0 + n)
-            r1, rc, rs, r2, rl = (384, 0, 128, 0, 0) if full else (192, 256, 320, 384, 64)
-            X_ = [a for h in hs for a in xs[h]]
-            allx = [a for h in range(hs[-1] + 1) for a in xs[h]]
-            ally = [a for h in range(hs[-1] + 1) for a in ys[h]]
-            pw = 1024 * (hs[-1] + 1)
-            d_ = lambda T, c0=c0, c1=c1: T.dh[:, c0:c1]
-            bias[0] = cfg["bh"] * (1 - h0) * (not full)
-            for h in hs:
-                PE(lambda T, TB=TB, k0=1024 * h, r1=r1 + 64 * (h - h0): [(T[TB][:, r1:r1 + 64], T.S1[:, 15 - k:143 - k], T.A1[:, k0 + k:k0 + 1024:16], k == 0, k == 15) for k in range(16)], 1024,
-                   ["S1"] + ["A1%d%d" % (h, c) for c in range(2)], [TB], TB)
-            for h in hs:
-                for c in range(2):
-                    Y = "Y%d%d" % (h, c)
-                    PE(lambda T, Y=Y, o0=2048 + 1024 * h + c, o1=3072 + 1024 * h: [(T[Y][:], T.Id[:], T.XY[:, o0:o1:2], True, False)], 512, ["Id"] + ys[h], [Y], Y)
-            if cfg["sgn"] & 1:
-                A(act(S("ov", c0, c1), S(TB, r1, r1 + n), AF.Sign, S("thc", 2, 3)), n, ["nth"], [TB] + tg("ov"), TB)
-            else:
-                V(ts(S("ov", c0, c1), S(TB, r1, r1 + n), S("thc", 0, 1), None, GT), n, ["th1"], [TB] + tg("ov"), TB)
-            PE(lambda T, TB=TB, c0=c0, c1=c1, rc=rc, n=n: [(T[TB][:, rc:rc + n], T.Tri[:], T.ov[:, c0:c1], True, True)], n, ["Tri"] + tg("ov"), [TB], TB)
-            lv, lb = (pc(15), pc(14)) if cfg["sgn"] & 1 else (0.5, 1.0)
-            VA(ts(S("lt", c0, c1), S(TB, rc, rc + n), lv, None, LT), n, act(S("lt", c0, c1), S(TB, rc, rc + n), AF.Relu, lb, -1.0), n, ["nb", "nb1"], [TB] + tg("lt"), TB)
-            PE(lambda T, TB=TB, c0=c0, c1=c1, rs=rs, n=n: [(T[TB][:, rs:rs + n], T.Id[:], T.ix[:, c0:c1], True, False), (T[TB][:, rs:rs + n], T.Bo[:], T.lt[:, c0:c1], False, True)], 2 * n,
-               ["Id", "ix", "Bo"] + tg("lt"), [TB], TB)
-            V(scan(S("sc", s0, s0 + n), S("ms", 0, n), S(TB, rs, rs + n), MUL, MAX), n, ["ms0"], [TB] + tg("sc"), TB)
-            V(ts(S("s16", w0, w1), S("sc", s0 + 15, s0 + n, 16), pc(10), -2048.0, MUL, ADD), 4, tg("sc") + ["mp"], tg("s16"))
-            dx = lambda T, B=T2, r2=r2, n=n: T[B][:, r2:r2 + n]
-            dy = lambda T, B=T2, r2=r2, n=n: T[B][:, r2 + n:r2 + 2 * n]
-            opened = lambda T, B=T2, r2=r2, n=n: [(T[B][:, r2:r2 + 2 * n], T.Id[:], T.opn[:, 128 - n:128 + n], True, False)]
-            corr = lambda T, dx=dx, k0=k0, k1=k1, ks=range(16): [(dx(T), T.Sn[:, 15 - k:143 - k], T.XY[:, k0 + k:k1:16], False, False) for k in ks]
-            PE(lambda T, o=opened, c=corr: o(T) + c(T, ks=range(1, 8)), 9 * n, ["Id", "opn0", "opn1", "Sn"] + X_, [T2], T2)
-            PE(lambda T, c=corr: c(T, ks=range(8, 16)), 8 * n, ["Sn"] + X_, [T2], T2)
-            PE(lambda T, dx=dx, dy=dy, c0=c0, c1=c1: [(dx(T), T.Sh[:], T.lt[:, c0:c1], False, False), (dy(T), T.Sh[:], T.lt[:, c0:c1], False, False)], 2 * n, ["Sh"] + tg("lt"), [T2], T2)
-            V(tt(S("Mq", c0, c1), IND("pm", 0, pw, "s16", w0, w1), S("qh", c0, c1), SUB), gv(n), ["pmz", "pm0"] + tg("pm") + tg("s16") + tg("qh"), tg("Mq"))
-            A(act(S("dh", c0, c1), S("Mq", c0, c1), AF.Abs), n, tg("Mq"), tg("dh"))
-            PE(lambda T, B=PB_, d_=d_, n=n: [(T[B][:, 0:n], T.Id[:], d_(T), True, True)], n, ["Id"] + tg("dh"), tg("dps"), PB_)
-            for c in range(2):
-                for h in hs:
-                    Y = "Y%d%d" % (h, c)
-                    PE(lambda T, Y=Y, h=h: [(T[Y][:, j:512:8], T.nI[:], T.dh[:, 64 * h:64 * h + 64], False, j == 7) for j in range(8)], 512, ["nI", "dh%d" % h], [Y], Y)
-                    A(act(S("AY", 1024 * c + 512 * h, 1024 * c + 512 * h + 512), S(Y), AF.Abs), 512, [], [Y, "AY%d%d" % (h, c)], Y)
-            gx, gy = IND("XY", 0, pw, "s16", w0, w1), IND("XY", 2048, 2048 + pw, "s16", w0, w1)
+                Y, o0 = S("Y%d%d" % (h, c)), k0 + 512 * c
+                mm([(Y, S("Id"), S("XY", o0, o0 + 512))], last=False)
+                mm([(Y, S("nI"), S("XY", o0 + 1024, o0 + 1536))], first=False)
+                do(act(S3("A1", 4 * h + 2 * c, 4 * h + 2 * c + 2, 0, 256), Y, AF.Abs))
+            do(scan(S("pm", 1040 * h + 1, 1040 * h + 1025), S("XY", k0, k0 + 1024), S("rp"), MAX, MUL))
+        for h in range(2):
+            c0, c1, w0, w1, k0, s0 = 64 * h, 64 * h + 64, 4 * h, 4 * h + 4, 2048 * h, 128 * h
+            P, Q, TB, Y0, Y1 = "P%d" % h, "P%d" % (1 - h), "T%d" % h, "Y%d0" % h, "Y%d1" % h
+            part = lambda name: S(name, c0, c1)
+            step[1] = h
+            d, s16, e16 = part("d"), S("s16", w0, w1), S("e16", w0, w1)
+            D1 = S(P, 0, 64)
+            mm([(D1, S("Id"), S("frc"))] + [(D1, slide("S4", b), S3("A1", w0, w1, 16 * b, 16 * b + 16)) for b in range(16)])
+            do(scan(S("sc", c1 - 1, c0 - 1 if h else None, -1), S(P, 63, None, -1), S("idc", None, None, -1), MIN, MAX))
+            do(ts(s16, S("sc", c0, c1, 16), thc(0), None, ADD))
+            do(tt(part("Mq"), IND(S("pm", 1040 * h, 1040 * h + 1025), s16), part("qb"), SUB))
+            do(act(d, part("Mq"), AF.Abs))
+            lin(part("lt"), IND(S("LT"), s16))
+            lin(part("d2"), d, 1.0, 2047.5)
+            dx, dy = S(TB, 0, 64), S(TB, 64, 128)
+            onv, ona = list(range(1, 16 - cfg["ax"][h])), list(range(16 - cfg["ax"][h], 16))
+            mm([(S(TB, 0, 128), S("Id"), S("opn"))] + [(dx, slide("Sn", k), S("XY", k0 + k, k0 + 1024, 16)) for k in onv[:7]], last=False)
+            if onv[7:]:
+                mm([(dx, slide("Sn", k), S("XY", k0 + k, k0 + 1024, 16)) for k in onv[7:]], False, False)
+            mm([(dx, S("Sh"), part("lt")), (dy, S("Sh"), part("lt"))], False, False)
+            dp = S(P, 64, 128)
+            mm([(dp, S("Id"), d)])
+            for c, Y in enumerate((Y0, Y1)):
+                mm([(S(Y), S("Id"), S("XY", k0 + 1024 + c, k0 + 2048, 2))], last=False)
+                mm([(S(Y, j, 512, 8), S("nI"), d) for j in range(8)], first=False)
+                do(act(S("AY", 1024 * h + 512 * c, 1024 * h + 512 * c + 512), S(Y), AF.Abs))
+            gx, gy = IND(S("XY", k0, k0 + 1024), s16), IND(S("XY", k0 + 1024, k0 + 2048), s16)
             if cfg["sda"]:
-                GAT(S("sd", s0, s0 + n), gx, n, allx + tg("s16"), tg("sdx"))
-                GAT(S("sd", s0 + n, s0 + 2 * n), gy, n, ally + tg("s16"), tg("sdy"))
-                PE(lambda T, B=PO, s0=s0, n=n, d_=d_: [(T[B][:, 256:256 + 2 * n], T.Id[:], T.sd[:, s0:s0 + 2 * n], True, False), (T[B][:, 256:256 + n], T.nI[:], d_(T), False, False),
-                                                     (T[B][:, 256 + n:256 + 2 * n], T.nI[:], d_(T), False, True)], 4 * n, ["Id", "nI"] + tg("sdx") + tg("sdy") + tg("dh"), tg("sp"), PO)
-                A(act(S("sa", s0, s0 + 2 * n), S(PO, 256, 256 + 2 * n), AF.Abs), 2 * n, tg("sp"), tg("sa"), PO)
+                lin(S("sd", s0, s0 + 64), gx)
+                lin(S("sd", s0 + 64, s0 + 128), gy)
+                mm([(S(Q, 384, 512), S("Id"), S("sd", s0, s0 + 128)), (S(Q, 384, 448), S("nI"), d), (S(Q, 448, 512), S("nI"), d)])
+                do(act(S("sa", s0, s0 + 128), S(Q, 384, 512), AF.Abs))
             else:
-                V(tt(S("sd", s0, s0 + n), gx, S("dh", c0, c1), SUB), gv(n), allx + tg("s16") + tg("dh"), tg("sdx"))
-                V(tt(S("sd", s0 + n, s0 + 2 * n), gy, S("dh", c0, c1), SUB), gv(n), ally + tg("s16") + tg("dh"), tg("sdy"))
-                A(act(S("sa", s0, s0 + 2 * n), S("sd", s0, s0 + 2 * n), AF.Abs), 2 * n, tg("sdx") + tg("sdy"), tg("sa"))
-            PE(lambda T, B=PO, s0=s0, n=n, rl=rl: [(T[B][:, rl:rl + n], T.Bo[:], T.sa[:, s0 + n:s0 + 2 * n], True, False), (T[B][:, rl:rl + n], T.nBo[:], T.sa[:, s0:s0 + n], False, True)], 2 * n,
-               ["Bo", "nBo"] + tg("sa"), tg("lp"), PO)
-            V(ts(S("lost", c0, c1), S(PO, rl, rl + n), 0.0, None, LT), n, tg("lp"), tg("lost"), PO)
-            VA(ts(S("dq", c0, c1), S("dh", c0, c1), -0.25, None, ADD), n, act(S("dq", c0, c1), S("dh", c0, c1), AF.Identity, -0.25), n, tg("dh"), tg("dq"))
-            for k in range(1, 16):
-                V(tt(S("MX", k0 + n * k, k0 + n * k + n), S("XY", k0 + k, k1, 16), S(PB_, 0, n), MAX), n, X_ + tg("dps"), ["MX%d_%d" % (h, k) for h in hs], PB_)
-            PE(lambda T, dx=dx, d_=d_: [(dx(T), T.nBo[:], d_(T), False, False)], n, ["nBo"] + tg("dh"), [T2], T2)
-            for j in range(4):
-                PE(lambda T, dx=dx, k0=k0, j=j, n=n: [(dx(T), T.S2[:, 15 - k:143 - k], T.MX[:, k0 + n * k:k0 + n * k + n], False, False) for k in range(max(1, 4 * j), 4 * j + 4)], 4 * n,
-                   ["S2"] + ["MX%d_%d" % (h, k) for h in hs for k in range(4 * j, 4 * j + 4)], [T2], T2)
-                if j % 2:
-                    c = j // 2
-                    PE(lambda T, dy=dy, o0=1024 * c + 8 * c0, c=c, n=n: [(dy(T), T.S1[:, 15 - (2 * i + c):143 - (2 * i + c)], T.AY[:, o0 + i:o0 + 8 * n:8], False, False) for i in range(8)], 8 * n,
-                       ["S1"] + ["AY%d%d" % (h, c) for h in hs], [T2], T2)
-                if j == 2:
-                    PE(lambda T, dx=dx, dy=dy, c0=c0, c1=c1: [(dx(T), T.nBI[:], T.lost[:, c0:c1], False, False), (dy(T), T.BI[:], T.lost[:, c0:c1], False, False)], 2 * n,
-                       ["nBI", "BI"] + tg("lost"), [T2], T2)
-            fn = ops[-1]["alts"]["p"]
-            o0 = 1024 + 8 * c0
-            ops[-1]["alts"]["p"] = (fn[0], lambda g, T, x, dy=dy, o0=o0, n=n: [g.tensor.matmul(dy(T), T.S1[:, 14 - 2 * i:142 - 2 * i], T.AY[:, o0 + i:o0 + 8 * n:8], False, i == 7) for i in range(8)][-1])
-            PE(lambda T, B=PO, c0=c0, c1=c1: [(T[B][:, 384:448], T.Id[:], T.lost[:, c0:c1], True, False), (T[B][:, 384:448], T.nI[:], T.lt[:, c0:c1], False, True)], 2 * n,
-               ["Id", "nI"] + tg("lost") + tg("lt"), tg("mq"), PO)
-            mm = S("D0", b3 + 1, b4, 3)
-            VA(ts(mm, S(PO, 384, 448), 0.0, None, MAX), n, act(mm, S(PO, 384, 448), AF.Relu), n, tg("mq"), tg("D0"), PO)
-            if cfg["sgn"] & 2:
-                A(act(S("o2", s0, s0 + 2 * n), S(T2, r2, r2 + 2 * n), AF.Sign, S("thc", 3, 4)), 2 * n, ["nth"], [T2] + tg("o2"), T2)
+                do(tt(S("sd", s0, s0 + 64), gx, d, SUB))
+                do(tt(S("sd", s0 + 64, s0 + 128), gy, d, SUB))
+                do(act(S("sa", s0, s0 + 128), S("sd", s0, s0 + 128), AF.Abs))
+            lp, nl = S(Q, 256, 320), part("nl")
+            mm([(lp, S("Bo"), S("sa", s0 + 64, s0 + 128)), (lp, S("nBo"), S("sa", s0, s0 + 64))])
+            do(ts(nl, lp, 0.0, None, GE))
+            mx = lambda k: S("MX", 1024 * h + 64 * k, 1024 * h + 64 * k + 64)
+            for k in onv:
+                do(tt(mx(k), S("XY", k0 + k, k0 + 1024, 16), dp, MAX))
+            if onv:
+                mm([(dx, S("nB%d" % h if any(cfg["ax"]) else "nBo"), d)], False, False)
+            for j in range(0, len(onv), 4):
+                mm([(dx, slide("S2", k), mx(k)) for k in onv[j:j + 4]], False, False)
+            for B, ks in ((P, ona[:6]), (Y0, ona[6:14])):
+                if ks:
+                    w = 64 * len(ks)
+                    mm([m for j, k in enumerate(ks) for m in ((S(B, 128 * (B == P) + 64 * j, 128 * (B == P) + 64 * j + 64), S("Id"), S("XY", k0 + k, k0 + 1024, 16), 1),
+                                                              (S(B, 128 * (B == P) + 64 * j, 128 * (B == P) + 64 * j + 64), S("nI"), d, 2))])
+                    do(act(S("MX", 1024 * h + 64 * ks[0], 1024 * h + 64 * ks[0] + w), S(B, 128 * (B == P), 128 * (B == P) + w), AF.Abs))
+                    mm([(dx, slide("S1", k), mx(k)) for k in ks], False, False)
+            mm([(dx, S("BI"), nl), (dy, S("nBI"), nl)], False, False)
+            for c in range(2):
+                o0 = 1024 * h + 512 * c
+                mm([(dy, slide("S1", 2 * i + c), S("AY", o0 + i, o0 + 512, 8)) for i in range(8)], False, c == 1)
+            for a, sign in ((384, "nBI"), (448, "BI")):
+                b = S(Y0, a, a + 64)
+                mm([(b, S("Id"), S("PBh", 128 + c0, 128 + c1)), (b, S(sign), part("lt")), (b, S(sign), nl)])
+            do(tt(part("Za"), part("PBh"), S(Y0, 384, 448), MAX))
+            do(tt(part("Z"), part("Za"), S(Y0, 448, 512), MIN))
+            lo2, hi2, cnt, et = S(Y0, 0, 64), S(Y0, 64, 128), S(Y1, 0, 64), S(TB, 128, 132)
+            ox, oy = S("o2", s0, s0 + 64), S("o2", s0 + 64, s0 + 128)
+            mm([(S(Y0, 0, 128), S("Id"), S("c2k")), (lo2, S("Id"), part("Z")), (hi2, S("Id"), part("Z"))], last=False)
+            mm([(cnt, S("R0"), nl)], last=False)
+            do(ts(S("o2", s0, s0 + 128), S(TB, 0, 128), thc(2), None, GT), act(S("o2", s0, s0 + 128), S(TB, 0, 128), AF.Relu, thc(3)))
+            mm([(cnt, S("Tri"), ox), (cnt, S("Tri"), oy)], first=False)
+            mm([(lo2, S("nTB"), ox), (lo2, S("nTB"), oy), (hi2, S("TB"), ox), (hi2, S("TB"), oy)], first=False)
+            do(tt(part("Ea"), part("En") if t else part("e0i"), lo2, MAX))
+            do(tt(part("En"), part("Ea"), hi2, MIN))
+            if not last:
+                send("e%d%d" % (t + 1, h), t + 1, part("En"), S("ER%d" % (t + 1), c0, c1), 32768)
+            do(cp(IND(S("G", 512 * h, 512 * h + 512), S("clx", w0, w1)), part("En")))
+            do(act(part("l2"), cnt, AF.Relu, pc(13), -1.0))
+            mm([(et, S("Id"), S("eb", 0, 4))] + [(et, slide("Sw", b), S("l2", c0 + b, c1, 16)) for b in range(16)])
+            do(ts(e16, et, pc(6), None, ADD))
+            do(tt(part("qp"), IND(S("XY", k0, k0 + 2048), e16), part("d2"), ADD))
+            lin(part("qb"), part("qp"), 0.5, -1024.0)
+            rec = IND(S("X", 2048 * h, 2048 * h + 2048), S("clx", 8 + w0, 8 + w1))
+            if cfg["xta"]:
+                lin(part("xo"), rec)
+                mm([(S(Q, 192, 256), S("Id"), part("xo")), (S(Q, 192, 256), S("Id"), d)])
+                lin(part("xt"), S(Q, 192, 256), 1.0, 2047.5)
             else:
-                V(ts(S("o2", s0, s0 + 2 * n), S(T2, r2, r2 + 2 * n), S("thc", 1, 2), None, GT), 2 * n, ["th2"], [T2] + tg("o2"), T2)
-            PE(lambda T, TB=TB, s0=s0, rc=rc, n=n: [(T[TB][:, rc:rc + n], T.Tri[:], T.o2[:, s0:s0 + n], True, False), (T[TB][:, rc:rc + n], T.Tri[:], T.o2[:, s0 + n:s0 + 2 * n], False, True)], 2 * n,
-               ["Tri"] + tg("o2"), [TB], TB)
-            l2 = S("D0", b3 + 2, b4, 3)
-            lv, lb, ls = (pc(16), pc(14), -0.5) if cfg["sgn"] & 2 else (0.5, 1.0, -1.0)
-            VA(ts(l2, S(TB, rc, rc + n), lv, None, LT), n, act(l2, S(TB, rc, rc + n), AF.Relu, lb, ls), n, ["nb", "nb2"], [TB] + tg("D0"), TB)
-
-            def wrap_e(TB=TB, s0=s0, n=n, rs=rs, tg=tg):
-                V(scan(S("sc", s0, s0 + n), S("ms", 0, n), S(TB, rs, rs + n), MUL, MAX), n, ["ms0"], [TB] + tg("sc"), TB)
-            PE(lambda T, TB=TB, c0=c0, c1=c1, l2=l2, rs=rs, n=n: [(T[TB][:, rs:rs + n], T.Id[:], T.ix[:, c0:c1], True, False), (T[TB][:, rs:rs + n], T.BI[:], T.lost[:, c0:c1], False, False),
-                                                                (T[TB][:, rs:rs + n], T.Bo[:], l2(T), False, True)], 3 * n,
-               ["Id", "ix", "BI", "Bo"] + tg("lost") + tg("D0"), [TB], TB)
-            if not cfg["efi"]:
-                wrap_e()
-            for h in hs:
-                H, a0, a3 = str(h), 64 * h, 192 * h
-                if cfg["trv"]:
-                    V(scan(S(nxt, a3, a3 + 192), S("D0", a3, a3 + 192), S(cur, a3, a3 + 192), MUL, ADD), 192, ["D0" + H, cur + H], [nxt + H])
-                else:
-                    V(scan(S(nxt, a3, a3 + 192), S("D0", a3, a3 + 192), S(TB, 0, 192), MUL, ADD), 192, ["D0" + H], [TB, nxt + H], TB)
-                en = S(nxt, a3 + 2, a3 + 192, 3)
-                if not last:
-                    ec = S("Ec", a0, a0 + 64)
-                    VA(cp(ec, en), 64, act(ec, en, AF.Copy), 64, [nxt + H], ["Ec" + H])
-                    if not full:
-                        SEND("e%d%d" % (t + 1, h), t + 1, ec, S("ER%d" % (t + 1), a0, a0 + 64), 32768, ["Ec" + H], ["ER%d%d" % (t + 1, h)])
-                V(cp(IND("G", 512 * h, 512 * h + 512, "clx", 4 * h, 4 * h + 4), en), gs(64), ["clx", nxt + H], ["G" + H])
-            if full and not last:
-                SEND("e%d" % (t + 1), t + 1, S("Ec"), S("ER%d" % (t + 1)), 65536, ["Ec0", "Ec1"], ["ER%d0" % (t + 1), "ER%d1" % (t + 1)])
-            if cfg["efi"]:
-                wrap_e()
-            V(ts(S("e16", w0, w1), S("sc", s0 + 15, s0 + n, 16), pc(10), -2049.0, MUL, ADD), 4, tg("sc") + ["mp"], tg("e16"))
-            V(tt(S("qi", c0, c1), IND("XY", 0, 2048 + pw, "e16", w0, w1), S("dq", c0, c1), ADD), gv(n), xs[0] + xs[1] + ally + tg("e16") + tg("dq"), tg("qi"))
+                do(tt(part("xt"), rec, part("d2"), ADD))
+            lin(part("xn"), part("xt"), 0.5, -1024.0)
+            do(cp(rec, part("xn")))
             if last:
-                V(cp(S("yqb", c0, c1), S("qi", c0, c1)), n, tg("qi"), tg("yq"))
-            else:
-                V(ts(S("qh", c0, c1), S("qi", c0, c1), 0.5, None, MUL), n, tg("qi"), tg("qh"))
-            PE(lambda T, B=PO, c0=c0, c1=c1, d_=d_: [(T[B][:, 448:512], T.Id[:], T.oldh[:, c0:c1], True, False), (T[B][:, 448:512], T.Id[:], d_(T), False, True)], 2 * n,
-               ["Id"] + tg("oldh") + tg("dh"), tg("xp"), PO)
-            V(ts(S("xi", c0, c1), S(PO, 448, 512), -0.25, None, ADD), n, tg("xp"), tg("xi"), PO)
-            for h in hs:
-                H = str(h)
-                V(cp(IND("X", 2048 * h, 2048 * h + 2048, "clx", 8 + 4 * h, 12 + 4 * h), S("xi", 64 * h, 64 * h + 64)), gs(64), ["clx", "xi" + H], ["X" + H])
-                if last:
-                    DMA("s", "ox" + H, ld(lambda T, h=h: T.yx[:, 2048 * h:2048 * h + 2048], S("X", 2048 * h, 2048 * h + 2048)), 524288, ["X" + H], [])
-                    DMA("s", "ol" + H, ld(lambda T, h=h: T.yl[:, 512 * h:512 * h + 512], S("G", 512 * h, 512 * h + 512)), 262144, ["G" + H], [])
-        bias[0] = 0.0
+                dma("s", "ox%d" % h, HBM("yx", 2048 * h, 2048 * h + 2048), S("X", 2048 * h, 2048 * h + 2048), 524288)
+                dma("s", "ol%d" % h, HBM("yl", 512 * h, 512 * h + 512), S("G", 512 * h, 512 * h + 512), 262144)
         if last:
-            DMA("s", "oq", ld(lambda T: T.yq[:], S("yqb")), 32768, ["yq0", "yq1"], [])
+            dma("s", "oq", HBM("yq"), S("qb"), 32768)
         else:
-            PE(lambda T: [(T.P1[:, 128:192], T.o16th[:], T.lost[:, 0:64], True, False), (T.P1[:, 128:192], T.o16th[:], T.lost[:, 64:128], False, True)], 128,
-               ["o16th", "lost0", "lost1"], ["Ap"], "P1")
-            V(lambda g, T, x: g.vector.tensor_reduce(T.Ac[:, 0:1], T.P1[:, 128:192], AxisListType.X, ADD), 64, ["Ap"], ["Ac"], "P1")
+            cn = S("P1", 0, 64)
+            mm([(cn, S("n16th"), S("nl", 0, 64)), (cn, S("n16th"), S("nl", 64, 128))])
+            do(act(S("tmp", 0, 64), cn, AF.Identity, (1024.0 + A0) / 64, 1.0, S("Ac", 0, 1)), also=[S("Ac", 0, 1)])
     return ops
 
 
-def schedule(ops, cfg, fixed=None):
+def place(ops, cfg, rank, edges, fixed):
+    wake, n = cfg["wake"], len(ops)
+    left = [len(e) for e in edges]
+    after = [[] for _ in range(n)]
+    for i, e in enumerate(edges):
+        for d, _lag in e:
+            after[d].append(i)
+    busy = {e: [] for e in "vapgs"}
+    banks = {}
+    start, end, eng = [0.0] * n, [0.0] * n, [None] * n
+    ready = [(rank[i], i) for i in range(n) if not left[i]]
+    while ready:
+        k = ready.index(min(ready))
+        i = ready[k][1]
+        ready[k] = ready[-1]
+        ready.pop()
+        t0 = max([end[d] + lag for d, lag in edges[i]] or [0.0])
+        best = (t0, t0, "r")
+        if ops[i]["alts"]:
+            best = None
+            for e in ([fixed[i]] if fixed else ops[i]["alts"]):
+                c, t, moved = ops[i]["alts"][e][0], t0, True
+                while moved:
+                    moved = False
+                    line = busy[e]
+                    lo, hi = 0, len(line)
+                    while lo < hi:
+                        mid = (lo + hi) // 2
+                        if line[mid][1] <= t:
+                            lo = mid + 1
+                        else:
+                            hi = mid
+                    while lo < len(line) and line[lo][0] < t + c:
+                        t = line[lo][1]
+                        lo += 1
+                    for b in ops[i]["banks"]:
+                        for s2, e2, who in banks.get(b, ()):
+                            if who != e and s2 < t + c + wake and t < e2 + wake:
+                                t, moved = e2 + wake, True
+                key = t + c + (cfg["vpen"] if e == "v" else 0.0)
+                if best is None or key < best[3]:
+                    best = (t, t + c, e, key, lo)
+            busy[best[2]].insert(best[4], (best[0], best[1]))
+            for b in ops[i]["banks"]:
+                banks.setdefault(b, []).append((best[0], best[1], best[2]))
+        start[i], end[i], eng[i] = best[:3]
+        for s in after[i]:
+            left[s] -= 1
+            if not left[s]:
+                ready.append((rank[s], s))
+    return start, end, eng
+
+
+def schedule(ops, cfg):
+    n, wake = len(ops), cfg["wake"]
+    lag = lambda d, i: 0.0 if "p" in ops[d]["alts"] and "p" in ops[i]["alts"] else ops[d]["lat"] + (wake if ops[i]["alts"] else 0.0)
+    fwd = [[(d, lag(d, i)) for d in o["deps"]] for i, o in enumerate(ops)]
+    bwd = [[] for _ in range(n)]
+    for i in range(n):
+        for d, l in fwd[i]:
+            bwd[d].append((i, l))
+    seed = [cfg["seed"] * 7919 + 12345]
+
+    def rnd():
+        seed[0] = (seed[0] * 1103515245 + 12345) % 2147483648
+        return seed[0] / 2147483648.0
+    tail = [0.0] * n
+    for i in range(n - 1, -1, -1):
+        tail[i] = min([a[0] for a in ops[i]["alts"].values()] or [0.0]) + max([tail[s] + l for s, l in bwd[i]] or [ops[i]["lat"]])
+    rank, best = [cfg["stag"] * o["half"] - x for x, o in zip(tail, ops)], None
+    last = [bwd[i] or [(n, ops[i]["lat"])] for i in range(n)] + [[]]
+    for _ in range(cfg["passes"]):
+        start, end, eng = place(ops, cfg, [r + cfg["noise"] * rnd() for r in rank], fwd, None)
+        total = max(end[i] + ops[i]["lat"] for i in range(n))
+        if best is None or total < best[0]:
+            best = (total, start, end, eng)
+        _s, back, _e = place(ops + [{"alts": {}, "banks": []}], cfg, [-x for x in end] + [-1e18], last, eng + ["r"])
+        rank = [-x for x in back[:n]]
+    total, start, end, eng = best
+    order = {e: sorted((i for i in range(n) if eng[i] == e), key=lambda i: (start[i], end[i], i)) for e in "vapgs"}
+    more, seen = [set() for _ in range(n)], {}
+    for i in sorted(range(n), key=lambda i: (start[i], i)):
+        for b in ops[i]["banks"]:
+            more[i].update(j for e, j in seen.get(b, {}).items() if e != eng[i])
+            seen.setdefault(b, {})[eng[i]] = i
+    return order, eng, more, total, [end[i] + ops[i]["lat"] for i in range(n)]
+
+
+def schedule_old(ops, cfg):
     n, wake = len(ops), cfg["wake"]
     succ = [[] for _ in range(n)]
     for i, o in enumerate(ops):
@@ -528,8 +536,8 @@ def schedule(ops, cfg, fixed=None):
     for i in range(n - 1, -1, -1):
         c = min([a[0] for a in ops[i]["alts"].values()] or [0.0]) + ops[i]["lat"]
         prio[i] = c + wake + max([prio[s] for s in succ[i]] or [0.0])
-    prio = [p + cfg["noise"] * rnd() + o["bias"] + cfg["B"].get(o["key"], 0.0) for p, o in zip(prio, ops)]
-    engs = [[cfg["E"][o["key"]]] if len(o["alts"]) == 2 and o["key"] in cfg["E"] else list(o["alts"]) for o in ops]
+    prio = [p + cfg["noise"] * rnd() for p in prio]
+    engs = [list(o["alts"]) for o in ops]
     rdy = [0.0] * n
     left = [len(o["deps"]) for o in ops]
     fin, eng = [0.0] * n, [None] * n
@@ -554,8 +562,7 @@ def schedule(ops, cfg, fixed=None):
 
     def start(i, e):
         t = max(free[e], rdy[i])
-        b = ops[i]["bank"]
-        if b:
+        for b in ops[i]["banks"]:
             for e2, j in banks.get(b, {}).items():
                 if e2 != e:
                     t = max(t, fin[j] + wake)
@@ -583,8 +590,7 @@ def schedule(ops, cfg, fixed=None):
         fin[i] = t + cost + ops[i]["lat"]
         eng[i] = e
         order[e].append(i)
-        b = ops[i]["bank"]
-        if b:
+        for b in ops[i]["banks"]:
             more[i].update(j for e2, j in banks.get(b, {}).items() if e2 != e)
             banks.setdefault(b, {})[e] = i
         done(i)
@@ -649,6 +655,8 @@ def plan(cfg):
 
 
 _PLAN = plan(CFG)
+_ALL = dict(SCRATCH)
+SCRATCH = {_n: _v for _n, _v in _ALL.items() if _n in {_o["name"] for _o in _PLAN[0]} | {"Ac"}}
 SEMAPHORES = sorted({s for s, _v in _PLAN[3].values()}) + ["hg%d" % _t for _t in range(1, STEPS)] + ["kg%d" % _t for _t in range(1, STEPS)]
 
 

from concourse.mybir import dt, AluOpType, AxisListType, ActivationFunctionType

N, STEPS = 8, 5
F32, BF, H16, I32, U16 = "float32", "bfloat16", "float16", "int32", "uint16"
ADD, SUB, MUL, MAX, MIN = AluOpType.add, AluOpType.subtract, AluOpType.mult, AluOpType.max, AluOpType.min
AND, SHR = AluOpType.bitwise_and, AluOpType.arith_shift_right
EQ, NE, GT, GE = AluOpType.is_equal, AluOpType.not_equal, AluOpType.is_gt, AluOpType.is_ge
AF = ActivationFunctionType
BIG = 4096.0

COLUMNS = {
    BF: {"X": 4096, "qb": 128, "w0": 8, "XY": 4096, "pm": 2080, "MX": 2048, "AY": 2048, "hm": 128, "hq": 128, "lor": 128, "lt": 128,
         "Mq": 128, "d": 128, "sd": 256, "sa": 256, "nl": 128, "o2": 256, "l2": 128, "xn": 128, "ab": 512, "mn": 512, "junk": 64,
         "colg": 128, "colb": 1024, "col": 144, "pos": 256, "poi": 256, "Bo": 128, "nBo": 128, "Bhi": 128, "Id": 128, "nI": 128, "I8k": 128,
         "BI": 128, "nBI": 128, "Sh": 128, "tmp": 128, "Tri": 128, "TB": 128, "nTB": 128, "R0": 128, "S1": 144, "S2": 144, "Sn": 144,
         "S4": 144, "Sw": 144, "dl": 16, "LT": 1024, "rp": 1024, "frc": 64, "eb": 8, "n16th": 128, "c2k": 128, "opn": 128, "cu": 16, "xo": 128, "colm": 128, "nB0": 128, "nB1": 128},
    H16: {"qp": 128, "cand": 256, "PBh": 256, "Za": 128, "Z": 128, "xt": 128, "W1": 144, "W2": 128, "th16": 8},
    F32: {"G": 1024, "v": 8, "sq": 8, "Ac": 4, "sc": 128, "d2": 128, "Ea": 128, "En": 128, "clR": 128, "nn": 8, "ow": 8, "oo": 8,
          "pc": 20, "thc": 8, "idx": 64, "idc": 64, "aq": 8, "spare": 8, "iot": 512},
    I32: {"Gi": 1024, "Dm": 4160, "Dd": 256, "e0i": 128, "thi": 4, "hh": 8, "nf": 8, "nlh": 16, "ui": 8, "cx0": 16, "cx1": 16,
          "n32": 8, "pI": 4, "pb": 4, "stw": 16},
    U16: {"n16": 16, "nq": 16, "c16": 16, "PB": 256, "Bq": 128, "s16": 8, "e16": 8, "clx": 16, "o16": 8},
}
for _t in range(1, STEPS):
    COLUMNS[F32].update({"GR%d" % _t: 1024, "ER%d" % _t: 128})
    COLUMNS[I32]["DR%d" % _t] = 256
    COLUMNS[U16]["CR%d" % _t] = 8
SCRATCH = {_n: ("sbuf", [128, _c], _d) for _d in COLUMNS for _n, _c in COLUMNS[_d].items()}
SCRATCH["A1"] = ("sbuf", [128, 8, 256], BF)
for _b in ("Y00", "Y01", "Y10", "Y11", "T0", "T1", "P0", "P1"):
    SCRATCH[_b] = ("psum", [128, 512], F32)

CFG = {"nu": 2, "gch": 512, "sda": 0, "wake": 240.0, "fix": 10.0, "gat": 1.56, "sca": 3.8, "pe": 0.5, "bw": 80.0, "rlat": 2000.0,
       "look": 200.0, "vpen": 300.0, "slack": 150.0, "noise": 0.0, "seed": 0, "pin": {}, "ax": (0, 0), "xta": 0, "passes": 8, "stag": 2000.0}


def S(name, a=None, b=None, c=None):
    r = range(SCRATCH[name][1][1])[a:b:c]
    return ("s", name, min(r[0], r[-1]), max(r[0], r[-1]) + 1, len(r), slice(a, b, c))


def S3(name, j0, j1, a, b):
    w = SCRATCH[name][1][2]
    return ("3", name, j0 * w + a, (j1 - 1) * w + b, (j1 - j0) * (b - a), (slice(j0, j1), slice(a, b)))


def LEAD(name, a, b):
    return ("l", name, a, b, b - a, slice(a, b))


def HBM(name, a=None, b=None):
    return ("h", name, 0, 0, 0, slice(a, b))


def IND(win, off):
    return ("i", win, off)


def ap(T, a):
    if not isinstance(a, tuple):
        return a
    if a[0] == "i":
        return ap(T, a[1]).indirect(ap(T, a[2]))
    if a[0] == "3":
        return T[a[1]][:, a[5][0], a[5][1]]
    if a[0] == "l":
        return T[a[1]][0:128:16, a[5]]
    return T[a[1]][:, a[5]]


def build_ops(cfg):
    ops, writes, reads, step = [], {}, {}, [-1, 0]
    fix, pe = cfg["fix"], cfg["pe"]
    psum = lambda a: SCRATCH[a[1]][0] == "psum"
    narrow = lambda a: SCRATCH[a[1]][2] in (BF, H16, U16)

    def add(alts, R, W, kind="c", lat=0.0, sem=None, extra=()):
        i, deps = len(ops), set(extra)
        for a in R + W:
            deps.update(j for lo, hi, j in writes.get(a[1], ()) if lo < a[3] and a[2] < hi)
        for a in W:
            deps.update(j for lo, hi, j in reads.get(a[1], ()) if lo < a[3] and a[2] < hi)
        for a in W:
            for book in (writes, reads):
                book[a[1]] = [e for e in book.get(a[1], ()) if not (a[2] <= e[0] and e[1] <= a[3])]
            writes[a[1]].append((a[2], a[3], i))
        for a in R:
            reads.setdefault(a[1], []).append((a[2], a[3], i))
        banks = sorted({a[1] for a in R + W if a[1] in SCRATCH and psum(a)})
        name = (W[0][1] if W else sem) or "-"
        if name in cfg["pin"] and cfg["pin"][name] in alts:
            alts = {cfg["pin"][name]: alts[cfg["pin"][name]]}
        ops.append({"alts": alts, "deps": deps, "banks": banks, "kind": kind, "lat": lat, "sem": sem, "name": name, "step": step[0],
                    "half": step[1]})
        return i

    def sides(out, ins):
        R, W = [], [out[1] if out[0] == "i" else out]
        for a in ins:
            if isinstance(a, tuple):
                R += [a[1], a[2]] if a[0] == "i" else [a]
        return R + ([out[2]] if out[0] == "i" else []), W

    def cost(out, first, rate):
        if out[0] == "i":
            return 60.0 + cfg["sca"] * first[4]
        if first[0] == "i":
            return 60.0 + cfg["gat"] * out[4]
        return fix + max(64.0, rate * first[4])
    half = lambda *a: 0.5 if all(narrow(x) for x in a if x[0] != "i") else 1.0
    ts = lambda o, i, a, b, p, q=None: ("v", cost(o, i, half(o, i)), o, [i, a, b],
                                        lambda g, T, x: g.vector.tensor_scalar(ap(T, o), ap(T, i), ap(T, a), ap(T, b), *([p] if q is None else [p, q])))
    cp = lambda o, i: ("v", cost(o, i, half(o, i)), o, [i], lambda g, T, x: g.vector.tensor_copy(ap(T, o), ap(T, i)))
    tt = lambda o, i, j, p: ("v", cost(o, i, 1.0 if i[0] == "i" or psum(i) or psum(j) else 2.0), o, [i, j],
                             lambda g, T, x: g.vector.tensor_tensor(ap(T, o), ap(T, i), ap(T, j), p))
    scan = lambda o, i, j, p, q: ("v", cost(o, i, half(o, i, j)), o, [i, j],
                                  lambda g, T, x: g.vector.tensor_tensor_scan(ap(T, o), ap(T, i), ap(T, j), 0.0, p, q))
    mset = lambda o, c: ("v", cost(o, o, half(o)), o, [], lambda g, T, x: g.vector.memset(ap(T, o), c))

    def act(o, i, f, b=0.0, s=1.0, acc=None):
        def run(g, T, x):
            more = {} if b == 0.0 else {"bias": ap(T, b)}
            if acc:
                more["accum_out"] = ap(T, acc)
            return g.scalar.activation(ap(T, o), ap(T, i), f, scale=ap(T, s), **more)
        return ("a", cost(o, i, 1.0) + (15.0 if i[0] == "i" else 0.0), o, [i, b, s], run)

    def do(*forms, also=()):
        R, W = [], []
        for f in forms:
            r, W = sides(f[2], f[3])
            R += r
        return add({f[0]: (f[1], f[4]) for f in forms}, R, W + list(also))

    def lin(o, i, s=1.0, b=0.0):
        fv = cp(o, i) if s == 1.0 and b == 0.0 else (ts(o, i, s, None, MUL) if b == 0.0 else ts(o, i, s, b, MUL, ADD))
        return do(fv, act(o, i, AF.Copy if b == 0.0 and not isinstance(s, tuple) else AF.Identity, b, s))

    def mm(calls, first=True, last=True):
        def run(g, T, x):
            for k, c in enumerate(calls):
                ins = g.tensor.matmul(ap(T, c[0]), ap(T, c[1]), ap(T, c[2]), c[3] == 1 if c[3:] else first and k == 0, c[3] == 2 if c[3:] else last and k == len(calls) - 1)
            return ins
        outs = [c[0] for c in calls]
        R = [a for c in calls for a in c[1:3]]
        bank = outs[0][1]
        turn = [("t", "turn" + bank, 0, 1)] if bank[0] in "YT" else []
        cyc = sum(max(64.0, c[2][4]) for c in calls) * pe
        if first or last:
            return add({"p": (cyc, run)}, R, outs + turn)
        i = add({"p": (cyc, run)}, R + outs + turn, [])
        ops[i]["name"] = bank
        return i

    def iota(o, pat, cm=0):
        loose = {} if SCRATCH[o[1]][2] == I32 else {"allow_small_or_imprecise_dtypes": True}
        return add({"g": (150.0 + 2.0 * o[4], lambda g, T, x: g.iota(ap(T, o), pat, 0, cm, **loose))}, [], [o])

    def dma(q, name, o, i, nbytes):
        return add({q: (60.0, lambda g, T, x: x["q"].dma_start(ap(T, o), ap(T, i)))}, [i] if i[0] != "h" else [], [o] if o[0] != "h" else [],
                   kind="d", lat=2000.0 + nbytes / 200.0, sem=name)

    def send(name, to, src, dst, nbytes, extra=()):
        via = name[0] == "g"

        def run(g, T, x):
            rid, pid, mask = x["helper"] if via else x["to"][to]
            return g.remote_dma(ap(T, dst), ap(T, src), T.sem[("h" if via else "r") + name], T.sem["l" + name], pid, rid, mask)
        s = add({"g": (400.0, run)}, [src], [], kind="s", lat=cfg["rlat"] - 500.0 + nbytes / (150.0 if via else cfg["bw"]), sem="l" + name, extra=extra)
        add({}, [], [dst], kind="r", lat=cfg["rlat"] + 1000.0 + nbytes / cfg["bw"] if via else 500.0, sem="r" + name, extra=(s,))
        ops[s]["move"] = (to, src, dst)
        return s
    slide = lambda name, k: S(name, 15 - k, 143 - k)

    dma("s", "dq", S("qb"), HBM("qd"), 32768)
    dma("a", "dw", S("w0", 0, 1), HBM("wt"), 256)
    dma("s", "dd0", S("Dd"), HBM("dr"), 160000)
    dma("s", "dg", S("Gi"), HBM("lg"), 690000)
    dma("s", "dx", S("X"), HBM("xr"), 1700000)
    do(mset(S("thi"), 0))
    dma("a", "dt", LEAD("thi", 0, 2), HBM("th"), 64)
    dma("s", "de", S("e0i"), HBM("e0"), 1800000)
    dma("s", "dm", LEAD("Dm", 0, 4096), HBM("dr"), 1900000)

    pc = lambda j: S("pc", j, j + 1)
    iota(S("pI", 0, 1), [[1, 1]], 1)
    iota(S("col"), [[1, 144]])
    iota(S("colg"), [[1, 8], [0, 16]])
    iota(S("colb"), [[0, 64], [1, 16]])
    iota(S("aq"), [[0, 2], [1, 4]])
    iota(S("idx"), [[256, 4], [1, 16]])
    iota(S("iot"), [[1, 512]])
    iota(S("ab", 0, 256), [[-16, 4], [1, 64]])
    do(ts(S("pb", 0, 1), S("pI", 0, 1), 15, None, AND))
    do(ts(S("pb", 1, 2), S("pI", 0, 1), 4, None, SHR))
    do(cp(S("pc", 0, 2), S("pb", 0, 2)))
    do(cp(pc(2), S("pI", 0, 1)))
    for j, src, s, b in ((3, 2, 1, 1), (4, 0, 8, 0), (5, 0, 32, 0), (6, 0, 16, 0), (7, 1, 16, 15), (8, 0, 1, 4096), (9, 0, 2.0 ** 21, 0)):
        lin(pc(j), pc(src), float(s), float(b))
    do(ts(pc(10), pc(0), 0.0, None, EQ))
    for j, s, b in ((11, -2048, 0), (12, 7, 1), (13, 127, 1), (14, 128, 0), (15, 1.0e6, 2048)):
        lin(pc(j), pc(10), float(s), float(b))
    do(ts(S("S1"), S("col"), pc(7), None, EQ))
    do(ts(S("Bo"), S("colg"), pc(1), None, EQ))
    do(ts(S("Id"), S("col", 0, 128), pc(2), None, EQ))
    do(ts(S("W1"), S("S1"), S("w0", 0, 1), 2.0 ** -13, MUL, MUL))
    do(ts(S("W2"), S("Bo"), S("w0", 0, 1), 2.0 ** -13, MUL, MUL))
    for o, i, s in (("nBo", "Bo", -1.0), ("Bhi", "Bo", pc(9)), ("nI", "Id", -1.0), ("I8k", "Id", 8192.0), ("BI", "Id", BIG), ("nBI", "Id", -BIG),
                    ("R0", "Id", pc(14)), ("S2", "S1", 2.0), ("Sn", "S1", -1.0), ("S4", "S1", -BIG), ("Sw", "S1", pc(12))):
        lin(S(o), S(i), s)
    do(ts(S("Sh"), S("col", 0, 128), pc(3), -BIG, EQ, MUL))
    do(ts(S("tmp"), S("col", 0, 128), pc(2), None, GE))
    do(tt(S("Tri"), S("tmp"), S("Bo"), MUL))
    for h in range(2 if any(cfg["ax"]) else 0):
        do(ts(S("colm"), S("colb", 0, 128), 15.5 - cfg["ax"][h], -1.0, AluOpType.is_lt, MUL))
        do(tt(S("nB%d" % h), S("colm"), S("Bo"), MUL))
    lin(S("TB"), S("Tri"), BIG)
    lin(S("nTB"), S("Tri"), -BIG)
    do(ts(S("dl"), S("col", 0, 16), pc(0), None, EQ))
    do(ts(S("LT"), S("colb"), pc(0), None, GT))
    do(ts(S("rp"), S("colb"), 15.0, None, NE))
    do(ts(S("frc"), S("colb", 0, 64), 15.0, -2.0 ** 25, EQ, MUL))
    do(ts(S("poi"), S("ab", 0, 256), pc(0), 8192.0, GE, MUL))
    lin(S("eb"), S("aq"), 256.0)
    do(ts(S("spare"), S("aq"), 16.0, pc(8), MUL, ADD))
    do(ts(S("stw", 0, 8), S("aq"), 128.0, pc(4), MUL, ADD))
    do(ts(S("stw", 8, 16), S("aq"), 512.0, pc(5), MUL, ADD))
    for o, c in ((S("cu", 0, 8), -2048.0), (S("cu", 8, 16), 592.0 / 4096), (S("n16th"), -0.0625), (S("c2k"), 2048.0), (S("opn", 0, 64), -BIG),
                 (S("opn", 64, 128), 0.0), (S("pm", 0, 2080, 1040), 0.0)):
        do(mset(o, c))
    thc = lambda j: S("thc", j, j + 1)
    do(ts(S("th16", 0, 2), S("thi", 0, 2), pc(11), None, ADD))
    mm([(S("P0", 256, 258), S("Bo"), S("th16", 0, 2))])
    do(ts(thc(0), S("P0", 256, 257), BIG, 2048.0 * BIG + 2048.0, MUL, ADD))
    do(ts(thc(1), thc(0), -1.0, pc(6), MUL, ADD))
    do(ts(thc(2), S("P0", 257, 258), pc(15), None, ADD))
    do(ts(thc(3), thc(2), -1.0, None, MUL))
    do(ts(S("idc"), S("idx"), thc(1), None, ADD))
    do(ts(S("qp"), S("qb"), 2.0, 2048.0, MUL, ADD))
    for j in range(4):
        do(cp(S("G", 256 * j, 256 * j + 256), S("Gi", 256 * j, 256 * j + 256)))

    A0 = -10952.0 - 13.0 / 32
    gch = cfg["gch"]
    for t in range(STEPS):
        last = t == STEPS - 1
        step[0] = t
        GR, DR, G1 = "GR%d" % t, "DR%d" % t, "GR%d" % (t + 1)
        GO = S("G") if t else S("Gi")
        bulk = lambda extra: [send("%s%d" % (k, t + 1), t + 1, S("G", a, a + 512), S(G1, a, a + 512), 262144, extra) for k, a in (("f", 0), ("g", 512))]
        if 1 <= t < STEPS - 1:
            bulk(())
        if t:
            for h in range(2):
                do(cp(IND(S(GR, 512 * h, 512 * h + 512), S("CR%d" % t, 4 * h, 4 * h + 4)), S("ER%d" % t, 64 * h, 64 * h + 64)))
        for c0, n in ([(0, 128)] if t == 0 or cfg["nu"] == 1 else [(0, 64), (64, 64)]):
            c1, w0, nw = c0 + n, c0 // 16, n // 16
            step[1] = c0 // 64
            w1, n0, Y = w0 + nw, 2 * w0, "P%d" % (c0 // 64)
            y, tile = S(Y, 128, 128 + nw), lambda name: S(name, w0, w1)
            mm([(y, S("W2"), S("cu", 0, nw)), (y, S("Id"), S("cu", 8, 8 + nw))] + [(y, slide("W1", b), S("qp", c0 + b, c1, 16)) for b in range(16)])
            do(ts(tile("hh"), y, -2639.5 / 4096, None, ADD))
            do(tt(tile("v"), y, tile("hh"), SUB))
            do(tt(tile("sq"), tile("v"), tile("v"), MUL), act(tile("sq"), tile("v"), AF.Square))
            do(ts(tile("nf"), tile("sq"), 2.0 ** 19, S("Ac", 0, 1) if t else A0, MUL, ADD))
            do(ts(S("nlh", n0, n0 + nw), tile("nf"), 255, None, AND))
            do(ts(S("nlh", n0 + nw, n0 + 2 * nw), tile("nf"), 8, 15, SHR, AND))
            do(cp(S("n16", n0, n0 + 2 * nw), S("nlh", n0, n0 + 2 * nw)))
            lo, hi = S("n16", n0, n0 + nw), S("n16", n0 + nw, n0 + 2 * nw)
            if t == 0:
                send("nb", "b", S("n16"), S("nq"), 4096)
            lin(S("hm", c0, c1), IND(S("dl"), hi))
            s0 = 2 * c0
            do(tt(S("cand", s0, s0 + n), IND(S("Dd"), lo), S("hm", c0, c1), MUL))
            if t:
                do(tt(S("cand", s0 + n, s0 + 2 * n), IND(S(DR), lo), S("hm", c0, c1), MUL))
                parts = [(0, 2 * n)]
            else:
                lin(S("lt"), IND(S("dl"), S("nq", 8, 16)))
                do(tt(S("cand", n, 2 * n), IND(S("Dd"), S("nq", 0, 8)), S("lt"), MUL))
                parts = [(0, n), (n, 2 * n)]
            for a, b in parts:
                ct = S(Y, 144 + a // 16, 144 + b // 16)
                mm([(ct, slide("S1", k), S("cand", s0 + a + k, s0 + b, 16)) for k in range(16)])
                do(cp(S("c16", n0 + a // 16, n0 + b // 16), ct))
            if not last:
                lin(S("lor", c0, c1), IND(S("iot", 0, 256), lo))
            do(cp(S("PB", c0, c1), IND(GO, S("c16", n0, n0 + nw))))
            if t:
                do(cp(S("PB", 128 + c0, 128 + c1), IND(S(GR), S("c16", n0 + nw, n0 + 2 * nw))))
            else:
                do(cp(S("Bq"), IND(GO, S("c16", 8, 16))))
                bulk((send("b0", 0, S("Bq"), S("PB", 128, 256), 32768),))
        for z in range(2):
            do(ts(S("PBh", 128 * z, 128 * z + 128), S("PB", 128 * z, 128 * z + 128), -2048.0, None, ADD))
        for z in range(2):
            for h in range(2):
                step[1] = h
                for j in range(0, 1024, gch):
                    o0, f0 = 2048 * h + 1024 * z + j, 128 * z + 64 * h + j // 16
                    lin(S("XY", o0, o0 + gch), IND(S("X"), S("PB", f0, f0 + gch // 16)))
        do(ts(S("ui"), S("v"), 4096.0, -592.0, MUL, ADD))
        do(ts(S("cx0", 0, 8), S("ui"), 7, None, AND))
        do(ts(S("cx0", 8, 16), S("ui"), 31, None, AND))
        do(tt(S("cx1"), S("cx0"), S("stw"), ADD))
        do(cp(S("clx"), S("cx1")))
        if not last:
            send("c%d" % (t + 1), t + 1, S("clx", 0, 8), S("CR%d" % (t + 1)), 2048)
            do(ts(S("n32"), S("nf"), 4095, None, AND))
            do(ts(S("nn"), S("n32"), -8192.0, None, MUL))
            for h in range(2):
                c0, c1 = 64 * h, 64 * h + 64
                lin(S("clR", c0, c1), IND(S("iot"), S("clx", 4 * h, 4 * h + 4)), 1.0, 512.0 * h)
                rep = S("P%d" % h, 320, 384)
                mm([(rep, S("Bhi"), S("hm", c0, c1)), (rep, S("I8k"), S("lor", c0, c1))])
                for a in range(4 * h, 4 * h + 4):
                    do(act(S("ab", 64 * a, 64 * a + 64), rep, AF.Abs, S("nn", a, a + 1)))
                back = lambda name: S(name, 256 * h + 255, 256 * h - 1 if h else None, -1)
                do(scan(back("mn"), back("ab"), S("poi", None, None, -1), MIN, MAX))
            do(tt(S("ow"), S("spare"), S("mn", 0, 512, 64), SUB))
            do(tt(S("ow"), S("ow"), S("n32"), MAX))
            do(cp(S("o16"), S("ow")))
            for h in (1, 0):
                do(cp(IND(S("Dm"), S("o16", 4 * h, 4 * h + 4)), S("clR", 64 * h, 64 * h + 64)))
            dma("s", "dd%d" % (t + 1), S("Dd"), LEAD("Dm", 0, 4096), 131072)
            send("d%d" % (t + 1), t + 1, S("Dd"), S("DR%d" % (t + 1)), 131072)
        for h in range(2):
            k0 = 2048 * h
            step[1] = h
            for c in range(2):
                Y, o0 = S("Y%d%d" % (h, c)), k0 + 512 * c
                mm([(Y, S("Id"), S("XY", o0, o0 + 512))], last=False)
                mm([(Y, S("nI"), S("XY", o0 + 1024, o0 + 1536))], first=False)
                do(act(S3("A1", 4 * h + 2 * c, 4 * h + 2 * c + 2, 0, 256), Y, AF.Abs))
            do(scan(S("pm", 1040 * h + 1, 1040 * h + 1025), S("XY", k0, k0 + 1024), S("rp"), MAX, MUL))
        for h in range(2):
            c0, c1, w0, w1, k0, s0 = 64 * h, 64 * h + 64, 4 * h, 4 * h + 4, 2048 * h, 128 * h
            P, Q, TB, Y0, Y1 = "P%d" % h, "P%d" % (1 - h), "T%d" % h, "Y%d0" % h, "Y%d1" % h
            part = lambda name: S(name, c0, c1)
            step[1] = h
            d, s16, e16 = part("d"), S("s16", w0, w1), S("e16", w0, w1)
            D1 = S(P, 0, 64)
            mm([(D1, S("Id"), S("frc"))] + [(D1, slide("S4", b), S3("A1", w0, w1, 16 * b, 16 * b + 16)) for b in range(16)])
            do(scan(S("sc", c1 - 1, c0 - 1 if h else None, -1), S(P, 63, None, -1), S("idc", None, None, -1), MIN, MAX))
            do(ts(s16, S("sc", c0, c1, 16), thc(0), None, ADD))
            do(tt(part("Mq"), IND(S("pm", 1040 * h, 1040 * h + 1025), s16), part("qb"), SUB))
            do(act(d, part("Mq"), AF.Abs))
            lin(part("lt"), IND(S("LT"), s16))
            lin(part("d2"), d, 1.0, 2047.5)
            dx, dy = S(TB, 0, 64), S(TB, 64, 128)
            onv, ona = list(range(1, 16 - cfg["ax"][h])), list(range(16 - cfg["ax"][h], 16))
            mm([(S(TB, 0, 128), S("Id"), S("opn"))] + [(dx, slide("Sn", k), S("XY", k0 + k, k0 + 1024, 16)) for k in onv[:7]], last=False)
            if onv[7:]:
                mm([(dx, slide("Sn", k), S("XY", k0 + k, k0 + 1024, 16)) for k in onv[7:]], False, False)
            mm([(dx, S("Sh"), part("lt")), (dy, S("Sh"), part("lt"))], False, False)
            dp = S(P, 64, 128)
            mm([(dp, S("Id"), d)])
            for c, Y in enumerate((Y0, Y1)):
                mm([(S(Y), S("Id"), S("XY", k0 + 1024 + c, k0 + 2048, 2))], last=False)
                mm([(S(Y, j, 512, 8), S("nI"), d) for j in range(8)], first=False)
                do(act(S("AY", 1024 * h + 512 * c, 1024 * h + 512 * c + 512), S(Y), AF.Abs))
            gx, gy = IND(S("XY", k0, k0 + 1024), s16), IND(S("XY", k0 + 1024, k0 + 2048), s16)
            if cfg["sda"]:
                lin(S("sd", s0, s0 + 64), gx)
                lin(S("sd", s0 + 64, s0 + 128), gy)
                mm([(S(Q, 384, 512), S("Id"), S("sd", s0, s0 + 128)), (S(Q, 384, 448), S("nI"), d), (S(Q, 448, 512), S("nI"), d)])
                do(act(S("sa", s0, s0 + 128), S(Q, 384, 512), AF.Abs))
            else:
                do(tt(S("sd", s0, s0 + 64), gx, d, SUB))
                do(tt(S("sd", s0 + 64, s0 + 128), gy, d, SUB))
                do(act(S("sa", s0, s0 + 128), S("sd", s0, s0 + 128), AF.Abs))
            lp, nl = S(Q, 256, 320), part("nl")
            mm([(lp, S("Bo"), S("sa", s0 + 64, s0 + 128)), (lp, S("nBo"), S("sa", s0, s0 + 64))])
            do(ts(nl, lp, 0.0, None, GE))
            mx = lambda k: S("MX", 1024 * h + 64 * k, 1024 * h + 64 * k + 64)
            for k in onv:
                do(tt(mx(k), S("XY", k0 + k, k0 + 1024, 16), dp, MAX))
            if onv:
                mm([(dx, S("nB%d" % h if any(cfg["ax"]) else "nBo"), d)], False, False)
            for j in range(0, len(onv), 4):
                mm([(dx, slide("S2", k), mx(k)) for k in onv[j:j + 4]], False, False)
            for B, ks in ((P, ona[:6]), (Y0, ona[6:14])):
                if ks:
                    w = 64 * len(ks)
                    mm([m for j, k in enumerate(ks) for m in ((S(B, 128 * (B == P) + 64 * j, 128 * (B == P) + 64 * j + 64), S("Id"), S("XY", k0 + k, k0 + 1024, 16), 1),
                                                              (S(B, 128 * (B == P) + 64 * j, 128 * (B == P) + 64 * j + 64), S("nI"), d, 2))])
                    do(act(S("MX", 1024 * h + 64 * ks[0], 1024 * h + 64 * ks[0] + w), S(B, 128 * (B == P), 128 * (B == P) + w), AF.Abs))
                    mm([(dx, slide("S1", k), mx(k)) for k in ks], False, False)
            mm([(dx, S("BI"), nl), (dy, S("nBI"), nl)], False, False)
            for c in range(2):
                o0 = 1024 * h + 512 * c
                mm([(dy, slide("S1", 2 * i + c), S("AY", o0 + i, o0 + 512, 8)) for i in range(8)], False, c == 1)
            for a, sign in ((384, "nBI"), (448, "BI")):
                b = S(Y0, a, a + 64)
                mm([(b, S("Id"), S("PBh", 128 + c0, 128 + c1)), (b, S(sign), part("lt")), (b, S(sign), nl)])
            do(tt(part("Za"), part("PBh"), S(Y0, 384, 448), MAX))
            do(tt(part("Z"), part("Za"), S(Y0, 448, 512), MIN))
            lo2, hi2, cnt, et = S(Y0, 0, 64), S(Y0, 64, 128), S(Y1, 0, 64), S(TB, 128, 132)
            ox, oy = S("o2", s0, s0 + 64), S("o2", s0 + 64, s0 + 128)
            mm([(S(Y0, 0, 128), S("Id"), S("c2k")), (lo2, S("Id"), part("Z")), (hi2, S("Id"), part("Z"))], last=False)
            mm([(cnt, S("R0"), nl)], last=False)
            do(ts(S("o2", s0, s0 + 128), S(TB, 0, 128), thc(2), None, GT), act(S("o2", s0, s0 + 128), S(TB, 0, 128), AF.Relu, thc(3)))
            mm([(cnt, S("Tri"), ox), (cnt, S("Tri"), oy)], first=False)
            mm([(lo2, S("nTB"), ox), (lo2, S("nTB"), oy), (hi2, S("TB"), ox), (hi2, S("TB"), oy)], first=False)
            do(tt(part("Ea"), part("En") if t else part("e0i"), lo2, MAX))
            do(tt(part("En"), part("Ea"), hi2, MIN))
            if not last:
                send("e%d%d" % (t + 1, h), t + 1, part("En"), S("ER%d" % (t + 1), c0, c1), 32768)
            do(cp(IND(S("G", 512 * h, 512 * h + 512), S("clx", w0, w1)), part("En")))
            do(act(part("l2"), cnt, AF.Relu, pc(13), -1.0))
            mm([(et, S("Id"), S("eb", 0, 4))] + [(et, slide("Sw", b), S("l2", c0 + b, c1, 16)) for b in range(16)])
            do(ts(e16, et, pc(6), None, ADD))
            do(tt(part("qp"), IND(S("XY", k0, k0 + 2048), e16), part("d2"), ADD))
            lin(part("qb"), part("qp"), 0.5, -1024.0)
            rec = IND(S("X", 2048 * h, 2048 * h + 2048), S("clx", 8 + w0, 8 + w1))
            if cfg["xta"]:
                lin(part("xo"), rec)
                mm([(S(Q, 192, 256), S("Id"), part("xo")), (S(Q, 192, 256), S("Id"), d)])
                lin(part("xt"), S(Q, 192, 256), 1.0, 2047.5)
            else:
                do(tt(part("xt"), rec, part("d2"), ADD))
            lin(part("xn"), part("xt"), 0.5, -1024.0)
            do(cp(rec, part("xn")))
            if last:
                dma("s", "ox%d" % h, HBM("yx", 2048 * h, 2048 * h + 2048), S("X", 2048 * h, 2048 * h + 2048), 524288)
                dma("s", "ol%d" % h, HBM("yl", 512 * h, 512 * h + 512), S("G", 512 * h, 512 * h + 512), 262144)
        if last:
            dma("s", "oq", HBM("yq"), S("qb"), 32768)
        else:
            cn = S("P1", 0, 64)
            mm([(cn, S("n16th"), S("nl", 0, 64)), (cn, S("n16th"), S("nl", 64, 128))])
            do(act(S("tmp", 0, 64), cn, AF.Identity, (1024.0 + A0) / 64, 1.0, S("Ac", 0, 1)), also=[S("Ac", 0, 1)])
    return ops


def place(ops, cfg, rank, edges, fixed):
    wake, n = cfg["wake"], len(ops)
    left = [len(e) for e in edges]
    after = [[] for _ in range(n)]
    for i, e in enumerate(edges):
        for d, _lag in e:
            after[d].append(i)
    busy = {e: [] for e in "vapgs"}
    banks = {}
    start, end, eng = [0.0] * n, [0.0] * n, [None] * n
    ready = [(rank[i], i) for i in range(n) if not left[i]]
    while ready:
        k = ready.index(min(ready))
        i = ready[k][1]
        ready[k] = ready[-1]
        ready.pop()
        t0 = max([end[d] + lag for d, lag in edges[i]] or [0.0])
        best = (t0, t0, "r")
        if ops[i]["alts"]:
            best = None
            for e in ([fixed[i]] if fixed else ops[i]["alts"]):
                c, t, moved = ops[i]["alts"][e][0], t0, True
                while moved:
                    moved = False
                    line = busy[e]
                    lo, hi = 0, len(line)
                    while lo < hi:
                        mid = (lo + hi) // 2
                        if line[mid][1] <= t:
                            lo = mid + 1
                        else:
                            hi = mid
                    while lo < len(line) and line[lo][0] < t + c:
                        t = line[lo][1]
                        lo += 1
                    for b in ops[i]["banks"]:
                        for s2, e2, who in banks.get(b, ()):
                            if who != e and s2 < t + c + wake and t < e2 + wake:
                                t, moved = e2 + wake, True
                key = t + c + (cfg["vpen"] if e == "v" else 0.0)
                if best is None or key < best[3]:
                    best = (t, t + c, e, key, lo)
            busy[best[2]].insert(best[4], (best[0], best[1]))
            for b in ops[i]["banks"]:
                banks.setdefault(b, []).append((best[0], best[1], best[2]))
        start[i], end[i], eng[i] = best[:3]
        for s in after[i]:
            left[s] -= 1
            if not left[s]:
                ready.append((rank[s], s))
    return start, end, eng


def schedule(ops, cfg):
    n, wake = len(ops), cfg["wake"]
    lag = lambda d, i: 0.0 if "p" in ops[d]["alts"] and "p" in ops[i]["alts"] else ops[d]["lat"] + (wake if ops[i]["alts"] else 0.0)
    fwd = [[(d, lag(d, i)) for d in o["deps"]] for i, o in enumerate(ops)]
    bwd = [[] for _ in range(n)]
    for i in range(n):
        for d, l in fwd[i]:
            bwd[d].append((i, l))
    seed = [cfg["seed"] * 7919 + 12345]

    def rnd():
        seed[0] = (seed[0] * 1103515245 + 12345) % 2147483648
        return seed[0] / 2147483648.0
    tail = [0.0] * n
    for i in range(n - 1, -1, -1):
        tail[i] = min([a[0] for a in ops[i]["alts"].values()] or [0.0]) + max([tail[s] + l for s, l in bwd[i]] or [ops[i]["lat"]])
    rank, best = [cfg["stag"] * o["half"] - x for x, o in zip(tail, ops)], None
    last = [bwd[i] or [(n, ops[i]["lat"])] for i in range(n)] + [[]]
    for _ in range(cfg["passes"]):
        start, end, eng = place(ops, cfg, [r + cfg["noise"] * rnd() for r in rank], fwd, None)
        total = max(end[i] + ops[i]["lat"] for i in range(n))
        if best is None or total < best[0]:
            best = (total, start, end, eng)
        _s, back, _e = place(ops + [{"alts": {}, "banks": []}], cfg, [-x for x in end] + [-1e18], last, eng + ["r"])
        rank = [-x for x in back[:n]]
    total, start, end, eng = best
    order = {e: sorted((i for i in range(n) if eng[i] == e), key=lambda i: (start[i], end[i], i)) for e in "vapgs"}
    more, seen = [set() for _ in range(n)], {}
    for i in sorted(range(n), key=lambda i: (start[i], i)):
        for b in ops[i]["banks"]:
            more[i].update(j for e, j in seen.get(b, {}).items() if e != eng[i])
            seen.setdefault(b, {})[eng[i]] = i
    return order, eng, more, total, [end[i] + ops[i]["lat"] for i in range(n)]


def schedule_old(ops, cfg):
    n, wake = len(ops), cfg["wake"]
    succ = [[] for _ in range(n)]
    for i, o in enumerate(ops):
        for d in o["deps"]:
            succ[d].append(i)
    seed = [cfg["seed"] * 7919 + 12345]

    def rnd():
        seed[0] = (seed[0] * 1103515245 + 12345) % 2147483648
        return seed[0] / 2147483648.0
    prio = [0.0] * n
    for i in range(n - 1, -1, -1):
        c = min([a[0] for a in ops[i]["alts"].values()] or [0.0]) + ops[i]["lat"]
        prio[i] = c + wake + max([prio[s] for s in succ[i]] or [0.0])
    prio = [p + cfg["noise"] * rnd() for p in prio]
    engs = [list(o["alts"]) for o in ops]
    rdy = [0.0] * n
    left = [len(o["deps"]) for o in ops]
    fin, eng = [0.0] * n, [None] * n
    free = {e: 0.0 for e in "vapgs"}
    order = {e: [] for e in "vapgs"}
    banks = {}
    more = [set() for _ in range(n)]
    ready = [i for i in range(n) if left[i] == 0]

    def done(i):
        for s in succ[i]:
            left[s] -= 1
            if left[s] == 0:
                if ops[s]["kind"] == "r":
                    fin[s] = fin[i] + ops[s]["lat"]
                    eng[s] = "r"
                    done(s)
                else:
                    pe_ = engs[s][0] == "p"
                    rdy[s] = max([fin[d] + wake for d in ops[s]["deps"] if not (pe_ and eng[d] == "p")] or [0.0])
                    ready.append(s)

    def start(i, e):
        t = max(free[e], rdy[i])
        for b in ops[i]["banks"]:
            for e2, j in banks.get(b, {}).items():
                if e2 != e:
                    t = max(t, fin[j] + wake)
        return t
    while ready:
        cands = []
        for i in ready:
            es = engs[i]
            if len(es) == 1:
                cands.append((start(i, es[0]), i, es[0]))
                continue
            sv, sa = start(i, "v"), start(i, "a")
            cands.append((sa, i, "a"))
            if sa - sv >= cfg["vpen"]:
                cands.append((sv, i, "v"))
        t0, _, e0 = min(cands)
        near = [c for c in cands if c[2] == e0 and c[0] <= t0 + cfg["look"]]
        t, i, e = max(near, key=lambda c: prio[c[1]] - (c[0] - t0))
        fits = [c for c in near if c[0] + ops[c[1]]["alts"][e][0] <= t + cfg["slack"] and c[0] < t]
        if fits:
            t, i, e = max(fits, key=lambda c: prio[c[1]])
        ready.remove(i)
        cost = ops[i]["alts"][e][0]
        free[e] = t + cost
        fin[i] = t + cost + ops[i]["lat"]
        eng[i] = e
        order[e].append(i)
        for b in ops[i]["banks"]:
            more[i].update(j for e2, j in banks.get(b, {}).items() if e2 != e)
            banks.setdefault(b, {})[e] = i
        done(i)
    return order, eng, more, max(fin), fin


def plan(cfg):
    ops = build_ops(cfg)
    order, eng, more, total, fin = schedule(ops, cfg)
    token = {}
    for e in "vapg":
        k = 0
        for i in order[e]:
            if ops[i]["kind"] == "c":
                k += 1
                token[i] = ("c" + e, k)
    for i, o in enumerate(ops):
        if o["kind"] == "d":
            token[i] = (o["sem"], 16)
        elif o["kind"] in "sr":
            token[i] = (o["sem"], -1)
    know, waits = {}, {}
    clock = {e: {} for e in "vapgs"}
    pos = {e: 0 for e in "vapgs"}
    for i, o in enumerate(ops):
        if o["kind"] == "r":
            know[i] = {token[i][0]: 1}
    moved = True
    while moved:
        moved = False
        for e in "vapgs":
            while pos[e] < len(order[e]):
                i = order[e][pos[e]]
                deps = [d for d in ops[i]["deps"] | more[i] if not (e == "p" and eng[d] == "p")]
                if any(d not in know for d in deps):
                    break
                w = []
                for d in sorted(deps, key=lambda d: -fin[d]):
                    s, v = token[d]
                    if clock[e].get(s, 0) < abs(v):
                        w.append((s, v))
                        for s2, v2 in know[d].items():
                            if clock[e].get(s2, 0) < v2:
                                clock[e][s2] = v2
                waits[i] = w
                kn = dict(clock[e])
                kn[token[i][0]] = max(kn.get(token[i][0], 0), abs(token[i][1]))
                know[i] = kn
                pos[e] += 1
                moved = True
    seen = {}
    for e in "vapgs":
        for s, v in clock[e].items():
            seen[s] = max(seen.get(s, 0), v)
    top = {}
    for i in sorted(token, key=lambda i: fin[i]):
        s, v = token[i]
        if abs(v) >= abs(top.get(s, 0)):
            top[s] = v
    tail = [(s, v) for s, v in top.items() if seen.get(s, 0) < abs(v)]
    return ops, order, waits, token, tail, total


_PLAN = plan(CFG)
_ALL = dict(SCRATCH)
SCRATCH = {_n: _v for _n, _v in _ALL.items() if _n in {_o["name"] for _o in _PLAN[0]} | {"Ac"}}
SEMAPHORES = sorted({s for s, _v in _PLAN[3].values()}) + ["hg%d" % _t for _t in range(1, STEPS)] + ["kg%d" % _t for _t in range(1, STEPS)]


def helper_of(c, T, topo):
    return [k for k in topo.cores_of(c) if T.rank_of(k) is None and topo.die(k) != topo.die(c)
            and all(topo.may_write(k, r) for r in T.cores)][0]


def rank_program(g, core, T, topo):
    rank = T.rank_of(core)
    if rank is None:
        for r, c in enumerate(T.cores):
            if helper_of(c, T, topo) == core:
                for t in range(1, STEPS):
                    dst = T.cores[(r - 1 - t % (N - 1)) % N]
                    rid, pid, _se = topo.addr(dst)
                    g.wait_ge(T.sem["hg%d" % t], len(topo.engines(c, core)))
                    g.remote_dma(T["GR%d" % t][:, 512:1024], T["GR%d" % t][:, 512:1024], T.sem["rg%d" % t], T.sem["kg%d" % t], pid, rid, topo.mask(core, dst))
                for t in range(1, STEPS):
                    g.wait_ge(T.sem["kg%d" % t], len(topo.engines(core, T.cores[(r - 1 - t % (N - 1)) % N])))
        return
    hc = helper_of(core, T, topo)
    helper = (topo.addr(hc)[0], topo.addr(hc)[1], topo.mask(core, hc))
    ops, order, waits, token, tail, _total = _PLAN
    to, frm = {}, {}
    for t in range(STEPS):
        dst = T.cores[(rank - 1 - t % (N - 1)) % N]
        src = T.cores[(rank + 1 + t % (N - 1)) % N]
        rid, pid, _se = topo.addr(dst)
        to[t] = (rid, pid, topo.mask(core, dst))
        frm[t] = (len(topo.engines(core, dst)), len(topo.engines(src, core)))
        if t == 0:
            rid, pid, _se = topo.addr(src)
            to["b"] = (rid, pid, topo.mask(core, src))
            frm["b"] = (len(topo.engines(core, src)), len(topo.engines(dst, core)))
    queues = {"v": g.vector, "a": g.scalar, "p": g.tensor, "g": g, "s": g.sync}

    def count(s, v):
        if v < 0 and s[1] == "g":
            if s[0] == "l":
                return len(topo.engines(core, hc))
            return len(topo.engines(helper_of(T.cores[(rank + 1 + int(s[2]) % (N - 1)) % N], T, topo), core))
        return v if v > 0 else frm[s[2] if s[2] == "b" else int(s[2])][0 if s[0] == "l" else 1]
    for e in "sgvap":
        q = queues[e]
        for i in order[e]:
            for s, v in waits[i]:
                q.wait_ge(T.sem[s], count(s, v))
            ins = ops[i]["alts"][e][1](g, T, {"to": to, "q": q, "helper": helper})
            if ops[i]["kind"] == "c":
                ins.then_inc(T.sem[token[i][0]], 1)
            elif ops[i]["kind"] == "d":
                ins.then_inc(T.sem[token[i][0]], 16)
    for s, v in tail:
        g.sync.wait_ge(T.sem[s], count(s, v))
